import numpy as np
import ml_dtypes


def mxq(x, axis, fmt="e4m3"):
    dtype, down = {"e4m3": (ml_dtypes.float8_e4m3fn, 7), "e5m2": (ml_dtypes.float8_e5m2, 14)}[fmt]
    v = np.moveaxis(np.asarray(x, np.float32).astype(ml_dtypes.bfloat16).astype(np.float64), axis, -1)
    blocks = v.reshape(v.shape[:-1] + (-1, 32))
    amax = np.abs(blocks).max(-1, keepdims=True)
    byte = np.maximum(np.where(amax > 0, np.frexp(amax)[1] - 1 + 127, 0) - down, 1)
    scale = np.exp2(byte - 127.0)
    codes = (blocks / scale).astype(np.float32).astype(dtype).astype(np.float64)
    return np.moveaxis((codes * scale).reshape(v.shape), -1, axis)


WIDE = False


def mx_kscale(k):
    if not WIDE:
        return np.ones(k)
    levels = np.array([10, -10, 5, -5, 0])
    if k % 512:
        return np.exp2(np.random.permutation(np.resize(levels, k // 32))).repeat(32)
    a = np.empty((k // 512, 16))
    for p in range(k // 512):
        a[p, :8] = np.random.permutation(np.resize(levels, 8))
        for g in range(8):
            far = levels[np.abs(levels - a[p, g]) >= 10]
            a[p, g + 8] = far[np.random.randint(len(far))]
    return np.exp2(a.ravel()).repeat(32)


def f64(x):
    return np.asarray(x).astype(np.float64)


def striped(idx):
    return np.tile(idx.reshape(-1, 16).T, (8, 1)).astype(np.uint16)


def unstriped(offs):
    return offs[:16].T.reshape(-1).astype(np.int64)


E2M1 = np.array([0.0, 0.5, 1.0, 1.5, 2.0, 3.0, 4.0, 6.0, -0.0, -0.5, -1.0, -1.5, -2.0, -3.0, -4.0, -6.0])


def pack_weight(w, fmt):
    k, n = w.shape
    w = f64(np.asarray(w, np.float32).astype(ml_dtypes.bfloat16)).reshape(k // 32, 32, n)
    amax = np.abs(w).max(1)
    if fmt == "e4m3":
        byte = np.frexp(amax)[1] - 1 + 127 - 7
    else:
        mant, ex = np.frexp(amax / 6.0)
        byte = np.where(mant > 0.5, ex, ex - 1) + 127
    byte = np.clip(np.where(amax > 0, byte, 1), 1, 254)
    scaled = (w * np.exp2(127.0 - byte)[:, None, :]).reshape(k, n).astype(np.float32)
    by_word = np.ascontiguousarray(scaled.reshape(k // 512, 128, 4, n).transpose(0, 1, 3, 2))
    if fmt == "e4m3":
        words = by_word.astype(ml_dtypes.float8_e4m3fn).view(np.uint8)
    else:
        c = by_word.astype(ml_dtypes.float4_e2m1fn).view(np.uint8) & 0xF
        words = (c[..., 0::2] | (c[..., 1::2] << 4)).reshape(k // 512, 128, 2 * n)
    return np.ascontiguousarray(words), np.ascontiguousarray(byte.astype(np.uint8).reshape(k // 512, 16, n))


def unpack_weight(words, scales, fmt):
    g, _, n = scales.shape
    words = np.ascontiguousarray(words).reshape(g, 128, n, -1)
    if fmt == "e4m3":
        vals = words.view(ml_dtypes.float8_e4m3fn).astype(np.float64)
    else:
        nib = np.empty((g, 128, n, 4), np.uint8)
        nib[..., 0::2] = words & 0xF
        nib[..., 1::2] = words >> 4
        vals = E2M1[nib]
    vals = vals * np.repeat(np.exp2(scales.astype(np.float64) - 127.0), 8, axis=1)[..., None]
    return vals.transpose(0, 1, 3, 2).reshape(g * 512, n)


def gelu(v):
    return 0.5 * v * (1.0 + np.tanh(np.sqrt(2.0 / np.pi) * (v + 0.044715 * v**3)))


def striped8(idx):
    return np.concatenate([v.reshape(-1, 16).T for v in idx]).astype(np.uint16)


def unstriped8(offs):
    return np.stack([offs[16 * g:16 * g + 16].T.reshape(-1) for g in range(8)]).astype(np.int64)


def heads(h, wgt, idx8):
    r = np.arange(h.shape[0])
    return wgt[r // 4 % 128] * h[r[:, None], idx8[r % 512 // 64]]


K, H, N, T, S, P = 1024, 1024, 1024, 4096, 1024, 512

def setup_inputs():
    n = np.random.standard_normal
    s = mx_kscale(K)[:, None]
    u = mx_kscale(H)[:, None]
    tab_words, tab_scales = pack_weight(n((K, T)) * s, "e4m3")
    w4_words, w4_scales = pack_weight(n((K, H)) / np.sqrt(K) / s * u.T, "e2m1")
    wr_words, wr_scales = pack_weight(np.linalg.qr(n((H, N)))[0] / u, "e4m3")
    return {
        "tab_words": tab_words, "tab_scales": tab_scales,
        "offs": striped(np.random.permutation(T)[:S]),
        "w4_words": w4_words, "w4_scales": w4_scales,
        "offs2": striped8(np.stack([np.random.permutation(S)[:P] for _ in range(8)])),
        "wgt": np.repeat(np.random.uniform(0.5, 2.0, (8, P)), 16, axis=0).astype(np.float32),
        "mom": (n((K, P)) * s).astype(np.float32),
        "wm": (n((K, H)) / np.sqrt(K) / s).astype(np.float32),
        "eps": np.random.uniform(0.3, 1.2, H).astype(np.float32),
        "wr_words": wr_words, "wr_scales": wr_scales,
        "rate": np.exp(0.4 * n(N)).astype(np.float32),
    }

def reference(tab_words, tab_scales, offs, w4_words, w4_scales, offs2, wgt, mom, wm, eps, wr_words, wr_scales, rate):
    v = unpack_weight(tab_words, tab_scales, "e4m3")[:, unstriped(offs)]
    w4 = unpack_weight(w4_words, w4_scales, "e2m1")
    wr = unpack_weight(wr_words, wr_scales, "e4m3")
    h = w4.T @ v
    x = heads(h, f64(wgt), unstriped8(offs2))
    b = mxq(f64(wm), 0, "e4m3").T @ mxq(f64(mom), 0, "e4m3")
    z = x / np.sqrt(f64(eps)[:, None] + np.square(b))
    y = wr.T @ mxq(z, 0, "e4m3")
    return f64(rate)[:, None] * y

@@ -1,0 +1,301 @@
+from contextlib import ExitStack
+
+import concourse.mybir as mybir
+
+K, H, N, T, S, M = 1024, 1024, 1024, 4096, 1024, 512
+FLOPS = 2 * K * H * S + 2 * K * H * M + 2 * H * N * M
+
+F32 = mybir.dt.float32
+BF16 = mybir.dt.bfloat16
+I32 = mybir.dt.int32
+U32 = mybir.dt.uint32
+U16 = mybir.dt.uint16
+U8 = mybir.dt.uint8
+FP8X4 = mybir.dt.float8_e4m3fn_x4
+FP4X4 = mybir.dt.float4_e2m1fn_x4
+ACT = mybir.ActivationFunctionType
+MULT = mybir.AluOpType.mult
+
+P = 128
+PACK = 4
+K_PASS = P * PACK
+PASSES = 2
+QUADS = 4
+BANK = 512
+M_HALF = M // 2
+WR_ROW = 8
+
+
+def tile_list_sharded_embedding_preconditioning_kernel(
+    tc, tab_words, tab_scales, offs, w4_words, w4_scales, offs2, wgt, mom, wm, eps, wr_words, wr_scales, rate, out
+):
+    nc = tc.nc
+    with ExitStack() as ctx:
+        keep = ctx.enter_context(tc.tile_pool(name="keep", bufs=1))
+        stage = ctx.enter_context(tc.tile_pool(name="stage", bufs=3))
+        psum = ctx.enter_context(tc.psum_pool(name="psum", bufs=8))
+
+        def held(shape, dtype, name):
+            return keep.tile(shape, dtype, name=name, align_bytes=64)
+
+        idx = keep.tile([P, S // 16], U16, name="idx")
+        idx2 = keep.tile([P, M // 16], U16, name="idx2")
+        tab = [held([P, T], I32, f"tab{a}") for a in range(PASSES)]
+        tab_sc = held([P, PASSES, T], U8, "tab_sc")
+        w4 = held([P, PASSES, 2 * H], U8, "w4")
+        w4_sc = held([P, PASSES, H], U8, "w4_sc")
+        wr = held([P, PASSES, N], I32, "wr")
+        wr_sc = held([P, PASSES, N], U8, "wr_sc")
+        eps_sb = held([P, PASSES * PACK], F32, "eps_sb")
+        rate_sb = held([P, N // P], F32, "rate_sb")
+        wgt_sb = held([P, M], F32, "wgt_sb")
+        v_planes = [held([P, S], U8, f"v_sc{a}") for a in range(PASSES)]
+
+        nc.vector.memset(tab_sc[:].bitcast(I32), 0)
+        nc.vector.memset(w4_sc[:].bitcast(I32), 0)
+        nc.vector.memset(wr_sc[:].bitcast(I32), 0)
+
+        def load_scales(queue, tile, scales, row):
+            for q in range(QUADS):
+                queue.dma_start(
+                    tile[32 * q + row : 32 * q + row + 4].bitcast(I32),
+                    scales[:, 4 * q : 4 * q + 4, :].rearrange("a r n -> r a n").bitcast(I32),
+                )
+
+        def load_table(a):
+            nc.sync.dma_start(tab[a][:], tab_words[a].rearrange("p n t -> p (n t)").bitcast(I32))
+
+        nc.sync.dma_start(w4[:].bitcast(I32), w4_words.rearrange("a p n -> p a n").bitcast(I32))
+        nc.sync.dma_start(idx[:], offs)
+        load_scales(nc.sync, tab_sc, tab_scales, 0)
+        load_table(0)
+        load_scales(nc.sync, w4_sc, w4_scales, 0)
+        load_table(1)
+        nc.gpsimd.dma_start(
+            eps_sb[:].rearrange("p (b t) -> p b t", t=PACK), eps.rearrange("(b p t) -> p b t", p=P, t=PACK)
+        )
+        load_scales(nc.gpsimd, wr_sc, wr_scales, WR_ROW)
+
+        nc.sync.dma_start(idx2[:], offs2)
+        nc.sync.dma_start(wgt_sb[:], wgt)
+
+        wm_raw = {}
+        mom_raw = {}
+
+        def load_wm(b):
+            for a in range(PASSES):
+                wm_raw[a, b] = held([P, PACK, K_PASS], F32, f"wm_raw{a}{b}")
+                rows = wm[K_PASS * a : K_PASS * (a + 1), K_PASS * b : K_PASS * (b + 1)]
+                nc.sync.dma_start(wm_raw[a, b][:], rows.rearrange("(p j) c -> p j c", j=PACK))
+
+        def load_mom(half):
+            for a in range(PASSES):
+                mom_raw[a, half] = held([P, PACK, M_HALF], F32, f"mom_raw{a}{half}")
+                rows = mom[K_PASS * a : K_PASS * (a + 1), M_HALF * half : M_HALF * (half + 1)]
+                nc.sync.dma_start(mom_raw[a, half][:], rows.rearrange("(p j) m -> p j m", j=PACK))
+
+        load_wm(0)
+        load_mom(0)
+        load_wm(1)
+        load_mom(1)
+        nc.sync.dma_start(wr[:], wr_words.rearrange("a p n t -> p a (n t)").bitcast(I32))
+        with nc.allow_non_contiguous_dma(reason="one rate a partition"):
+            nc.sync.dma_start(rate_sb[:], rate.rearrange("(s p) -> p s", p=P))
+
+        r0 = held([P, PASSES * PACK], F32, "r0")
+        nc.scalar.activation(r0[:], eps_sb[:], ACT.Abs_reciprocal_sqrt)
+
+        w4p = held([P, PASSES, 2 * H], U8, "w4p")
+        w4p_sc = held([P, PASSES, H], U8, "w4p_sc")
+        nc.vector.tensor_copy(
+            w4p[:].bitcast(U16).rearrange("p a (b t m) -> p (a b) t m", b=2, t=PACK),
+            w4[:].bitcast(U16).rearrange("p a (b m t) -> p (a b) t m", b=2, t=PACK),
+        )
+
+        nc.vector.tensor_copy(v_planes[0][:], tab_sc[:, 0, :].indirect(idx[:]))
+        v = {}
+
+        def gather_words(a, jh):
+            v[a, jh] = held([P, BANK], U32, f"v{a}{jh}")
+            cols = BANK // 16
+            nc.vector.tensor_copy(v[a, jh][:], tab[a][:].bitcast(U32).indirect(idx[:, cols * jh : cols * (jh + 1)]))
+
+        gather_words(0, 0)
+        nc.vector.tensor_copy(
+            w4p_sc[:].rearrange("p a (b t m) -> p (a b) t m", b=2, t=PACK),
+            w4_sc[:].rearrange("p a (b m t) -> p (a b) t m", b=2, t=PACK),
+        )
+        gather_words(0, 1)
+        nc.vector.tensor_copy(v_planes[1][:], tab_sc[:, 1, :].indirect(idx[:]))
+        gather_words(1, 0)
+        gather_words(1, 1)
+
+        def h_pass(bank, s, jh, a):
+            nc.tensor.matmul_mx(
+                out=bank[:],
+                lhsT=w4p[:, a, 2 * P * s : 2 * P * (s + 1)].bitcast(FP4X4),
+                lhsT_scale=w4p_sc[:, a, P * s : P * (s + 1)],
+                rhs=v[a, jh][:].bitcast(FP8X4),
+                rhs_scale=v_planes[a][:, BANK * jh : BANK * (jh + 1)],
+                start=(a == 0),
+                stop=(a == PASSES - 1),
+            )
+
+        h = [held([P, S], F32, f"h{s}") for s in range(2 * PACK)]
+        x = [held([P, PACK, M], F32, f"x{b}") for b in range(2)]
+
+        def h_out(bank, s, jh):
+            nc.scalar.activation(h[s][:, BANK * jh : BANK * (jh + 1)], bank[:], ACT.Copy, scale=r0[:, s : s + 1])
+
+        def pick(s):
+            nc.vector.tensor_tensor(x[s // PACK][:, s % PACK, :], h[s][:].indirect(idx2[:]), wgt_sb[:], MULT)
+
+        wm_q = {}
+        wm_sc = {}
+        mom_q = {}
+        mom_sc = {}
+        rounded = {}
+
+        def round_wm(a, b, copy):
+            rounded[a, b] = stage.tile([P, PACK * K_PASS], BF16, name="rounded", tag="rounded", align_bytes=64)
+            copy(
+                rounded[a, b][:].rearrange("p (t m j) -> p m j t", t=PACK, j=PACK),
+                wm_raw[a, b][:].rearrange("p j (m t) -> p m j t", t=PACK),
+            )
+
+        def quantise_wm(a, b):
+            wm_q[a, b] = held([P, K_PASS], U32, f"wm_q{a}{b}")
+            wm_sc[a, b] = held([P, K_PASS], U8, f"wm_sc{a}{b}")
+            nc.vector.quantize_mx(out=wm_q[a, b][:].bitcast(FP8X4), scales=wm_sc[a, b][:], in_=rounded[a, b][:])
+
+        def round_mom(half, copy):
+            rounded[half] = stage.tile([P, PACK * K_PASS], BF16, name="rounded", tag="rounded", align_bytes=64)
+            for a in range(PASSES):
+                part = rounded[half][:, PACK * M_HALF * a : PACK * M_HALF * (a + 1)]
+                copy(
+                    part.rearrange("p (c i j) -> p c j i", i=4, j=PACK),
+                    mom_raw[a, half][:].rearrange("p j (c i) -> p c j i", i=4),
+                )
+
+        def quantise_mom(half):
+            mom_q[half] = held([P, PASSES * M_HALF], U32, f"mom_q{half}")
+            mom_sc[half] = held([P, PASSES * M_HALF], U8, f"mom_sc{half}")
+            nc.vector.quantize_mx(out=mom_q[half][:].bitcast(FP8X4), scales=mom_sc[half][:], in_=rounded[half][:])
+
+        damp = {}
+
+        def project_momentum(b, half):
+            damp[b, half] = held([P, PACK, M_HALF], F32, f"damp{b}{half}")
+            for pair in range(2):
+                bank = psum.tile([P, BANK], F32, name="bank", tag="bank")
+                for u in range(2):
+                    t = 2 * pair + u
+                    for a in range(PASSES):
+                        nc.tensor.matmul_mx(
+                            out=bank[:, M_HALF * u : M_HALF * (u + 1)],
+                            lhsT=wm_q[a, b][:, P * t : P * (t + 1)].bitcast(FP8X4),
+                            lhsT_scale=wm_sc[a, b][:, P * t : P * (t + 1)],
+                            rhs=mom_q[half][:, M_HALF * a : M_HALF * (a + 1)].bitcast(FP8X4),
+                            rhs_scale=mom_sc[half][:, M_HALF * a : M_HALF * (a + 1)],
+                            start=(a == 0),
+                            stop=(a == PASSES - 1),
+                        )
+                for u in range(2):
+                    t = 2 * pair + u
+                    s = PACK * b + t
+                    nc.scalar.activation(
+                        damp[b, half][:, t, :], bank[:, M_HALF * u : M_HALF * (u + 1)], ACT.Square, scale=r0[:, s : s + 1]
+                    )
+            whole = damp[b, half][:].rearrange("p t m -> p (t m)")
+            nc.scalar.activation(whole, whole, ACT.Abs_reciprocal_sqrt, bias=1.0)
+
+        z = {}
+        z_q = {}
+        z_sc = {}
+
+        def precondition(b, half):
+            z[b, half] = stage.tile([P, PACK * M_HALF], BF16, name="z", tag="z", align_bytes=64)
+            nc.vector.tensor_tensor(
+                z[b, half][:].rearrange("p (c i t) -> p c t i", i=2, t=PACK),
+                x[b][:, :, M_HALF * half : M_HALF * (half + 1)].rearrange("p t (c i) -> p c t i", i=2),
+                damp[b, half][:].rearrange("p t (c i) -> p c t i", i=2),
+                MULT,
+            )
+
+        def quantise_z(b, half):
+            z_q[b, half] = held([P, M_HALF], U32, f"z_q{b}{half}")
+            z_sc[b, half] = held([P, M_HALF], U8, f"z_sc{b}{half}")
+            nc.vector.quantize_mx(out=z_q[b, half][:].bitcast(FP8X4), scales=z_sc[b, half][:], in_=z[b, half][:])
+
+        def rotate_back(half):
+            for pair in range(N // P // 2):
+                bank = psum.tile([P, BANK], F32, name="bank", tag="bank")
+                for u in range(2):
+                    s = 2 * pair + u
+                    for b in range(PASSES):
+                        nc.tensor.matmul_mx(
+                            out=bank[:, M_HALF * u : M_HALF * (u + 1)],
+                            lhsT=wr[:, b, P * s : P * (s + 1)].bitcast(FP8X4),
+                            lhsT_scale=wr_sc[WR_ROW:, b, P * s : P * (s + 1)],
+                            rhs=z_q[b, half][:].bitcast(FP8X4),
+                            rhs_scale=z_sc[b, half][:],
+                            start=(b == 0),
+                            stop=(b == PASSES - 1),
+                        )
+                y = stage.tile([P, 2, M_HALF], F32, name="y", tag="y", bufs=4)
+                for u in range(2):
+                    s = 2 * pair + u
+                    src = bank[:, M_HALF * u : M_HALF * (u + 1)]
+                    if half == 1 and pair % 2 == 1:
+                        nc.vector.tensor_scalar(y[:, u, :], src, rate_sb[:, s : s + 1], None, MULT)
+                    else:
+                        nc.scalar.activation(y[:, u, :], src, ACT.Copy, scale=rate_sb[:, s : s + 1])
+                rows = out.rearrange("(s p) m -> p s m", p=P)
+                nc.sync.dma_start(rows[:, 2 * pair : 2 * pair + 2, M_HALF * half : M_HALF * (half + 1)], y[:])
+
+        first = {}
+        for jh in range(2):
+            for s in range(PACK):
+                first[s, jh] = psum.tile([P, BANK], F32, name="bank", tag="bank")
+                h_pass(first[s, jh], s, jh, 0)
+        for jh in range(2):
+            for s in range(PACK):
+                h_pass(first[s, jh], s, jh, 1)
+        round_wm(0, 0, nc.vector.tensor_copy)
+        quantise_wm(0, 0)
+        round_wm(1, 0, nc.vector.tensor_copy)
+        quantise_wm(1, 0)
+        round_mom(0, nc.vector.tensor_copy)
+        quantise_mom(0)
+        for s in range(PACK):
+            for jh in range(2):
+                h_out(first[s, jh], s, jh)
+            pick(s)
+        for s in range(PACK, 2 * PACK):
+            for jh in range(2):
+                bank = psum.tile([P, BANK], F32, name="bank", tag="bank")
+                for a in range(PASSES):
+                    h_pass(bank, s, jh, a)
+                h_out(bank, s, jh)
+        project_momentum(0, 0)
+        round_wm(0, 1, nc.scalar.copy)
+        quantise_wm(0, 1)
+        round_wm(1, 1, nc.scalar.copy)
+        quantise_wm(1, 1)
+        round_mom(1, nc.scalar.copy)
+        quantise_mom(1)
+        for s in range(PACK, 2 * PACK):
+            pick(s)
+        project_momentum(1, 0)
+        project_momentum(0, 1)
+        project_momentum(1, 1)
+        precondition(0, 0)
+        quantise_z(0, 0)
+        precondition(1, 0)
+        quantise_z(1, 0)
+        rotate_back(0)
+        precondition(0, 1)
+        quantise_z(0, 1)
+        precondition(1, 1)
+        quantise_z(1, 1)
+        rotate_back(1)

@@ -24,6 +24,7 @@ QUADS = 4
 BANK = 512
 M_HALF = M // 2
 WR_ROW = 8
+ON_VECTOR = ((1, 0), (1, 1), (1, 2))
 
 
 def tile_list_sharded_embedding_preconditioning_kernel(
@@ -33,27 +34,30 @@ def tile_list_sharded_embedding_preconditioning_kernel(
     with ExitStack() as ctx:
         keep = ctx.enter_context(tc.tile_pool(name="keep", bufs=1))
         stage = ctx.enter_context(tc.tile_pool(name="stage", bufs=3))
+        shared = ctx.enter_context(tc.tile_pool(name="shared", bufs=1))
         psum = ctx.enter_context(tc.psum_pool(name="psum", bufs=8))
 
-        def held(shape, dtype, name):
-            return keep.tile(shape, dtype, name=name, align_bytes=64)
+        def held(shape, dtype, name, tag=None):
+            return keep.tile(shape, dtype, name=name, tag=tag or name, align_bytes=64)
+
+        def placed(shape, dtype, name, kib):
+            return shared.tile(shape, dtype, name=name, align_bytes=64, offset=1024 * kib)
 
         idx = keep.tile([P, S // 16], U16, name="idx")
         idx2 = keep.tile([P, M // 16], U16, name="idx2")
-        tab = [held([P, T], I32, f"tab{a}") for a in range(PASSES)]
-        tab_sc = held([P, PASSES, T], U8, "tab_sc")
-        w4 = held([P, PASSES, 2 * H], U8, "w4")
-        w4_sc = held([P, PASSES, H], U8, "w4_sc")
-        wr = held([P, PASSES, N], I32, "wr")
-        wr_sc = held([P, PASSES, N], U8, "wr_sc")
-        eps_sb = held([P, PASSES * PACK], F32, "eps_sb")
-        rate_sb = held([P, N // P], F32, "rate_sb")
-        wgt_sb = held([P, M], F32, "wgt_sb")
+        tab = [placed([P, T], I32, f"tab{a}", 18 * a) for a in range(PASSES)]
+        tab_sc = placed([P, PASSES, T], U8, "tab_sc", 34)
+        w4 = placed([P, PASSES, 2 * H], U8, "w4", 18)
+        w4_sc = placed([P, PASSES, H], U8, "w4_sc", 16)
+        wr = placed([P, PASSES, N], I32, "wr", 8)
+        wr_sc = placed([P, PASSES, N], U8, "wr_sc", 38)
+        eps_sb = shared.tile([P, PASSES, 2 * PACK], F32, name="eps_sb", offset=16 * 1024 - 32)
+        rate_sb = placed([P, N // P], F32, "rate_sb", 18)
+        wgt_sb = placed([P, M], F32, "wgt_sb", 16)
         v_planes = [held([P, S], U8, f"v_sc{a}") for a in range(PASSES)]
 
-        nc.vector.memset(tab_sc[:].bitcast(I32), 0)
-        nc.vector.memset(w4_sc[:].bitcast(I32), 0)
-        nc.vector.memset(wr_sc[:].bitcast(I32), 0)
+        nc.vector.memset(tab_sc[:, 0, :].bitcast(I32), 0)
+        nc.gpsimd.memset(tab_sc[:, 1, :].bitcast(I32), 0)
 
         def load_scales(queue, tile, scales, row):
             for q in range(QUADS):
@@ -65,45 +69,34 @@ def tile_list_sharded_embedding_preconditioning_kernel(
         def load_table(a):
             nc.sync.dma_start(tab[a][:], tab_words[a].rearrange("p n t -> p (n t)").bitcast(I32))
 
+        nc.sync.dma_start(
+            eps_sb[:, :, 0:PACK], eps.rearrange("(b p t) -> p b t", p=P, t=PACK)
+        )
         nc.sync.dma_start(w4[:].bitcast(I32), w4_words.rearrange("a p n -> p a n").bitcast(I32))
         nc.sync.dma_start(idx[:], offs)
-        load_scales(nc.sync, tab_sc, tab_scales, 0)
-        load_table(0)
-        load_scales(nc.sync, w4_sc, w4_scales, 0)
-        load_table(1)
-        nc.gpsimd.dma_start(
-            eps_sb[:].rearrange("p (b t) -> p b t", t=PACK), eps.rearrange("(b p t) -> p b t", p=P, t=PACK)
-        )
-        load_scales(nc.gpsimd, wr_sc, wr_scales, WR_ROW)
-
         nc.sync.dma_start(idx2[:], offs2)
-        nc.sync.dma_start(wgt_sb[:], wgt)
+        load_scales(nc.sync, tab_sc, tab_scales, 0)
 
         wm_raw = {}
         mom_raw = {}
 
         def load_wm(b):
             for a in range(PASSES):
-                wm_raw[a, b] = held([P, PACK, K_PASS], F32, f"wm_raw{a}{b}")
+                wm_raw[a, b] = placed([P, PACK, K_PASS], F32, f"wm_raw{a}{b}", 18 * b + 8 * a)
                 rows = wm[K_PASS * a : K_PASS * (a + 1), K_PASS * b : K_PASS * (b + 1)]
                 nc.sync.dma_start(wm_raw[a, b][:], rows.rearrange("(p j) c -> p j c", j=PACK))
 
         def load_mom(half):
             for a in range(PASSES):
-                mom_raw[a, half] = held([P, PACK, M_HALF], F32, f"mom_raw{a}{half}")
+                mom_raw[a, half] = placed([P, PACK, M_HALF], F32, f"mom_raw{a}{half}", 34 * (1 - half) + 4 * a)
                 rows = mom[K_PASS * a : K_PASS * (a + 1), M_HALF * half : M_HALF * (half + 1)]
                 nc.sync.dma_start(mom_raw[a, half][:], rows.rearrange("(p j) m -> p j m", j=PACK))
 
-        load_wm(0)
-        load_mom(0)
-        load_wm(1)
-        load_mom(1)
-        nc.sync.dma_start(wr[:], wr_words.rearrange("a p n t -> p a (n t)").bitcast(I32))
-        with nc.allow_non_contiguous_dma(reason="one rate a partition"):
-            nc.sync.dma_start(rate_sb[:], rate.rearrange("(s p) -> p s", p=P))
-
         r0 = held([P, PASSES * PACK], F32, "r0")
-        nc.scalar.activation(r0[:], eps_sb[:], ACT.Abs_reciprocal_sqrt)
+        nc.scalar.activation(r0[:].rearrange("p (b t) -> p b t", t=PACK), eps_sb[:, :, 0:PACK], ACT.Abs_reciprocal_sqrt)
+        load_table(0)
+        nc.gpsimd.memset(w4_sc[:].bitcast(I32), 0)
+        load_scales(nc.sync, w4_sc, w4_scales, 0)
 
         w4p = held([P, PASSES, 2 * H], U8, "w4p")
         w4p_sc = held([P, PASSES, H], U8, "w4p_sc")
@@ -111,6 +104,8 @@ def tile_list_sharded_embedding_preconditioning_kernel(
             w4p[:].bitcast(U16).rearrange("p a (b t m) -> p (a b) t m", b=2, t=PACK),
             w4[:].bitcast(U16).rearrange("p a (b m t) -> p (a b) t m", b=2, t=PACK),
         )
+
+        load_table(1)
 
         nc.vector.tensor_copy(v_planes[0][:], tab_sc[:, 0, :].indirect(idx[:]))
         v = {}
@@ -120,15 +115,19 @@ def tile_list_sharded_embedding_preconditioning_kernel(
             cols = BANK // 16
             nc.vector.tensor_copy(v[a, jh][:], tab[a][:].bitcast(U32).indirect(idx[:, cols * jh : cols * (jh + 1)]))
 
-        gather_words(0, 0)
         nc.vector.tensor_copy(
             w4p_sc[:].rearrange("p a (b t m) -> p (a b) t m", b=2, t=PACK),
             w4_sc[:].rearrange("p a (b m t) -> p (a b) t m", b=2, t=PACK),
         )
+        nc.sync.dma_start(wgt_sb[:], wgt)
+        gather_words(0, 0)
         gather_words(0, 1)
         nc.vector.tensor_copy(v_planes[1][:], tab_sc[:, 1, :].indirect(idx[:]))
+        load_mom(0)
+        load_wm(0)
         gather_words(1, 0)
         gather_words(1, 1)
+        load_wm(1)
 
         def h_pass(bank, s, jh, a):
             nc.tensor.matmul_mx(
@@ -142,7 +141,7 @@ def tile_list_sharded_embedding_preconditioning_kernel(
             )
 
         h = [held([P, S], F32, f"h{s}") for s in range(2 * PACK)]
-        x = [held([P, PACK, M], F32, f"x{b}") for b in range(2)]
+        x = [held([P, PACK, M], F32, "x0"), placed([P, PACK, M], F32, "x1", 42)]
 
         def h_out(bank, s, jh):
             nc.scalar.activation(h[s][:, BANK * jh : BANK * (jh + 1)], bank[:], ACT.Copy, scale=r0[:, s : s + 1])
@@ -157,7 +156,10 @@ def tile_list_sharded_embedding_preconditioning_kernel(
         rounded = {}
 
         def round_wm(a, b, copy):
-            rounded[a, b] = stage.tile([P, PACK * K_PASS], BF16, name="rounded", tag="rounded", align_bytes=64)
+            if (a, b) == (1, 1):
+                rounded[a, b] = placed([P, PACK * K_PASS], BF16, "rounded_last", 42)
+            else:
+                rounded[a, b] = stage.tile([P, PACK * K_PASS], BF16, name="rounded", tag="rounded", align_bytes=64)
             copy(
                 rounded[a, b][:].rearrange("p (t m j) -> p m j t", t=PACK, j=PACK),
                 wm_raw[a, b][:].rearrange("p j (m t) -> p m j t", t=PACK),
@@ -214,7 +216,7 @@ def tile_list_sharded_embedding_preconditioning_kernel(
         z_sc = {}
 
         def precondition(b, half):
-            z[b, half] = stage.tile([P, PACK * M_HALF], BF16, name="z", tag="z", align_bytes=64)
+            z[b, half] = held([P, PACK * M_HALF], BF16, f"z{b}{half}")
             nc.vector.tensor_tensor(
                 z[b, half][:].rearrange("p (c i t) -> p c t i", i=2, t=PACK),
                 x[b][:, :, M_HALF * half : M_HALF * (half + 1)].rearrange("p t (c i) -> p c t i", i=2),
@@ -227,29 +229,35 @@ def tile_list_sharded_embedding_preconditioning_kernel(
             z_sc[b, half] = held([P, M_HALF], U8, f"z_sc{b}{half}")
             nc.vector.quantize_mx(out=z_q[b, half][:].bitcast(FP8X4), scales=z_sc[b, half][:], in_=z[b, half][:])
 
-        def rotate_back(half):
+        y_banks = {}
+
+        def rotate_pass(half, b):
             for pair in range(N // P // 2):
-                bank = psum.tile([P, BANK], F32, name="bank", tag="bank")
+                if b == 0:
+                    y_banks[half, pair] = psum.tile([P, BANK], F32, name="bank", tag="bank")
                 for u in range(2):
                     s = 2 * pair + u
-                    for b in range(PASSES):
-                        nc.tensor.matmul_mx(
-                            out=bank[:, M_HALF * u : M_HALF * (u + 1)],
-                            lhsT=wr[:, b, P * s : P * (s + 1)].bitcast(FP8X4),
-                            lhsT_scale=wr_sc[WR_ROW:, b, P * s : P * (s + 1)],
-                            rhs=z_q[b, half][:].bitcast(FP8X4),
-                            rhs_scale=z_sc[b, half][:],
-                            start=(b == 0),
-                            stop=(b == PASSES - 1),
-                        )
-                y = stage.tile([P, 2, M_HALF], F32, name="y", tag="y", bufs=4)
-                for u in range(2):
-                    s = 2 * pair + u
-                    src = bank[:, M_HALF * u : M_HALF * (u + 1)]
-                    if half == 1 and pair % 2 == 1:
-                        nc.vector.tensor_scalar(y[:, u, :], src, rate_sb[:, s : s + 1], None, MULT)
-                    else:
-                        nc.scalar.activation(y[:, u, :], src, ACT.Copy, scale=rate_sb[:, s : s + 1])
+                    nc.tensor.matmul_mx(
+                        out=y_banks[half, pair][:, M_HALF * u : M_HALF * (u + 1)],
+                        lhsT=wr[:, b, P * s : P * (s + 1)].bitcast(FP8X4),
+                        lhsT_scale=wr_sc[WR_ROW:, b, P * s : P * (s + 1)],
+                        rhs=z_q[b, half][:].bitcast(FP8X4),
+                        rhs_scale=z_sc[b, half][:],
+                        start=(b == 0 and u == 0),
+                        stop=(b == PASSES - 1 and u == 1),
+                    )
+
+        def store(half):
+            for pair in range(N // P // 2):
+                y = stage.tile([P, 2, M_HALF], F32, name="y", tag="y", bufs=8)
+                bank = y_banks[half, pair][:].rearrange("p (u m) -> p u m", u=2)
+                if (half, pair) in ON_VECTOR:
+                    rates = rate_sb[:, 2 * pair : 2 * pair + 2].unsqueeze(2).to_broadcast([P, 2, M_HALF])
+                    nc.vector.tensor_tensor(y[:], bank, rates, MULT)
+                else:
+                    for u in range(2):
+                        s = 2 * pair + u
+                        nc.scalar.activation(y[:, u, :], bank[:, u, :], ACT.Copy, scale=rate_sb[:, s : s + 1])
                 rows = out.rearrange("(s p) m -> p s m", p=P)
                 nc.sync.dma_start(rows[:, 2 * pair : 2 * pair + 2, M_HALF * half : M_HALF * (half + 1)], y[:])
 
@@ -261,12 +269,16 @@ def tile_list_sharded_embedding_preconditioning_kernel(
         for jh in range(2):
             for s in range(PACK):
                 h_pass(first[s, jh], s, jh, 1)
+        round_mom(0, nc.vector.tensor_copy)
+        nc.gpsimd.memset(wr_sc[:].bitcast(I32), 0)
+        load_scales(nc.sync, wr_sc, wr_scales, WR_ROW)
+        quantise_mom(0)
         round_wm(0, 0, nc.vector.tensor_copy)
+        load_mom(1)
         quantise_wm(0, 0)
         round_wm(1, 0, nc.vector.tensor_copy)
+        nc.sync.dma_start(wr[:], wr_words.rearrange("a p n t -> p a (n t)").bitcast(I32))
         quantise_wm(1, 0)
-        round_mom(0, nc.vector.tensor_copy)
-        quantise_mom(0)
         for s in range(PACK):
             for jh in range(2):
                 h_out(first[s, jh], s, jh)
@@ -277,25 +289,31 @@ def tile_list_sharded_embedding_preconditioning_kernel(
                 for a in range(PASSES):
                     h_pass(bank, s, jh, a)
                 h_out(bank, s, jh)
-        project_momentum(0, 0)
         round_wm(0, 1, nc.scalar.copy)
-        quantise_wm(0, 1)
+        with nc.allow_non_contiguous_dma(reason="one rate a partition"):
+            nc.sync.dma_start(rate_sb[:], rate.rearrange("(s p) -> p s", p=P))
         round_wm(1, 1, nc.scalar.copy)
-        quantise_wm(1, 1)
-        round_mom(1, nc.scalar.copy)
+        round_mom(1, nc.vector.tensor_copy)
         quantise_mom(1)
+        quantise_wm(0, 1)
+        quantise_wm(1, 1)
+        project_momentum(0, 0)
+        project_momentum(0, 1)
+        project_momentum(1, 0)
+        project_momentum(1, 1)
         for s in range(PACK, 2 * PACK):
             pick(s)
-        project_momentum(1, 0)
-        project_momentum(0, 1)
-        project_momentum(1, 1)
         precondition(0, 0)
+        precondition(0, 1)
         quantise_z(0, 0)
+        quantise_z(0, 1)
+        rotate_pass(0, 0)
+        rotate_pass(1, 0)
         precondition(1, 0)
         quantise_z(1, 0)
-        rotate_back(0)
-        precondition(0, 1)
-        quantise_z(0, 1)
+        rotate_pass(0, 1)
         precondition(1, 1)
         quantise_z(1, 1)
-        rotate_back(1)
+        rotate_pass(1, 1)
+        store(0)
+        store(1)

@@ -50,7 +50,7 @@ def tile_list_sharded_embedding_preconditioning_kernel(
         w4 = placed([P, PASSES, 2 * H], U8, "w4", 18)
         w4_sc = placed([P, PASSES, H], U8, "w4_sc", 16)
         wr = placed([P, PASSES, N], I32, "wr", 8)
-        wr_sc = placed([P, PASSES, N], U8, "wr_sc", 38)
+        wr_sc = placed([P, PASSES, N], U8, "wr_sc", 34)
         eps_sb = shared.tile([P, PASSES, 2 * PACK], F32, name="eps_sb", offset=16 * 1024 - 32)
         rate_sb = placed([P, N // P], F32, "rate_sb", 18)
         wgt_sb = placed([P, M], F32, "wgt_sb", 16)
@@ -88,7 +88,7 @@ def tile_list_sharded_embedding_preconditioning_kernel(
 
         def load_mom(half):
             for a in range(PASSES):
-                mom_raw[a, half] = placed([P, PACK, M_HALF], F32, f"mom_raw{a}{half}", 34 * (1 - half) + 4 * a)
+                mom_raw[a, half] = placed([P, PACK, M_HALF], F32, f"mom_raw{a}{half}", 36 * (1 - half) + 4 * a)
                 rows = mom[K_PASS * a : K_PASS * (a + 1), M_HALF * half : M_HALF * (half + 1)]
                 nc.sync.dma_start(mom_raw[a, half][:], rows.rearrange("(p j) m -> p j m", j=PACK))
 
@@ -124,6 +124,8 @@ def tile_list_sharded_embedding_preconditioning_kernel(
         gather_words(0, 1)
         nc.vector.tensor_copy(v_planes[1][:], tab_sc[:, 1, :].indirect(idx[:]))
         load_mom(0)
+        nc.gpsimd.memset(wr_sc[:].bitcast(I32), 0)
+        load_scales(nc.sync, wr_sc, wr_scales, WR_ROW)
         load_wm(0)
         gather_words(1, 0)
         gather_words(1, 1)
@@ -141,7 +143,7 @@ def tile_list_sharded_embedding_preconditioning_kernel(
             )
 
         h = [held([P, S], F32, f"h{s}") for s in range(2 * PACK)]
-        x = [held([P, PACK, M], F32, "x0"), placed([P, PACK, M], F32, "x1", 42)]
+        x = [held([P, PACK, M], F32, "x0"), placed([P, PACK, M], F32, "x1", 44)]
 
         def h_out(bank, s, jh):
             nc.scalar.activation(h[s][:, BANK * jh : BANK * (jh + 1)], bank[:], ACT.Copy, scale=r0[:, s : s + 1])
@@ -157,12 +159,12 @@ def tile_list_sharded_embedding_preconditioning_kernel(
 
         def round_wm(a, b, copy):
             if (a, b) == (1, 1):
-                rounded[a, b] = placed([P, PACK * K_PASS], BF16, "rounded_last", 42)
+                rounded[a, b] = placed([P, PACK * K_PASS], BF16, "rounded_last", 44)
             else:
                 rounded[a, b] = stage.tile([P, PACK * K_PASS], BF16, name="rounded", tag="rounded", align_bytes=64)
             copy(
-                rounded[a, b][:].rearrange("p (t m j) -> p m j t", t=PACK, j=PACK),
-                wm_raw[a, b][:].rearrange("p j (m t) -> p m j t", t=PACK),
+                rounded[a, b][:].rearrange("p (u e m j) -> p u m j e", u=2, e=2, j=PACK),
+                wm_raw[a, b][:].rearrange("p j (m u e) -> p u m j e", u=2, e=2),
             )
 
         def quantise_wm(a, b):
@@ -270,8 +272,6 @@ def tile_list_sharded_embedding_preconditioning_kernel(
             for s in range(PACK):
                 h_pass(first[s, jh], s, jh, 1)
         round_mom(0, nc.vector.tensor_copy)
-        nc.gpsimd.memset(wr_sc[:].bitcast(I32), 0)
-        load_scales(nc.sync, wr_sc, wr_scales, WR_ROW)
         quantise_mom(0)
         round_wm(0, 0, nc.vector.tensor_copy)
         load_mom(1)

@@ -24,7 +24,7 @@ QUADS = 4
 BANK = 512
 M_HALF = M // 2
 WR_ROW = 8
-ON_VECTOR = ((1, 0), (1, 1), (1, 2))
+ON_VECTOR = ((1, 0), (1, 2))
 
 
 def tile_list_sharded_embedding_preconditioning_kernel(
@@ -46,18 +46,22 @@ def tile_list_sharded_embedding_preconditioning_kernel(
         idx = keep.tile([P, S // 16], U16, name="idx")
         idx2 = keep.tile([P, M // 16], U16, name="idx2")
         tab = [placed([P, T], I32, f"tab{a}", 18 * a) for a in range(PASSES)]
-        tab_sc = placed([P, PASSES, T], U8, "tab_sc", 34)
+        tab_sc = placed([P, T], U8, "tab_sc", 36)
         w4 = placed([P, PASSES, 2 * H], U8, "w4", 18)
         w4_sc = placed([P, PASSES, H], U8, "w4_sc", 16)
-        wr = placed([P, PASSES, N], I32, "wr", 8)
-        wr_sc = placed([P, PASSES, N], U8, "wr_sc", 34)
+        wr = placed([P, PASSES, N], I32, "wr", 0)
+        wr_sc = placed([P, PASSES, N], U8, "wr_sc", 26)
         eps_sb = shared.tile([P, PASSES, 2 * PACK], F32, name="eps_sb", offset=16 * 1024 - 32)
-        rate_sb = placed([P, N // P], F32, "rate_sb", 18)
+        rate_sb = placed([P, N // P], F32, "rate_sb", 28)
         wgt_sb = placed([P, M], F32, "wgt_sb", 16)
         v_planes = [held([P, S], U8, f"v_sc{a}") for a in range(PASSES)]
 
-        nc.vector.memset(tab_sc[:, 0, :].bitcast(I32), 0)
-        nc.gpsimd.memset(tab_sc[:, 1, :].bitcast(I32), 0)
+        one = held([P, 1], F32, "one")
+        nc.gpsimd.memset(one[:], 1.0)
+        nc.scalar.activation(one[:], one[:], ACT.Abs_reciprocal_sqrt)
+        nc.vector.memset(tab_sc[:, 0 : T // 2].bitcast(I32), 0)
+        nc.gpsimd.memset(tab_sc[:, T // 2 : T].bitcast(I32), 0)
+        nc.vector.memset(v_planes[1][:].bitcast(I32), 0)
 
         def load_scales(queue, tile, scales, row):
             for q in range(QUADS):
@@ -75,7 +79,10 @@ def tile_list_sharded_embedding_preconditioning_kernel(
         nc.sync.dma_start(w4[:].bitcast(I32), w4_words.rearrange("a p n -> p a n").bitcast(I32))
         nc.sync.dma_start(idx[:], offs)
         nc.sync.dma_start(idx2[:], offs2)
-        load_scales(nc.sync, tab_sc, tab_scales, 0)
+        for q in range(QUADS):
+            nc.sync.dma_start(
+                tab_sc[32 * q : 32 * q + 8, :].bitcast(I32), tab_scales[:, 4 * q : 4 * q + 4, :].bitcast(I32)
+            )
 
         wm_raw = {}
         mom_raw = {}
@@ -88,7 +95,7 @@ def tile_list_sharded_embedding_preconditioning_kernel(
 
         def load_mom(half):
             for a in range(PASSES):
-                mom_raw[a, half] = placed([P, PACK, M_HALF], F32, f"mom_raw{a}{half}", 36 * (1 - half) + 4 * a)
+                mom_raw[a, half] = placed([P, PACK, M_HALF], F32, f"mom_raw{a}{half}", 34 + 4 * a)
                 rows = mom[K_PASS * a : K_PASS * (a + 1), M_HALF * half : M_HALF * (half + 1)]
                 nc.sync.dma_start(mom_raw[a, half][:], rows.rearrange("(p j) m -> p j m", j=PACK))
 
@@ -107,7 +114,8 @@ def tile_list_sharded_embedding_preconditioning_kernel(
 
         load_table(1)
 
-        nc.vector.tensor_copy(v_planes[0][:], tab_sc[:, 0, :].indirect(idx[:]))
+        nc.vector.tensor_copy(v_planes[0][:], tab_sc[:].indirect(idx[:]))
+        nc.scalar.dma_start(v_planes[1][0:112, :].bitcast(I32), v_planes[0][4:116, :].bitcast(I32))
         v = {}
 
         def gather_words(a, jh):
@@ -122,10 +130,7 @@ def tile_list_sharded_embedding_preconditioning_kernel(
         nc.sync.dma_start(wgt_sb[:], wgt)
         gather_words(0, 0)
         gather_words(0, 1)
-        nc.vector.tensor_copy(v_planes[1][:], tab_sc[:, 1, :].indirect(idx[:]))
         load_mom(0)
-        nc.gpsimd.memset(wr_sc[:].bitcast(I32), 0)
-        load_scales(nc.sync, wr_sc, wr_scales, WR_ROW)
         load_wm(0)
         gather_words(1, 0)
         gather_words(1, 1)
@@ -143,7 +148,7 @@ def tile_list_sharded_embedding_preconditioning_kernel(
             )
 
         h = [held([P, S], F32, f"h{s}") for s in range(2 * PACK)]
-        x = [held([P, PACK, M], F32, "x0"), placed([P, PACK, M], F32, "x1", 44)]
+        x = [held([P, PACK, M], F32, "x0"), placed([P, PACK, M], F32, "x1", 42)]
 
         def h_out(bank, s, jh):
             nc.scalar.activation(h[s][:, BANK * jh : BANK * (jh + 1)], bank[:], ACT.Copy, scale=r0[:, s : s + 1])
@@ -159,7 +164,7 @@ def tile_list_sharded_embedding_preconditioning_kernel(
 
         def round_wm(a, b, copy):
             if (a, b) == (1, 1):
-                rounded[a, b] = placed([P, PACK * K_PASS], BF16, "rounded_last", 44)
+                rounded[a, b] = placed([P, PACK * K_PASS], BF16, "rounded_last", 42)
             else:
                 rounded[a, b] = stage.tile([P, PACK * K_PASS], BF16, name="rounded", tag="rounded", align_bytes=64)
             copy(
@@ -190,6 +195,10 @@ def tile_list_sharded_embedding_preconditioning_kernel(
 
         def project_momentum(b, half):
             damp[b, half] = held([P, PACK, M_HALF], F32, f"damp{b}{half}")
+            if (b, half) == (0, 0):
+                square = placed([P, PACK, M_HALF], F32, "square00", 30)
+            else:
+                square = held([P, PACK, M_HALF], F32, f"square{b}{half}")
             for pair in range(2):
                 bank = psum.tile([P, BANK], F32, name="bank", tag="bank")
                 for u in range(2):
@@ -208,10 +217,9 @@ def tile_list_sharded_embedding_preconditioning_kernel(
                     t = 2 * pair + u
                     s = PACK * b + t
                     nc.scalar.activation(
-                        damp[b, half][:, t, :], bank[:, M_HALF * u : M_HALF * (u + 1)], ACT.Square, scale=r0[:, s : s + 1]
+                        square[:, t, :], bank[:, M_HALF * u : M_HALF * (u + 1)], ACT.Square, scale=r0[:, s : s + 1]
                     )
-            whole = damp[b, half][:].rearrange("p t m -> p (t m)")
-            nc.scalar.activation(whole, whole, ACT.Abs_reciprocal_sqrt, bias=1.0)
+            nc.scalar.activation(damp[b, half][:], square[:], ACT.Abs_reciprocal_sqrt, bias=one[:])
 
         z = {}
         z_q = {}
@@ -250,8 +258,9 @@ def tile_list_sharded_embedding_preconditioning_kernel(
                     )
 
         def store(half):
+            y_half = held([P, N // P, M_HALF], F32, f"y{half}", None if half else "square11")
             for pair in range(N // P // 2):
-                y = stage.tile([P, 2, M_HALF], F32, name="y", tag="y", bufs=8)
+                y = y_half[:, 2 * pair : 2 * pair + 2, :]
                 bank = y_banks[half, pair][:].rearrange("p (u m) -> p u m", u=2)
                 if (half, pair) in ON_VECTOR:
                     rates = rate_sb[:, 2 * pair : 2 * pair + 2].unsqueeze(2).to_broadcast([P, 2, M_HALF])
@@ -272,12 +281,12 @@ def tile_list_sharded_embedding_preconditioning_kernel(
             for s in range(PACK):
                 h_pass(first[s, jh], s, jh, 1)
         round_mom(0, nc.vector.tensor_copy)
+        load_mom(1)
         quantise_mom(0)
         round_wm(0, 0, nc.vector.tensor_copy)
-        load_mom(1)
+        nc.sync.dma_start(wr[:], wr_words.rearrange("a p n t -> p a (n t)").bitcast(I32))
         quantise_wm(0, 0)
         round_wm(1, 0, nc.vector.tensor_copy)
-        nc.sync.dma_start(wr[:], wr_words.rearrange("a p n t -> p a (n t)").bitcast(I32))
         quantise_wm(1, 0)
         for s in range(PACK):
             for jh in range(2):
@@ -290,6 +299,8 @@ def tile_list_sharded_embedding_preconditioning_kernel(
                     h_pass(bank, s, jh, a)
                 h_out(bank, s, jh)
         round_wm(0, 1, nc.scalar.copy)
+        nc.gpsimd.memset(wr_sc[:].bitcast(I32), 0)
+        load_scales(nc.sync, wr_sc, wr_scales, WR_ROW)
         with nc.allow_non_contiguous_dma(reason="one rate a partition"):
             nc.sync.dma_start(rate_sb[:], rate.rearrange("(s p) -> p s", p=P))
         round_wm(1, 1, nc.scalar.copy)
@@ -298,21 +309,21 @@ def tile_list_sharded_embedding_preconditioning_kernel(
         quantise_wm(0, 1)
         quantise_wm(1, 1)
         project_momentum(0, 0)
-        project_momentum(0, 1)
         project_momentum(1, 0)
+        project_momentum(0, 1)
         project_momentum(1, 1)
         for s in range(PACK, 2 * PACK):
             pick(s)
         precondition(0, 0)
-        precondition(0, 1)
-        quantise_z(0, 0)
-        quantise_z(0, 1)
-        rotate_pass(0, 0)
-        rotate_pass(1, 0)
         precondition(1, 0)
+        quantise_z(0, 0)
         quantise_z(1, 0)
+        rotate_pass(0, 0)
         rotate_pass(0, 1)
+        precondition(0, 1)
         precondition(1, 1)
+        quantise_z(0, 1)
+        rotate_pass(1, 0)
         quantise_z(1, 1)
         rotate_pass(1, 1)
         store(0)

@@ -21,10 +21,24 @@ PACK = 4
 K_PASS = P * PACK
 PASSES = 2
 QUADS = 4
+QUAD = P // QUADS
+SCALE_ROWS = 4
+GROUP = 16
 BANK = 512
+SLICES = H // P
 M_HALF = M // 2
 WR_ROW = 8
+MOVED_ROWS = 112
 ON_VECTOR = ((1, 0), (1, 2))
+
+TAB_AT = (0, 18)
+WM_RAW = 8
+W4_SC_AT = 16
+WR_AT = TAB_AT[0]
+LAST_WM_AT = TAB_AT[1] + WM_RAW
+MOM_AT = 34
+TAB_SC_AT = MOM_AT + 2
+X1_AT = 42
 
 
 def tile_list_sharded_embedding_preconditioning_kernel(
@@ -43,17 +57,17 @@ def tile_list_sharded_embedding_preconditioning_kernel(
         def placed(shape, dtype, name, kib):
             return shared.tile(shape, dtype, name=name, align_bytes=64, offset=1024 * kib)
 
-        idx = keep.tile([P, S // 16], U16, name="idx")
-        idx2 = keep.tile([P, M // 16], U16, name="idx2")
-        tab = [placed([P, T], I32, f"tab{a}", 18 * a) for a in range(PASSES)]
-        tab_sc = placed([P, T], U8, "tab_sc", 36)
-        w4 = placed([P, PASSES, 2 * H], U8, "w4", 18)
-        w4_sc = placed([P, PASSES, H], U8, "w4_sc", 16)
-        wr = placed([P, PASSES, N], I32, "wr", 0)
-        wr_sc = placed([P, PASSES, N], U8, "wr_sc", 26)
-        eps_sb = shared.tile([P, PASSES, 2 * PACK], F32, name="eps_sb", offset=16 * 1024 - 32)
-        rate_sb = placed([P, N // P], F32, "rate_sb", 28)
-        wgt_sb = placed([P, M], F32, "wgt_sb", 16)
+        idx = keep.tile([P, S // GROUP], U16, name="idx")
+        idx2 = keep.tile([P, M // GROUP], U16, name="idx2")
+        tab = [placed([P, T], I32, f"tab{a}", TAB_AT[a]) for a in range(PASSES)]
+        tab_sc = placed([P, T], U8, "tab_sc", TAB_SC_AT)
+        w4 = placed([P, PASSES, 2 * H], U8, "w4", TAB_AT[1])
+        w4_sc = placed([P, PASSES, H], U8, "w4_sc", W4_SC_AT)
+        wr = placed([P, PASSES, N], I32, "wr", WR_AT)
+        wr_sc = placed([P, PASSES, N], U8, "wr_sc", LAST_WM_AT)
+        eps_sb = shared.tile([P, PASSES, 2 * PACK], F32, name="eps_sb", offset=1024 * W4_SC_AT - 32)
+        rate_sb = placed([P, N // P], F32, "rate_sb", LAST_WM_AT + 2)
+        wgt_sb = placed([P, M], F32, "wgt_sb", W4_SC_AT)
         v_planes = [held([P, S], U8, f"v_sc{a}") for a in range(PASSES)]
 
         one = held([P, 1], F32, "one")
@@ -63,95 +77,98 @@ def tile_list_sharded_embedding_preconditioning_kernel(
         nc.gpsimd.memset(tab_sc[:, T // 2 : T].bitcast(I32), 0)
         nc.vector.memset(v_planes[1][:].bitcast(I32), 0)
 
-        def load_scales(queue, tile, scales, row):
-            for q in range(QUADS):
-                queue.dma_start(
-                    tile[32 * q + row : 32 * q + row + 4].bitcast(I32),
-                    scales[:, 4 * q : 4 * q + 4, :].rearrange("a r n -> r a n").bitcast(I32),
+        def load_plane(plane, scales, first_row):
+            nc.gpsimd.memset(plane[:].bitcast(I32), 0)
+            for quad in range(QUADS):
+                row = QUAD * quad + first_row
+                nc.sync.dma_start(
+                    plane[row : row + SCALE_ROWS].bitcast(I32),
+                    scales[:, SCALE_ROWS * quad : SCALE_ROWS * (quad + 1), :].rearrange("a q n -> q a n").bitcast(I32),
                 )
 
         def load_table(a):
-            nc.sync.dma_start(tab[a][:], tab_words[a].rearrange("p n t -> p (n t)").bitcast(I32))
+            nc.sync.dma_start(tab[a][:], tab_words[a].rearrange("p n j -> p (n j)").bitcast(I32))
 
-        nc.sync.dma_start(
-            eps_sb[:, :, 0:PACK], eps.rearrange("(b p t) -> p b t", p=P, t=PACK)
-        )
+        nc.sync.dma_start(eps_sb[:, :, 0:PACK], eps.rearrange("(rb p t) -> p rb t", p=P, t=PACK))
         nc.sync.dma_start(w4[:].bitcast(I32), w4_words.rearrange("a p n -> p a n").bitcast(I32))
         nc.sync.dma_start(idx[:], offs)
         nc.sync.dma_start(idx2[:], offs2)
-        for q in range(QUADS):
+        for quad in range(QUADS):
             nc.sync.dma_start(
-                tab_sc[32 * q : 32 * q + 8, :].bitcast(I32), tab_scales[:, 4 * q : 4 * q + 4, :].bitcast(I32)
+                tab_sc[QUAD * quad : QUAD * quad + PASSES * SCALE_ROWS, :].bitcast(I32),
+                tab_scales[:, SCALE_ROWS * quad : SCALE_ROWS * (quad + 1), :].bitcast(I32),
             )
 
         wm_raw = {}
         mom_raw = {}
 
-        def load_wm(b):
+        def load_wm(rb):
             for a in range(PASSES):
-                wm_raw[a, b] = placed([P, PACK, K_PASS], F32, f"wm_raw{a}{b}", 18 * b + 8 * a)
-                rows = wm[K_PASS * a : K_PASS * (a + 1), K_PASS * b : K_PASS * (b + 1)]
-                nc.sync.dma_start(wm_raw[a, b][:], rows.rearrange("(p j) c -> p j c", j=PACK))
+                wm_raw[a, rb] = placed([P, PACK, K_PASS], F32, f"wm_raw{a}{rb}", TAB_AT[rb] + WM_RAW * a)
+                rows = wm[K_PASS * a : K_PASS * (a + 1), K_PASS * rb : K_PASS * (rb + 1)]
+                nc.sync.dma_start(wm_raw[a, rb][:], rows.rearrange("(p j) r -> p j r", j=PACK))
 
         def load_mom(half):
             for a in range(PASSES):
-                mom_raw[a, half] = placed([P, PACK, M_HALF], F32, f"mom_raw{a}{half}", 34 + 4 * a)
+                mom_raw[a, half] = placed([P, PACK, M_HALF], F32, f"mom_raw{a}{half}", MOM_AT + 4 * a)
                 rows = mom[K_PASS * a : K_PASS * (a + 1), M_HALF * half : M_HALF * (half + 1)]
                 nc.sync.dma_start(mom_raw[a, half][:], rows.rearrange("(p j) m -> p j m", j=PACK))
 
-        r0 = held([P, PASSES * PACK], F32, "r0")
-        nc.scalar.activation(r0[:].rearrange("p (b t) -> p b t", t=PACK), eps_sb[:, :, 0:PACK], ACT.Abs_reciprocal_sqrt)
+        e = held([P, SLICES], F32, "r0")
+        nc.scalar.activation(e[:].rearrange("p (rb t) -> p rb t", t=PACK), eps_sb[:, :, 0:PACK], ACT.Abs_reciprocal_sqrt)
         load_table(0)
-        nc.gpsimd.memset(w4_sc[:].bitcast(I32), 0)
-        load_scales(nc.sync, w4_sc, w4_scales, 0)
+        load_plane(w4_sc, w4_scales, 0)
 
         w4p = held([P, PASSES, 2 * H], U8, "w4p")
         w4p_sc = held([P, PASSES, H], U8, "w4p_sc")
         nc.vector.tensor_copy(
-            w4p[:].bitcast(U16).rearrange("p a (b t m) -> p (a b) t m", b=2, t=PACK),
-            w4[:].bitcast(U16).rearrange("p a (b m t) -> p (a b) t m", b=2, t=PACK),
+            w4p[:].bitcast(U16).rearrange("p a (rb t c) -> p (a rb) t c", rb=PASSES, t=PACK),
+            w4[:].bitcast(U16).rearrange("p a (rb c t) -> p (a rb) t c", rb=PASSES, t=PACK),
         )
-
         load_table(1)
 
         nc.vector.tensor_copy(v_planes[0][:], tab_sc[:].indirect(idx[:]))
-        nc.scalar.dma_start(v_planes[1][0:112, :].bitcast(I32), v_planes[0][4:116, :].bitcast(I32))
+        nc.scalar.dma_start(
+            v_planes[1][0:MOVED_ROWS, :].bitcast(I32), v_planes[0][SCALE_ROWS : SCALE_ROWS + MOVED_ROWS, :].bitcast(I32)
+        )
         v = {}
 
-        def gather_words(a, jh):
-            v[a, jh] = held([P, BANK], U32, f"v{a}{jh}")
-            cols = BANK // 16
-            nc.vector.tensor_copy(v[a, jh][:], tab[a][:].bitcast(U32).indirect(idx[:, cols * jh : cols * (jh + 1)]))
+        def gather_words(a, part):
+            v[a, part] = held([P, BANK], U32, f"v{a}{part}")
+            cols = BANK // GROUP
+            entries = idx[:, cols * part : cols * (part + 1)]
+            nc.vector.tensor_copy(v[a, part][:], tab[a][:].bitcast(U32).indirect(entries))
 
         nc.vector.tensor_copy(
-            w4p_sc[:].rearrange("p a (b t m) -> p (a b) t m", b=2, t=PACK),
-            w4_sc[:].rearrange("p a (b m t) -> p (a b) t m", b=2, t=PACK),
+            w4p_sc[:].rearrange("p a (rb t c) -> p (a rb) t c", rb=PASSES, t=PACK),
+            w4_sc[:].rearrange("p a (rb c t) -> p (a rb) t c", rb=PASSES, t=PACK),
         )
         nc.sync.dma_start(wgt_sb[:], wgt)
-        gather_words(0, 0)
-        gather_words(0, 1)
+        parts = range(S // BANK)
+        for part in parts:
+            gather_words(0, part)
         load_mom(0)
         load_wm(0)
-        gather_words(1, 0)
-        gather_words(1, 1)
+        for part in parts:
+            gather_words(1, part)
         load_wm(1)
 
-        def h_pass(bank, s, jh, a):
+        def h_pass(bank, s, part, a):
             nc.tensor.matmul_mx(
                 out=bank[:],
                 lhsT=w4p[:, a, 2 * P * s : 2 * P * (s + 1)].bitcast(FP4X4),
                 lhsT_scale=w4p_sc[:, a, P * s : P * (s + 1)],
-                rhs=v[a, jh][:].bitcast(FP8X4),
-                rhs_scale=v_planes[a][:, BANK * jh : BANK * (jh + 1)],
+                rhs=v[a, part][:].bitcast(FP8X4),
+                rhs_scale=v_planes[a][:, BANK * part : BANK * (part + 1)],
                 start=(a == 0),
                 stop=(a == PASSES - 1),
             )
 
-        h = [held([P, S], F32, f"h{s}") for s in range(2 * PACK)]
-        x = [held([P, PACK, M], F32, "x0"), placed([P, PACK, M], F32, "x1", 42)]
+        h = [held([P, S], F32, f"h{s}") for s in range(SLICES)]
+        x = [held([P, PACK, M], F32, "x0"), placed([P, PACK, M], F32, "x1", X1_AT)]
 
-        def h_out(bank, s, jh):
-            nc.scalar.activation(h[s][:, BANK * jh : BANK * (jh + 1)], bank[:], ACT.Copy, scale=r0[:, s : s + 1])
+        def h_out(bank, s, part):
+            nc.scalar.activation(h[s][:, BANK * part : BANK * (part + 1)], bank[:], ACT.Copy, scale=e[:, s : s + 1])
 
         def pick(s):
             nc.vector.tensor_tensor(x[s // PACK][:, s % PACK, :], h[s][:].indirect(idx2[:]), wgt_sb[:], MULT)
@@ -160,54 +177,55 @@ def tile_list_sharded_embedding_preconditioning_kernel(
         wm_sc = {}
         mom_q = {}
         mom_sc = {}
-        rounded = {}
+        wm_rounded = {}
+        mom_rounded = {}
 
-        def round_wm(a, b, copy):
-            if (a, b) == (1, 1):
-                rounded[a, b] = placed([P, PACK * K_PASS], BF16, "rounded_last", 42)
+        def round_wm(a, rb, copy):
+            if (a, rb) == (PASSES - 1, PASSES - 1):
+                wm_rounded[a, rb] = placed([P, PACK * K_PASS], BF16, "rounded_last", X1_AT)
             else:
-                rounded[a, b] = stage.tile([P, PACK * K_PASS], BF16, name="rounded", tag="rounded", align_bytes=64)
+                wm_rounded[a, rb] = stage.tile([P, PACK * K_PASS], BF16, name="rounded", tag="rounded", align_bytes=64)
             copy(
-                rounded[a, b][:].rearrange("p (u e m j) -> p u m j e", u=2, e=2, j=PACK),
-                wm_raw[a, b][:].rearrange("p j (m u e) -> p u m j e", u=2, e=2),
+                wm_rounded[a, rb][:].rearrange("p (u w c j) -> p u c j w", u=2, w=2, j=PACK),
+                wm_raw[a, rb][:].rearrange("p j (c u w) -> p u c j w", u=2, w=2),
             )
 
-        def quantise_wm(a, b):
-            wm_q[a, b] = held([P, K_PASS], U32, f"wm_q{a}{b}")
-            wm_sc[a, b] = held([P, K_PASS], U8, f"wm_sc{a}{b}")
-            nc.vector.quantize_mx(out=wm_q[a, b][:].bitcast(FP8X4), scales=wm_sc[a, b][:], in_=rounded[a, b][:])
+        def quantise_wm(a, rb):
+            wm_q[a, rb] = held([P, K_PASS], U32, f"wm_q{a}{rb}")
+            wm_sc[a, rb] = held([P, K_PASS], U8, f"wm_sc{a}{rb}")
+            nc.vector.quantize_mx(out=wm_q[a, rb][:].bitcast(FP8X4), scales=wm_sc[a, rb][:], in_=wm_rounded[a, rb][:])
 
-        def round_mom(half, copy):
-            rounded[half] = stage.tile([P, PACK * K_PASS], BF16, name="rounded", tag="rounded", align_bytes=64)
+        def round_mom(half, *copies):
+            mom_rounded[half] = stage.tile([P, PACK * K_PASS], BF16, name="rounded", tag="rounded", align_bytes=64)
             for a in range(PASSES):
-                part = rounded[half][:, PACK * M_HALF * a : PACK * M_HALF * (a + 1)]
-                copy(
-                    part.rearrange("p (c i j) -> p c j i", i=4, j=PACK),
+                of_pass = mom_rounded[half][:, PACK * M_HALF * a : PACK * M_HALF * (a + 1)]
+                copies[a](
+                    of_pass.rearrange("p (c i j) -> p c j i", i=4, j=PACK),
                     mom_raw[a, half][:].rearrange("p j (c i) -> p c j i", i=4),
                 )
 
         def quantise_mom(half):
             mom_q[half] = held([P, PASSES * M_HALF], U32, f"mom_q{half}")
             mom_sc[half] = held([P, PASSES * M_HALF], U8, f"mom_sc{half}")
-            nc.vector.quantize_mx(out=mom_q[half][:].bitcast(FP8X4), scales=mom_sc[half][:], in_=rounded[half][:])
+            nc.vector.quantize_mx(out=mom_q[half][:].bitcast(FP8X4), scales=mom_sc[half][:], in_=mom_rounded[half][:])
 
         damp = {}
 
-        def project_momentum(b, half):
-            damp[b, half] = held([P, PACK, M_HALF], F32, f"damp{b}{half}")
-            if (b, half) == (0, 0):
-                square = placed([P, PACK, M_HALF], F32, "square00", 30)
+        def damping(rb, half):
+            damp[rb, half] = held([P, PACK, M_HALF], F32, f"damp{rb}{half}")
+            if (rb, half) == (0, 0):
+                square = placed([P, PACK, M_HALF], F32, "square00", LAST_WM_AT + 4)
             else:
-                square = held([P, PACK, M_HALF], F32, f"square{b}{half}")
-            for pair in range(2):
+                square = held([P, PACK, M_HALF], F32, f"square{rb}{half}")
+            for pair in range(PACK // 2):
                 bank = psum.tile([P, BANK], F32, name="bank", tag="bank")
                 for u in range(2):
                     t = 2 * pair + u
                     for a in range(PASSES):
                         nc.tensor.matmul_mx(
                             out=bank[:, M_HALF * u : M_HALF * (u + 1)],
-                            lhsT=wm_q[a, b][:, P * t : P * (t + 1)].bitcast(FP8X4),
-                            lhsT_scale=wm_sc[a, b][:, P * t : P * (t + 1)],
+                            lhsT=wm_q[a, rb][:, P * t : P * (t + 1)].bitcast(FP8X4),
+                            lhsT_scale=wm_sc[a, rb][:, P * t : P * (t + 1)],
                             rhs=mom_q[half][:, M_HALF * a : M_HALF * (a + 1)].bitcast(FP8X4),
                             rhs_scale=mom_sc[half][:, M_HALF * a : M_HALF * (a + 1)],
                             start=(a == 0),
@@ -215,116 +233,116 @@ def tile_list_sharded_embedding_preconditioning_kernel(
                         )
                 for u in range(2):
                     t = 2 * pair + u
-                    s = PACK * b + t
+                    s = PACK * rb + t
                     nc.scalar.activation(
-                        square[:, t, :], bank[:, M_HALF * u : M_HALF * (u + 1)], ACT.Square, scale=r0[:, s : s + 1]
+                        square[:, t, :], bank[:, M_HALF * u : M_HALF * (u + 1)], ACT.Square, scale=e[:, s : s + 1]
                     )
-            nc.scalar.activation(damp[b, half][:], square[:], ACT.Abs_reciprocal_sqrt, bias=one[:])
+            nc.scalar.activation(damp[rb, half][:], square[:], ACT.Abs_reciprocal_sqrt, bias=one[:])
 
         z = {}
         z_q = {}
         z_sc = {}
 
-        def precondition(b, half):
-            z[b, half] = held([P, PACK * M_HALF], BF16, f"z{b}{half}")
+        def precondition(rb, half):
+            z[rb, half] = held([P, PACK * M_HALF], BF16, f"z{rb}{half}")
             nc.vector.tensor_tensor(
-                z[b, half][:].rearrange("p (c i t) -> p c t i", i=2, t=PACK),
-                x[b][:, :, M_HALF * half : M_HALF * (half + 1)].rearrange("p t (c i) -> p c t i", i=2),
-                damp[b, half][:].rearrange("p t (c i) -> p c t i", i=2),
+                z[rb, half][:].rearrange("p (c i t) -> p c t i", i=2, t=PACK),
+                x[rb][:, :, M_HALF * half : M_HALF * (half + 1)].rearrange("p t (c i) -> p c t i", i=2),
+                damp[rb, half][:].rearrange("p t (c i) -> p c t i", i=2),
                 MULT,
             )
 
-        def quantise_z(b, half):
-            z_q[b, half] = held([P, M_HALF], U32, f"z_q{b}{half}")
-            z_sc[b, half] = held([P, M_HALF], U8, f"z_sc{b}{half}")
-            nc.vector.quantize_mx(out=z_q[b, half][:].bitcast(FP8X4), scales=z_sc[b, half][:], in_=z[b, half][:])
+        def quantise_z(rb, half):
+            z_q[rb, half] = held([P, M_HALF], U32, f"z_q{rb}{half}")
+            z_sc[rb, half] = held([P, M_HALF], U8, f"z_sc{rb}{half}")
+            nc.vector.quantize_mx(out=z_q[rb, half][:].bitcast(FP8X4), scales=z_sc[rb, half][:], in_=z[rb, half][:])
 
         y_banks = {}
 
-        def rotate_pass(half, b):
+        def rotate_pass(half, rb):
             for pair in range(N // P // 2):
-                if b == 0:
+                if rb == 0:
                     y_banks[half, pair] = psum.tile([P, BANK], F32, name="bank", tag="bank")
                 for u in range(2):
-                    s = 2 * pair + u
+                    n_tile = 2 * pair + u
                     nc.tensor.matmul_mx(
                         out=y_banks[half, pair][:, M_HALF * u : M_HALF * (u + 1)],
-                        lhsT=wr[:, b, P * s : P * (s + 1)].bitcast(FP8X4),
-                        lhsT_scale=wr_sc[WR_ROW:, b, P * s : P * (s + 1)],
-                        rhs=z_q[b, half][:].bitcast(FP8X4),
-                        rhs_scale=z_sc[b, half][:],
-                        start=(b == 0 and u == 0),
-                        stop=(b == PASSES - 1 and u == 1),
+                        lhsT=wr[:, rb, P * n_tile : P * (n_tile + 1)].bitcast(FP8X4),
+                        lhsT_scale=wr_sc[WR_ROW:, rb, P * n_tile : P * (n_tile + 1)],
+                        rhs=z_q[rb, half][:].bitcast(FP8X4),
+                        rhs_scale=z_sc[rb, half][:],
+                        start=(rb == 0 and u == 0),
+                        stop=(rb == PASSES - 1 and u == 1),
                     )
 
         def store(half):
             y_half = held([P, N // P, M_HALF], F32, f"y{half}", None if half else "square11")
             for pair in range(N // P // 2):
-                y = y_half[:, 2 * pair : 2 * pair + 2, :]
+                n_tiles = slice(2 * pair, 2 * pair + 2)
+                y = y_half[:, n_tiles, :]
                 bank = y_banks[half, pair][:].rearrange("p (u m) -> p u m", u=2)
                 if (half, pair) in ON_VECTOR:
-                    rates = rate_sb[:, 2 * pair : 2 * pair + 2].unsqueeze(2).to_broadcast([P, 2, M_HALF])
+                    rates = rate_sb[:, n_tiles].unsqueeze(2).to_broadcast([P, 2, M_HALF])
                     nc.vector.tensor_tensor(y[:], bank, rates, MULT)
                 else:
                     for u in range(2):
-                        s = 2 * pair + u
-                        nc.scalar.activation(y[:, u, :], bank[:, u, :], ACT.Copy, scale=rate_sb[:, s : s + 1])
-                rows = out.rearrange("(s p) m -> p s m", p=P)
-                nc.sync.dma_start(rows[:, 2 * pair : 2 * pair + 2, M_HALF * half : M_HALF * (half + 1)], y[:])
+                        n_tile = 2 * pair + u
+                        nc.scalar.activation(y[:, u, :], bank[:, u, :], ACT.Copy, scale=rate_sb[:, n_tile : n_tile + 1])
+                rows = out.rearrange("(n_tile p) m -> p n_tile m", p=P)
+                nc.sync.dma_start(rows[:, n_tiles, M_HALF * half : M_HALF * (half + 1)], y[:])
 
-        first = {}
-        for jh in range(2):
+        first_banks = {}
+        for part in parts:
             for s in range(PACK):
-                first[s, jh] = psum.tile([P, BANK], F32, name="bank", tag="bank")
-                h_pass(first[s, jh], s, jh, 0)
-        for jh in range(2):
+                first_banks[s, part] = psum.tile([P, BANK], F32, name="bank", tag="bank")
+                h_pass(first_banks[s, part], s, part, 0)
+        for part in parts:
             for s in range(PACK):
-                h_pass(first[s, jh], s, jh, 1)
-        round_mom(0, nc.vector.tensor_copy)
+                h_pass(first_banks[s, part], s, part, 1)
+
+        round_mom(0, nc.vector.tensor_copy, nc.vector.tensor_copy)
         load_mom(1)
         quantise_mom(0)
         round_wm(0, 0, nc.vector.tensor_copy)
-        nc.sync.dma_start(wr[:], wr_words.rearrange("a p n t -> p a (n t)").bitcast(I32))
+        nc.sync.dma_start(wr[:], wr_words.rearrange("a p n j -> p a (n j)").bitcast(I32))
         quantise_wm(0, 0)
         round_wm(1, 0, nc.vector.tensor_copy)
         quantise_wm(1, 0)
         for s in range(PACK):
-            for jh in range(2):
-                h_out(first[s, jh], s, jh)
+            for part in parts:
+                h_out(first_banks[s, part], s, part)
             pick(s)
-        for s in range(PACK, 2 * PACK):
-            for jh in range(2):
+        for s in range(PACK, SLICES):
+            for part in parts:
                 bank = psum.tile([P, BANK], F32, name="bank", tag="bank")
                 for a in range(PASSES):
-                    h_pass(bank, s, jh, a)
-                h_out(bank, s, jh)
+                    h_pass(bank, s, part, a)
+                h_out(bank, s, part)
         round_wm(0, 1, nc.scalar.copy)
-        nc.gpsimd.memset(wr_sc[:].bitcast(I32), 0)
-        load_scales(nc.sync, wr_sc, wr_scales, WR_ROW)
+        load_plane(wr_sc, wr_scales, WR_ROW)
         with nc.allow_non_contiguous_dma(reason="one rate a partition"):
-            nc.sync.dma_start(rate_sb[:], rate.rearrange("(s p) -> p s", p=P))
+            nc.sync.dma_start(rate_sb[:], rate.rearrange("(n_tile p) -> p n_tile", p=P))
         round_wm(1, 1, nc.scalar.copy)
-        round_mom(1, nc.vector.tensor_copy)
+        round_mom(1, nc.vector.tensor_copy, nc.scalar.copy)
         quantise_mom(1)
         quantise_wm(0, 1)
         quantise_wm(1, 1)
-        project_momentum(0, 0)
-        project_momentum(1, 0)
-        project_momentum(0, 1)
-        project_momentum(1, 1)
-        for s in range(PACK, 2 * PACK):
+
+        for half in range(2):
+            for rb in range(PASSES):
+                damping(rb, half)
+        for s in range(PACK, SLICES):
             pick(s)
-        precondition(0, 0)
-        precondition(1, 0)
-        quantise_z(0, 0)
-        quantise_z(1, 0)
-        rotate_pass(0, 0)
-        rotate_pass(0, 1)
-        precondition(0, 1)
-        precondition(1, 1)
-        quantise_z(0, 1)
-        rotate_pass(1, 0)
-        quantise_z(1, 1)
-        rotate_pass(1, 1)
-        store(0)
-        store(1)
+
+        for step in (precondition, quantise_z):
+            for rb in range(PASSES):
+                step(rb, 0)
+        for rb in range(PASSES):
+            rotate_pass(0, rb)
+        for rb in range(PASSES):
+            precondition(rb, 1)
+        for rb in range(PASSES):
+            quantise_z(rb, 1)
+            rotate_pass(1, rb)
+        for half in range(2):
+            store(half)

@@ -31,14 +31,15 @@ WR_ROW = 8
 MOVED_ROWS = 112
 ON_VECTOR = ((1, 0), (1, 2))
 
-TAB_AT = (0, 18)
+TAB_AT = (0, 16)
 WM_RAW = 8
-W4_SC_AT = 16
+WGT_AT = 33
+DEALT_AT = 34
+W4_ROW = QUAD - SCALE_ROWS
 WR_AT = TAB_AT[0]
 LAST_WM_AT = TAB_AT[1] + WM_RAW
-MOM_AT = 34
-TAB_SC_AT = MOM_AT + 2
-X1_AT = 42
+MOM_AT = 35
+X1_AT = 44
 
 
 def tile_list_sharded_embedding_preconditioning_kernel(
@@ -60,25 +61,26 @@ def tile_list_sharded_embedding_preconditioning_kernel(
         idx = keep.tile([P, S // GROUP], U16, name="idx")
         idx2 = keep.tile([P, M // GROUP], U16, name="idx2")
         tab = [placed([P, T], I32, f"tab{a}", TAB_AT[a]) for a in range(PASSES)]
-        tab_sc = placed([P, T], U8, "tab_sc", TAB_SC_AT)
+        tab_sc = held([P, T], U8, "tab_sc")
         w4 = placed([P, PASSES, 2 * H], U8, "w4", TAB_AT[1])
-        w4_sc = placed([P, PASSES, H], U8, "w4_sc", W4_SC_AT)
+        w_sc = held([P, PASSES, H], U8, "w_sc")
         wr = placed([P, PASSES, N], I32, "wr", WR_AT)
-        wr_sc = placed([P, PASSES, N], U8, "wr_sc", LAST_WM_AT)
-        eps_sb = shared.tile([P, PASSES, 2 * PACK], F32, name="eps_sb", offset=1024 * W4_SC_AT - 32)
+        eps_sb = held([P, PASSES, 2 * PACK], F32, "eps_sb")
         rate_sb = placed([P, N // P], F32, "rate_sb", LAST_WM_AT + 2)
-        wgt_sb = placed([P, M], F32, "wgt_sb", W4_SC_AT)
+        wgt_sb = placed([P, M], F32, "wgt_sb", WGT_AT)
         v_planes = [held([P, S], U8, f"v_sc{a}") for a in range(PASSES)]
 
         one = held([P, 1], F32, "one")
-        nc.gpsimd.memset(one[:], 1.0)
-        nc.scalar.activation(one[:], one[:], ACT.Abs_reciprocal_sqrt)
         nc.vector.memset(tab_sc[:, 0 : T // 2].bitcast(I32), 0)
         nc.gpsimd.memset(tab_sc[:, T // 2 : T].bitcast(I32), 0)
-        nc.vector.memset(v_planes[1][:].bitcast(I32), 0)
+        for quad in range(QUADS):
+            nc.vector.memset(w_sc[QUAD * quad : QUAD * quad + W4_ROW].bitcast(I32), 0)
+        w4p_sc = held([P, PASSES, H], U8, "w4p_sc")
+        nc.gpsimd.memset(w4p_sc[P - QUAD :].bitcast(I32), 0)
+        nc.gpsimd.memset(v_planes[1][P - QUAD :].bitcast(I32), 0)
+        nc.gpsimd.memset(one[:], 1.0)
 
         def load_plane(plane, scales, first_row):
-            nc.gpsimd.memset(plane[:].bitcast(I32), 0)
             for quad in range(QUADS):
                 row = QUAD * quad + first_row
                 nc.sync.dma_start(
@@ -89,15 +91,17 @@ def tile_list_sharded_embedding_preconditioning_kernel(
         def load_table(a):
             nc.sync.dma_start(tab[a][:], tab_words[a].rearrange("p n j -> p (n j)").bitcast(I32))
 
-        nc.sync.dma_start(eps_sb[:, :, 0:PACK], eps.rearrange("(rb p t) -> p rb t", p=P, t=PACK))
-        nc.sync.dma_start(w4[:].bitcast(I32), w4_words.rearrange("a p n -> p a n").bitcast(I32))
         nc.sync.dma_start(idx[:], offs)
         nc.sync.dma_start(idx2[:], offs2)
-        for quad in range(QUADS):
+        load_plane(w_sc, w4_scales, W4_ROW)
+        nc.sync.dma_start(w4[:].bitcast(I32), w4_words.rearrange("a p n -> p a n").bitcast(I32))
+        nc.sync.dma_start(eps_sb[:, :, 0:PACK], eps.rearrange("(rb p t) -> p rb t", p=P, t=PACK))
+        for row in range(SCALE_ROWS):
             nc.sync.dma_start(
-                tab_sc[QUAD * quad : QUAD * quad + PASSES * SCALE_ROWS, :].bitcast(I32),
-                tab_scales[:, SCALE_ROWS * quad : SCALE_ROWS * (quad + 1), :].bitcast(I32),
+                tab_sc[row:P:GROUP, :].bitcast(I32),
+                tab_scales.rearrange("a (quad r) n -> r quad a n", r=SCALE_ROWS)[row].bitcast(I32),
             )
+        load_table(0)
 
         wm_raw = {}
         mom_raw = {}
@@ -109,28 +113,30 @@ def tile_list_sharded_embedding_preconditioning_kernel(
                 nc.sync.dma_start(wm_raw[a, rb][:], rows.rearrange("(p j) r -> p j r", j=PACK))
 
         def load_mom(half):
+            mom_raw[half] = placed([P, PASSES * PACK * M_HALF], F32, f"mom_raw{half}", MOM_AT)
             for a in range(PASSES):
-                mom_raw[a, half] = placed([P, PACK, M_HALF], F32, f"mom_raw{a}{half}", MOM_AT + 4 * a)
                 rows = mom[K_PASS * a : K_PASS * (a + 1), M_HALF * half : M_HALF * (half + 1)]
-                nc.sync.dma_start(mom_raw[a, half][:], rows.rearrange("(p j) m -> p j m", j=PACK))
+                nc.sync.dma_start(mom_pass(half, a), rows.rearrange("(p j) m -> p j m", j=PACK))
 
-        e = held([P, SLICES], F32, "r0")
-        nc.scalar.activation(e[:].rearrange("p (rb t) -> p rb t", t=PACK), eps_sb[:, :, 0:PACK], ACT.Abs_reciprocal_sqrt)
-        load_table(0)
-        load_plane(w4_sc, w4_scales, 0)
+        def mom_pass(half, a):
+            return mom_raw[half][:, PACK * M_HALF * a : PACK * M_HALF * (a + 1)].rearrange("p (j m) -> p j m", j=PACK)
 
+
+        dealt = placed([P, PASSES, H], U8, "dealt", DEALT_AT)
+        nc.vector.tensor_copy(
+            dealt[:].rearrange("p a (rb t c) -> p (a rb) t c", rb=PASSES, t=PACK),
+            w_sc[:].rearrange("p a (rb c t) -> p (a rb) t c", rb=PASSES, t=PACK),
+        )
+        nc.scalar.dma_start(w4p_sc[0 : P - W4_ROW].bitcast(I32), dealt[W4_ROW:].bitcast(I32))
         w4p = held([P, PASSES, 2 * H], U8, "w4p")
-        w4p_sc = held([P, PASSES, H], U8, "w4p_sc")
         nc.vector.tensor_copy(
             w4p[:].bitcast(U16).rearrange("p a (rb t c) -> p (a rb) t c", rb=PASSES, t=PACK),
             w4[:].bitcast(U16).rearrange("p a (rb c t) -> p (a rb) t c", rb=PASSES, t=PACK),
         )
         load_table(1)
+        e = held([P, SLICES], F32, "r0")
+        nc.scalar.activation(e[:].rearrange("p (rb t) -> p rb t", t=PACK), eps_sb[:, :, 0:PACK], ACT.Abs_reciprocal_sqrt)
 
-        nc.vector.tensor_copy(v_planes[0][:], tab_sc[:].indirect(idx[:]))
-        nc.scalar.dma_start(
-            v_planes[1][0:MOVED_ROWS, :].bitcast(I32), v_planes[0][SCALE_ROWS : SCALE_ROWS + MOVED_ROWS, :].bitcast(I32)
-        )
         v = {}
 
         def gather_words(a, part):
@@ -139,14 +145,14 @@ def tile_list_sharded_embedding_preconditioning_kernel(
             entries = idx[:, cols * part : cols * (part + 1)]
             nc.vector.tensor_copy(v[a, part][:], tab[a][:].bitcast(U32).indirect(entries))
 
-        nc.vector.tensor_copy(
-            w4p_sc[:].rearrange("p a (rb t c) -> p (a rb) t c", rb=PASSES, t=PACK),
-            w4_sc[:].rearrange("p a (rb c t) -> p (a rb) t c", rb=PASSES, t=PACK),
-        )
-        nc.sync.dma_start(wgt_sb[:], wgt)
         parts = range(S // BANK)
+        nc.vector.tensor_copy(v_planes[0][:], tab_sc[:].indirect(idx[:]))
+        nc.scalar.dma_start(
+            v_planes[1][0:MOVED_ROWS, :].bitcast(I32), v_planes[0][GROUP : GROUP + MOVED_ROWS, :].bitcast(I32)
+        )
         for part in parts:
             gather_words(0, part)
+        nc.sync.dma_start(wgt_sb[:], wgt)
         load_mom(0)
         load_wm(0)
         for part in parts:
@@ -181,8 +187,8 @@ def tile_list_sharded_embedding_preconditioning_kernel(
         mom_rounded = {}
 
         def round_wm(a, rb, copy):
-            if (a, rb) == (PASSES - 1, PASSES - 1):
-                wm_rounded[a, rb] = placed([P, PACK * K_PASS], BF16, "rounded_last", X1_AT)
+            if rb == PASSES - 1:
+                wm_rounded[a, rb] = placed([P, PACK * K_PASS], BF16, f"rounded_last{a}", X1_AT + 4 * a)
             else:
                 wm_rounded[a, rb] = stage.tile([P, PACK * K_PASS], BF16, name="rounded", tag="rounded", align_bytes=64)
             copy(
@@ -201,7 +207,7 @@ def tile_list_sharded_embedding_preconditioning_kernel(
                 of_pass = mom_rounded[half][:, PACK * M_HALF * a : PACK * M_HALF * (a + 1)]
                 copies[a](
                     of_pass.rearrange("p (c i j) -> p c j i", i=4, j=PACK),
-                    mom_raw[a, half][:].rearrange("p j (c i) -> p c j i", i=4),
+                    mom_pass(half, a).rearrange("p j (c i) -> p c j i", i=4),
                 )
 
         def quantise_mom(half):
@@ -268,7 +274,7 @@ def tile_list_sharded_embedding_preconditioning_kernel(
                     nc.tensor.matmul_mx(
                         out=y_banks[half, pair][:, M_HALF * u : M_HALF * (u + 1)],
                         lhsT=wr[:, rb, P * n_tile : P * (n_tile + 1)].bitcast(FP8X4),
-                        lhsT_scale=wr_sc[WR_ROW:, rb, P * n_tile : P * (n_tile + 1)],
+                        lhsT_scale=w4p_sc[WR_ROW:, rb, P * n_tile : P * (n_tile + 1)],
                         rhs=z_q[rb, half][:].bitcast(FP8X4),
                         rhs_scale=z_sc[rb, half][:],
                         start=(rb == 0 and u == 0),
@@ -318,8 +324,8 @@ def tile_list_sharded_embedding_preconditioning_kernel(
                 for a in range(PASSES):
                     h_pass(bank, s, part, a)
                 h_out(bank, s, part)
+        load_plane(w4p_sc, wr_scales, WR_ROW)
         round_wm(0, 1, nc.scalar.copy)
-        load_plane(wr_sc, wr_scales, WR_ROW)
         with nc.allow_non_contiguous_dma(reason="one rate a partition"):
             nc.sync.dma_start(rate_sb[:], rate.rearrange("(n_tile p) -> p n_tile", p=P))
         round_wm(1, 1, nc.scalar.copy)

@@ -23,23 +23,22 @@ PASSES = 2
 QUADS = 4
 QUAD = P // QUADS
 SCALE_ROWS = 4
+ARRIVE = P - QUAD
 GROUP = 16
 BANK = 512
 SLICES = H // P
 M_HALF = M // 2
 WR_ROW = 8
-MOVED_ROWS = 112
+OF_V, OF_W = 0, 1
 ON_VECTOR = ((1, 0), (1, 2))
 
-TAB_AT = (0, 16)
-WM_RAW = 8
-WGT_AT = 33
-DEALT_AT = 34
-W4_ROW = QUAD - SCALE_ROWS
-WR_AT = TAB_AT[0]
-LAST_WM_AT = TAB_AT[1] + WM_RAW
-MOM_AT = 35
-X1_AT = 44
+TAB_AT = (0, 20)
+WM_AT = {(0, 0): 0, (1, 0): 16, (0, 1): 24, (1, 1): 8}
+V_SC_AT = 28
+MOM_AT = (8, 32)
+WR_AT = WM_AT[1, 0]
+RATE_AT = WM_AT[0, 1]
+HELD_PICKS_AT = 768
 
 
 def tile_list_sharded_embedding_preconditioning_kernel(
@@ -60,82 +59,57 @@ def tile_list_sharded_embedding_preconditioning_kernel(
 
         idx = keep.tile([P, S // GROUP], U16, name="idx")
         idx2 = keep.tile([P, M // GROUP], U16, name="idx2")
-        tab = [placed([P, T], I32, f"tab{a}", TAB_AT[a]) for a in range(PASSES)]
+        tab = {}
+        wgt_sb = held([P, M], F32, "wgt_sb")
         tab_sc = held([P, T], U8, "tab_sc")
-        w4 = placed([P, PASSES, 2 * H], U8, "w4", TAB_AT[1])
-        w_sc = held([P, PASSES, H], U8, "w_sc")
-        wr = placed([P, PASSES, N], I32, "wr", WR_AT)
+        w4_sc = held([P, H], U8, "w4_sc")
+        w4 = held([P, PASSES, 2 * H], U8, "w4")
         eps_sb = held([P, PASSES, 2 * PACK], F32, "eps_sb")
-        rate_sb = placed([P, N // P], F32, "rate_sb", LAST_WM_AT + 2)
-        wgt_sb = placed([P, M], F32, "wgt_sb", WGT_AT)
-        v_planes = [held([P, S], U8, f"v_sc{a}") for a in range(PASSES)]
-
+        planes = held([P, PASSES, 2, H], U8, "planes")
         one = held([P, 1], F32, "one")
-        nc.vector.memset(tab_sc[:, 0 : T // 2].bitcast(I32), 0)
-        nc.gpsimd.memset(tab_sc[:, T // 2 : T].bitcast(I32), 0)
-        for quad in range(QUADS):
-            nc.vector.memset(w_sc[QUAD * quad : QUAD * quad + W4_ROW].bitcast(I32), 0)
-        w4p_sc = held([P, PASSES, H], U8, "w4p_sc")
-        nc.gpsimd.memset(w4p_sc[P - QUAD :].bitcast(I32), 0)
-        nc.gpsimd.memset(v_planes[1][P - QUAD :].bitcast(I32), 0)
-        nc.gpsimd.memset(one[:], 1.0)
 
-        def load_plane(plane, scales, first_row):
-            for quad in range(QUADS):
-                row = QUAD * quad + first_row
-                nc.sync.dma_start(
-                    plane[row : row + SCALE_ROWS].bitcast(I32),
-                    scales[:, SCALE_ROWS * quad : SCALE_ROWS * (quad + 1), :].rearrange("a q n -> q a n").bitcast(I32),
-                )
+        nc.vector.memset(w4_sc[0:ARRIVE].bitcast(I32), 0)
+        nc.vector.memset(tab_sc[0:ARRIVE].bitcast(I32), 0)
+        nc.vector.memset(planes[:].rearrange("p a w n -> p (a w n)").bitcast(I32), 0)
+        nc.vector.memset(one[:], 1.0)
 
         def load_table(a):
+            tab[a] = placed([P, T], I32, f"tab{a}", TAB_AT[a])
             nc.sync.dma_start(tab[a][:], tab_words[a].rearrange("p n j -> p (n j)").bitcast(I32))
 
         nc.sync.dma_start(idx[:], offs)
-        nc.sync.dma_start(idx2[:], offs2)
-        load_plane(w_sc, w4_scales, W4_ROW)
+        for rows, scales in ((tab_sc, tab_scales), (w4_sc, w4_scales)):
+            nc.sync.dma_start(rows[ARRIVE:, :].bitcast(I32), scales.rearrange("a q n -> q a n").bitcast(I32))
         nc.sync.dma_start(w4[:].bitcast(I32), w4_words.rearrange("a p n -> p a n").bitcast(I32))
+        nc.sync.dma_start(idx2[:], offs2)
         nc.sync.dma_start(eps_sb[:, :, 0:PACK], eps.rearrange("(rb p t) -> p rb t", p=P, t=PACK))
-        for row in range(SCALE_ROWS):
-            nc.sync.dma_start(
-                tab_sc[row:P:GROUP, :].bitcast(I32),
-                tab_scales.rearrange("a (quad r) n -> r quad a n", r=SCALE_ROWS)[row].bitcast(I32),
-            )
         load_table(0)
+        nc.sync.dma_start(wgt_sb[:], wgt)
 
-        wm_raw = {}
-        mom_raw = {}
+        e = held([P, SLICES], F32, "e")
+        nc.scalar.activation(e[:].rearrange("p (rb t) -> p rb t", t=PACK), eps_sb[:, :, 0:PACK], ACT.Abs_reciprocal_sqrt)
 
-        def load_wm(rb):
-            for a in range(PASSES):
-                wm_raw[a, rb] = placed([P, PACK, K_PASS], F32, f"wm_raw{a}{rb}", TAB_AT[rb] + WM_RAW * a)
-                rows = wm[K_PASS * a : K_PASS * (a + 1), K_PASS * rb : K_PASS * (rb + 1)]
-                nc.sync.dma_start(wm_raw[a, rb][:], rows.rearrange("(p j) r -> p j r", j=PACK))
-
-        def load_mom(half):
-            mom_raw[half] = placed([P, PASSES * PACK * M_HALF], F32, f"mom_raw{half}", MOM_AT)
-            for a in range(PASSES):
-                rows = mom[K_PASS * a : K_PASS * (a + 1), M_HALF * half : M_HALF * (half + 1)]
-                nc.sync.dma_start(mom_pass(half, a), rows.rearrange("(p j) m -> p j m", j=PACK))
-
-        def mom_pass(half, a):
-            return mom_raw[half][:, PACK * M_HALF * a : PACK * M_HALF * (a + 1)].rearrange("p (j m) -> p j m", j=PACK)
-
-
-        dealt = placed([P, PASSES, H], U8, "dealt", DEALT_AT)
+        staged = held([P, 2, H], U8, "staged")
         nc.vector.tensor_copy(
-            dealt[:].rearrange("p a (rb t c) -> p (a rb) t c", rb=PASSES, t=PACK),
-            w_sc[:].rearrange("p a (rb c t) -> p (a rb) t c", rb=PASSES, t=PACK),
+            staged[:, OF_W, :].rearrange("p (rb t c) -> p rb t c", rb=PASSES, t=PACK),
+            w4_sc[:].rearrange("p (rb c t) -> p rb t c", rb=PASSES, t=PACK),
         )
-        nc.scalar.dma_start(w4p_sc[0 : P - W4_ROW].bitcast(I32), dealt[W4_ROW:].bitcast(I32))
+        v_sc = placed([P, S], U8, "v_sc", V_SC_AT)
+        nc.vector.tensor_copy(v_sc[:], tab_sc[:].indirect(idx[:]))
+        nc.vector.tensor_copy(staged[:, OF_V, :].bitcast(I32), v_sc[:].bitcast(I32))
+        for quad in range(QUADS):
+            row = QUAD * quad
+            first = ARRIVE + PASSES * SCALE_ROWS * quad
+            nc.sync.dma_start(
+                planes[row : row + SCALE_ROWS].rearrange("p a w n -> p a (w n)").bitcast(I32),
+                staged[first : first + PASSES * SCALE_ROWS].rearrange("p w n -> p (w n)").bitcast(I32),
+            )
+        load_table(1)
         w4p = held([P, PASSES, 2 * H], U8, "w4p")
         nc.vector.tensor_copy(
             w4p[:].bitcast(U16).rearrange("p a (rb t c) -> p (a rb) t c", rb=PASSES, t=PACK),
             w4[:].bitcast(U16).rearrange("p a (rb c t) -> p (a rb) t c", rb=PASSES, t=PACK),
         )
-        load_table(1)
-        e = held([P, SLICES], F32, "r0")
-        nc.scalar.activation(e[:].rearrange("p (rb t) -> p rb t", t=PACK), eps_sb[:, :, 0:PACK], ACT.Abs_reciprocal_sqrt)
 
         v = {}
 
@@ -146,38 +120,53 @@ def tile_list_sharded_embedding_preconditioning_kernel(
             nc.vector.tensor_copy(v[a, part][:], tab[a][:].bitcast(U32).indirect(entries))
 
         parts = range(S // BANK)
-        nc.vector.tensor_copy(v_planes[0][:], tab_sc[:].indirect(idx[:]))
-        nc.scalar.dma_start(
-            v_planes[1][0:MOVED_ROWS, :].bitcast(I32), v_planes[0][GROUP : GROUP + MOVED_ROWS, :].bitcast(I32)
-        )
+        wm_raw = {}
+        mom_raw = {}
+
+        def load_wm(a, rb):
+            wm_raw[a, rb] = placed([P, PACK, K_PASS], F32, f"wm_raw{a}{rb}", WM_AT[a, rb])
+            rows = wm[K_PASS * a : K_PASS * (a + 1), K_PASS * rb : K_PASS * (rb + 1)]
+            nc.sync.dma_start(wm_raw[a, rb][:], rows.rearrange("(p j) r -> p j r", j=PACK))
+
+        def mom_pass(half, a):
+            return mom_raw[half][:, PACK * M_HALF * a : PACK * M_HALF * (a + 1)].rearrange("p (j m) -> p j m", j=PACK)
+
+        def load_mom(half):
+            mom_raw[half] = placed([P, PASSES * PACK * M_HALF], F32, f"mom_raw{half}", MOM_AT[half])
+            for a in range(PASSES):
+                rows = mom[K_PASS * a : K_PASS * (a + 1), M_HALF * half : M_HALF * (half + 1)]
+                nc.sync.dma_start(mom_pass(half, a), rows.rearrange("(p j) m -> p j m", j=PACK))
+
         for part in parts:
             gather_words(0, part)
-        nc.sync.dma_start(wgt_sb[:], wgt)
+        load_wm(0, 0)
         load_mom(0)
-        load_wm(0)
         for part in parts:
             gather_words(1, part)
-        load_wm(1)
+        load_wm(1, 0)
+        load_wm(0, 1)
+        load_mom(1)
 
         def h_pass(bank, s, part, a):
             nc.tensor.matmul_mx(
                 out=bank[:],
                 lhsT=w4p[:, a, 2 * P * s : 2 * P * (s + 1)].bitcast(FP4X4),
-                lhsT_scale=w4p_sc[:, a, P * s : P * (s + 1)],
+                lhsT_scale=planes[:, a, OF_W, P * s : P * (s + 1)],
                 rhs=v[a, part][:].bitcast(FP8X4),
-                rhs_scale=v_planes[a][:, BANK * part : BANK * (part + 1)],
+                rhs_scale=planes[:, a, OF_V, BANK * part : BANK * (part + 1)],
                 start=(a == 0),
                 stop=(a == PASSES - 1),
             )
 
         h = [held([P, S], F32, f"h{s}") for s in range(SLICES)]
-        x = [held([P, PACK, M], F32, "x0"), placed([P, PACK, M], F32, "x1", X1_AT)]
+        x = [held([P, PACK * M], F32, f"x{rb}") for rb in range(PASSES)]
 
         def h_out(bank, s, part):
             nc.scalar.activation(h[s][:, BANK * part : BANK * (part + 1)], bank[:], ACT.Copy, scale=e[:, s : s + 1])
 
         def pick(s):
-            nc.vector.tensor_tensor(x[s // PACK][:, s % PACK, :], h[s][:].indirect(idx2[:]), wgt_sb[:], MULT)
+            t = s % PACK
+            nc.vector.tensor_tensor(x[s // PACK][:, M * t : M * (t + 1)], h[s][:].indirect(idx2[:]), wgt_sb[:], MULT)
 
         wm_q = {}
         wm_sc = {}
@@ -187,25 +176,26 @@ def tile_list_sharded_embedding_preconditioning_kernel(
         mom_rounded = {}
 
         def round_wm(a, rb, copy):
-            if rb == PASSES - 1:
-                wm_rounded[a, rb] = placed([P, PACK * K_PASS], BF16, f"rounded_last{a}", X1_AT + 4 * a)
+            if (a, rb) == (1, 1):
+                wm_rounded[a, rb] = x[1][:, HELD_PICKS_AT : HELD_PICKS_AT + PACK * K_PASS // 2].bitcast(BF16)
             else:
-                wm_rounded[a, rb] = stage.tile([P, PACK * K_PASS], BF16, name="rounded", tag="rounded", align_bytes=64)
+                rounded = stage.tile([P, PACK * K_PASS], BF16, name="rounded", tag="rounded", align_bytes=64)
+                wm_rounded[a, rb] = rounded[:]
             copy(
-                wm_rounded[a, rb][:].rearrange("p (u w c j) -> p u c j w", u=2, w=2, j=PACK),
+                wm_rounded[a, rb].rearrange("p (u w c j) -> p u c j w", u=2, w=2, j=PACK),
                 wm_raw[a, rb][:].rearrange("p j (c u w) -> p u c j w", u=2, w=2),
             )
 
         def quantise_wm(a, rb):
             wm_q[a, rb] = held([P, K_PASS], U32, f"wm_q{a}{rb}")
             wm_sc[a, rb] = held([P, K_PASS], U8, f"wm_sc{a}{rb}")
-            nc.vector.quantize_mx(out=wm_q[a, rb][:].bitcast(FP8X4), scales=wm_sc[a, rb][:], in_=wm_rounded[a, rb][:])
+            nc.vector.quantize_mx(out=wm_q[a, rb][:].bitcast(FP8X4), scales=wm_sc[a, rb][:], in_=wm_rounded[a, rb])
 
-        def round_mom(half, *copies):
+        def round_mom(half, copy):
             mom_rounded[half] = stage.tile([P, PACK * K_PASS], BF16, name="rounded", tag="rounded", align_bytes=64)
             for a in range(PASSES):
                 of_pass = mom_rounded[half][:, PACK * M_HALF * a : PACK * M_HALF * (a + 1)]
-                copies[a](
+                copy(
                     of_pass.rearrange("p (c i j) -> p c j i", i=4, j=PACK),
                     mom_pass(half, a).rearrange("p j (c i) -> p c j i", i=4),
                 )
@@ -220,7 +210,7 @@ def tile_list_sharded_embedding_preconditioning_kernel(
         def damping(rb, half):
             damp[rb, half] = held([P, PACK, M_HALF], F32, f"damp{rb}{half}")
             if (rb, half) == (0, 0):
-                square = placed([P, PACK, M_HALF], F32, "square00", LAST_WM_AT + 4)
+                square = placed([P, PACK, M_HALF], F32, "square00", MOM_AT[1] + 4)
             else:
                 square = held([P, PACK, M_HALF], F32, f"square{rb}{half}")
             for pair in range(PACK // 2):
@@ -251,9 +241,10 @@ def tile_list_sharded_embedding_preconditioning_kernel(
 
         def precondition(rb, half):
             z[rb, half] = held([P, PACK * M_HALF], BF16, f"z{rb}{half}")
+            x_half = x[rb][:].rearrange("p (t m) -> p t m", t=PACK)[:, :, M_HALF * half : M_HALF * (half + 1)]
             nc.vector.tensor_tensor(
                 z[rb, half][:].rearrange("p (c i t) -> p c t i", i=2, t=PACK),
-                x[rb][:, :, M_HALF * half : M_HALF * (half + 1)].rearrange("p t (c i) -> p c t i", i=2),
+                x_half.rearrange("p t (c i) -> p c t i", i=2),
                 damp[rb, half][:].rearrange("p t (c i) -> p c t i", i=2),
                 MULT,
             )
@@ -274,7 +265,7 @@ def tile_list_sharded_embedding_preconditioning_kernel(
                     nc.tensor.matmul_mx(
                         out=y_banks[half, pair][:, M_HALF * u : M_HALF * (u + 1)],
                         lhsT=wr[:, rb, P * n_tile : P * (n_tile + 1)].bitcast(FP8X4),
-                        lhsT_scale=w4p_sc[WR_ROW:, rb, P * n_tile : P * (n_tile + 1)],
+                        lhsT_scale=planes[WR_ROW:, rb, OF_W, P * n_tile : P * (n_tile + 1)],
                         rhs=z_q[rb, half][:].bitcast(FP8X4),
                         rhs_scale=z_sc[rb, half][:],
                         start=(rb == 0 and u == 0),
@@ -306,13 +297,14 @@ def tile_list_sharded_embedding_preconditioning_kernel(
             for s in range(PACK):
                 h_pass(first_banks[s, part], s, part, 1)
 
-        round_mom(0, nc.vector.tensor_copy, nc.vector.tensor_copy)
-        load_mom(1)
-        quantise_mom(0)
         round_wm(0, 0, nc.vector.tensor_copy)
-        nc.sync.dma_start(wr[:], wr_words.rearrange("a p n j -> p a (n j)").bitcast(I32))
         quantise_wm(0, 0)
+        round_mom(0, nc.vector.tensor_copy)
+        load_wm(1, 1)
+        quantise_mom(0)
         round_wm(1, 0, nc.vector.tensor_copy)
+        wr = placed([P, PASSES, N], I32, "wr", WR_AT)
+        nc.sync.dma_start(wr[:], wr_words.rearrange("a p n j -> p a (n j)").bitcast(I32))
         quantise_wm(1, 0)
         for s in range(PACK):
             for part in parts:
@@ -324,20 +316,27 @@ def tile_list_sharded_embedding_preconditioning_kernel(
                 for a in range(PASSES):
                     h_pass(bank, s, part, a)
                 h_out(bank, s, part)
-        load_plane(w4p_sc, wr_scales, WR_ROW)
+        pick(PACK)
+        for quad in range(QUADS):
+            row = QUAD * quad + WR_ROW
+            nc.sync.dma_start(
+                planes[row : row + SCALE_ROWS, :, OF_W, :].bitcast(I32),
+                wr_scales[:, SCALE_ROWS * quad : SCALE_ROWS * (quad + 1), :].rearrange("a q n -> q a n").bitcast(I32),
+            )
         round_wm(0, 1, nc.scalar.copy)
+        rate_sb = placed([P, N // P], F32, "rate_sb", RATE_AT)
         with nc.allow_non_contiguous_dma(reason="one rate a partition"):
             nc.sync.dma_start(rate_sb[:], rate.rearrange("(n_tile p) -> p n_tile", p=P))
-        round_wm(1, 1, nc.scalar.copy)
-        round_mom(1, nc.vector.tensor_copy, nc.scalar.copy)
-        quantise_mom(1)
+        round_mom(1, nc.scalar.copy)
         quantise_wm(0, 1)
+        round_wm(1, 1, nc.vector.tensor_copy)
         quantise_wm(1, 1)
+        quantise_mom(1)
 
         for half in range(2):
             for rb in range(PASSES):
                 damping(rb, half)
-        for s in range(PACK, SLICES):
+        for s in range(PACK + 1, SLICES):
             pick(s)
 
         for step in (precondition, quantise_z):

@@ -32,10 +32,11 @@ WR_ROW = 8
 OF_V, OF_W = 0, 1
 ON_VECTOR = ((1, 0), (1, 2))
 
-TAB_AT = (0, 20)
-WM_AT = {(0, 0): 0, (1, 0): 16, (0, 1): 24, (1, 1): 8}
-V_SC_AT = 28
-MOM_AT = (8, 32)
+TAB_AT = (0, 22)
+WM_AT = {(0, 0): 0, (1, 0): 18, (0, 1): 26, (1, 1): 10}
+WGT_AT = 8
+V_SC_AT = 30
+MOM_AT = (10, 34)
 WR_AT = WM_AT[1, 0]
 RATE_AT = WM_AT[0, 1]
 HELD_PICKS_AT = 768
@@ -60,7 +61,6 @@ def tile_list_sharded_embedding_preconditioning_kernel(
         idx = keep.tile([P, S // GROUP], U16, name="idx")
         idx2 = keep.tile([P, M // GROUP], U16, name="idx2")
         tab = {}
-        wgt_sb = held([P, M], F32, "wgt_sb")
         tab_sc = held([P, T], U8, "tab_sc")
         w4_sc = held([P, H], U8, "w4_sc")
         w4 = held([P, PASSES, 2 * H], U8, "w4")
@@ -84,18 +84,17 @@ def tile_list_sharded_embedding_preconditioning_kernel(
         nc.sync.dma_start(idx2[:], offs2)
         nc.sync.dma_start(eps_sb[:, :, 0:PACK], eps.rearrange("(rb p t) -> p rb t", p=P, t=PACK))
         load_table(0)
-        nc.sync.dma_start(wgt_sb[:], wgt)
 
         e = held([P, SLICES], F32, "e")
         nc.scalar.activation(e[:].rearrange("p (rb t) -> p rb t", t=PACK), eps_sb[:, :, 0:PACK], ACT.Abs_reciprocal_sqrt)
 
+        v_sc = placed([P, S], U8, "v_sc", V_SC_AT)
+        nc.vector.tensor_copy(v_sc[:], tab_sc[:].indirect(idx[:]))
         staged = held([P, 2, H], U8, "staged")
         nc.vector.tensor_copy(
             staged[:, OF_W, :].rearrange("p (rb t c) -> p rb t c", rb=PASSES, t=PACK),
             w4_sc[:].rearrange("p (rb c t) -> p rb t c", rb=PASSES, t=PACK),
         )
-        v_sc = placed([P, S], U8, "v_sc", V_SC_AT)
-        nc.vector.tensor_copy(v_sc[:], tab_sc[:].indirect(idx[:]))
         nc.vector.tensor_copy(staged[:, OF_V, :].bitcast(I32), v_sc[:].bitcast(I32))
         for quad in range(QUADS):
             row = QUAD * quad
@@ -140,6 +139,8 @@ def tile_list_sharded_embedding_preconditioning_kernel(
         for part in parts:
             gather_words(0, part)
         load_wm(0, 0)
+        wgt_sb = placed([P, M], F32, "wgt_sb", WGT_AT)
+        nc.sync.dma_start(wgt_sb[:], wgt)
         load_mom(0)
         for part in parts:
             gather_words(1, part)

@@ -30,16 +30,24 @@ SLICES = H // P
 M_HALF = M // 2
 WR_ROW = 8
 OF_V, OF_W = 0, 1
+MOVE_ORDER = (0, 2, 1, 3)
 ON_VECTOR = ((1, 0), (1, 2))
 
 TAB_AT = (0, 22)
-WM_AT = {(0, 0): 0, (1, 0): 18, (0, 1): 26, (1, 1): 10}
+WM_AT = {(0, 0): 0, (1, 0): 18, (0, 1): 26}
 WGT_AT = 8
 V_SC_AT = 30
 MOM_AT = (10, 34)
 WR_AT = WM_AT[1, 0]
 RATE_AT = WM_AT[0, 1]
-HELD_PICKS_AT = 768
+X1_STEP = 4 * M
+SQUARES = PACK * M_HALF
+LATE_MOM_AT = (M, 3 * X1_STEP - SQUARES)
+SQUARES_AT = {
+    (1, 0): 2 * X1_STEP + M_HALF,
+    (0, 0): 3 * X1_STEP + M_HALF - SQUARES,
+    (0, 1): 3 * X1_STEP + M_HALF,
+}
 
 
 def tile_list_sharded_embedding_preconditioning_kernel(
@@ -50,13 +58,16 @@ def tile_list_sharded_embedding_preconditioning_kernel(
         keep = ctx.enter_context(tc.tile_pool(name="keep", bufs=1))
         stage = ctx.enter_context(tc.tile_pool(name="stage", bufs=3))
         shared = ctx.enter_context(tc.tile_pool(name="shared", bufs=1))
-        psum = ctx.enter_context(tc.psum_pool(name="psum", bufs=8))
+        psum = ctx.enter_context(tc.psum_pool(name="psum", bufs=1))
 
         def held(shape, dtype, name, tag=None):
             return keep.tile(shape, dtype, name=name, tag=tag or name, align_bytes=64)
 
         def placed(shape, dtype, name, kib):
             return shared.tile(shape, dtype, name=name, align_bytes=64, offset=1024 * kib)
+
+        def bank_tile(number):
+            return psum.tile([P, BANK], F32, name=f"bank{number}", tag=f"bank{number}")
 
         idx = keep.tile([P, S // GROUP], U16, name="idx")
         idx2 = keep.tile([P, M // GROUP], U16, name="idx2")
@@ -79,7 +90,7 @@ def tile_list_sharded_embedding_preconditioning_kernel(
 
         nc.sync.dma_start(idx[:], offs)
         for rows, scales in ((tab_sc, tab_scales), (w4_sc, w4_scales)):
-            nc.sync.dma_start(rows[ARRIVE:, :].bitcast(I32), scales.rearrange("a q n -> q a n").bitcast(I32))
+            nc.sync.dma_start(rows[ARRIVE:, :].bitcast(I32), scales.rearrange("a q n -> (a q) n").bitcast(I32))
         nc.sync.dma_start(w4[:].bitcast(I32), w4_words.rearrange("a p n -> p a n").bitcast(I32))
         nc.sync.dma_start(idx2[:], offs2)
         nc.sync.dma_start(eps_sb[:, :, 0:PACK], eps.rearrange("(rb p t) -> p rb t", p=P, t=PACK))
@@ -96,14 +107,19 @@ def tile_list_sharded_embedding_preconditioning_kernel(
             w4_sc[:].rearrange("p (rb c t) -> p rb t c", rb=PASSES, t=PACK),
         )
         nc.vector.tensor_copy(staged[:, OF_V, :].bitcast(I32), v_sc[:].bitcast(I32))
-        for quad in range(QUADS):
-            row = QUAD * quad
-            first = ARRIVE + PASSES * SCALE_ROWS * quad
-            nc.sync.dma_start(
-                planes[row : row + SCALE_ROWS].rearrange("p a w n -> p a (w n)").bitcast(I32),
-                staged[first : first + PASSES * SCALE_ROWS].rearrange("p w n -> p (w n)").bitcast(I32),
-            )
+
+        def move_rows(a):
+            for quad in MOVE_ORDER:
+                row = QUAD * quad
+                first = ARRIVE + SCALE_ROWS * (QUADS * a + quad)
+                nc.sync.dma_start(
+                    planes[row : row + SCALE_ROWS, a].rearrange("p w n -> p (w n)").bitcast(I32),
+                    staged[first : first + SCALE_ROWS].rearrange("p w n -> p (w n)").bitcast(I32),
+                )
+
+        move_rows(0)
         load_table(1)
+        move_rows(1)
         w4p = held([P, PASSES, 2 * H], U8, "w4p")
         nc.vector.tensor_copy(
             w4p[:].bitcast(U16).rearrange("p a (rb t c) -> p (a rb) t c", rb=PASSES, t=PACK),
@@ -123,15 +139,24 @@ def tile_list_sharded_embedding_preconditioning_kernel(
         mom_raw = {}
 
         def load_wm(a, rb):
-            wm_raw[a, rb] = placed([P, PACK, K_PASS], F32, f"wm_raw{a}{rb}", WM_AT[a, rb])
+            if (a, rb) == (1, 1):
+                wm_raw[a, rb] = x[1][:].rearrange("p (j r) -> p j r", j=PACK)[:, :, 0:K_PASS]
+            else:
+                wm_raw[a, rb] = placed([P, PACK, K_PASS], F32, f"wm_raw{a}{rb}", WM_AT[a, rb])
             rows = wm[K_PASS * a : K_PASS * (a + 1), K_PASS * rb : K_PASS * (rb + 1)]
             nc.sync.dma_start(wm_raw[a, rb][:], rows.rearrange("(p j) r -> p j r", j=PACK))
 
         def mom_pass(half, a):
-            return mom_raw[half][:, PACK * M_HALF * a : PACK * M_HALF * (a + 1)].rearrange("p (j m) -> p j m", j=PACK)
+            at = LATE_MOM_AT[a] if half else PACK * M_HALF * a
+            return mom_raw[half][:, at : at + PACK * M_HALF].rearrange("p (j m) -> p j m", j=PACK)
+
+        x = [held([P, PACK * M], F32, "x0"), placed([P, PACK * X1_STEP], F32, "x1", MOM_AT[1])]
 
         def load_mom(half):
-            mom_raw[half] = placed([P, PASSES * PACK * M_HALF], F32, f"mom_raw{half}", MOM_AT[half])
+            if half:
+                mom_raw[half] = x[1]
+            else:
+                mom_raw[half] = placed([P, PASSES * PACK * M_HALF], F32, f"mom_raw{half}", MOM_AT[half])
             for a in range(PASSES):
                 rows = mom[K_PASS * a : K_PASS * (a + 1), M_HALF * half : M_HALF * (half + 1)]
                 nc.sync.dma_start(mom_pass(half, a), rows.rearrange("(p j) m -> p j m", j=PACK))
@@ -147,6 +172,7 @@ def tile_list_sharded_embedding_preconditioning_kernel(
         load_wm(1, 0)
         load_wm(0, 1)
         load_mom(1)
+        load_wm(1, 1)
 
         def h_pass(bank, s, part, a):
             nc.tensor.matmul_mx(
@@ -160,14 +186,23 @@ def tile_list_sharded_embedding_preconditioning_kernel(
             )
 
         h = [held([P, S], F32, f"h{s}") for s in range(SLICES)]
-        x = [held([P, PACK * M], F32, f"x{rb}") for rb in range(PASSES)]
 
         def h_out(bank, s, part):
             nc.scalar.activation(h[s][:, BANK * part : BANK * (part + 1)], bank[:], ACT.Copy, scale=e[:, s : s + 1])
 
         def pick(s):
-            t = s % PACK
-            nc.vector.tensor_tensor(x[s // PACK][:, M * t : M * (t + 1)], h[s][:].indirect(idx2[:]), wgt_sb[:], MULT)
+            at = (M, X1_STEP)[s // PACK] * (s % PACK)
+            nc.vector.tensor_tensor(x[s // PACK][:, at : at + M], h[s][:].indirect(idx2[:]), wgt_sb[:], MULT)
+
+        def pick_half(s, half):
+            at = X1_STEP * (s - PACK) + M_HALF * half
+            cols = M_HALF // GROUP
+            nc.vector.tensor_tensor(
+                x[1][:, at : at + M_HALF],
+                h[s][:].indirect(idx2[:, cols * half : cols * (half + 1)]),
+                wgt_sb[:, M_HALF * half : M_HALF * (half + 1)],
+                MULT,
+            )
 
         wm_q = {}
         wm_sc = {}
@@ -178,10 +213,10 @@ def tile_list_sharded_embedding_preconditioning_kernel(
 
         def round_wm(a, rb, copy):
             if (a, rb) == (1, 1):
-                wm_rounded[a, rb] = x[1][:, HELD_PICKS_AT : HELD_PICKS_AT + PACK * K_PASS // 2].bitcast(BF16)
+                rounded = held([P, PACK * K_PASS], BF16, "rounded_last")
             else:
                 rounded = stage.tile([P, PACK * K_PASS], BF16, name="rounded", tag="rounded", align_bytes=64)
-                wm_rounded[a, rb] = rounded[:]
+            wm_rounded[a, rb] = rounded[:]
             copy(
                 wm_rounded[a, rb].rearrange("p (u w c j) -> p u c j w", u=2, w=2, j=PACK),
                 wm_raw[a, rb][:].rearrange("p j (c u w) -> p u c j w", u=2, w=2),
@@ -202,7 +237,7 @@ def tile_list_sharded_embedding_preconditioning_kernel(
                 )
 
         def quantise_mom(half):
-            mom_q[half] = held([P, PASSES * M_HALF], U32, f"mom_q{half}")
+            mom_q[half] = held([P, PASSES * M_HALF], U32, f"mom_q{half}", "rounded_last" if half else None)
             mom_sc[half] = held([P, PASSES * M_HALF], U8, f"mom_sc{half}")
             nc.vector.quantize_mx(out=mom_q[half][:].bitcast(FP8X4), scales=mom_sc[half][:], in_=mom_rounded[half][:])
 
@@ -210,12 +245,13 @@ def tile_list_sharded_embedding_preconditioning_kernel(
 
         def damping(rb, half):
             damp[rb, half] = held([P, PACK, M_HALF], F32, f"damp{rb}{half}")
-            if (rb, half) == (0, 0):
-                square = placed([P, PACK, M_HALF], F32, "square00", MOM_AT[1] + 4)
+            if (rb, half) in SQUARES_AT:
+                at = SQUARES_AT[rb, half]
+                square = x[1][:, at : at + SQUARES].rearrange("p (t m) -> p t m", t=PACK)
             else:
                 square = held([P, PACK, M_HALF], F32, f"square{rb}{half}")
             for pair in range(PACK // 2):
-                bank = psum.tile([P, BANK], F32, name="bank", tag="bank")
+                bank = bank_tile(4 * half + 2 * rb + pair)
                 for u in range(2):
                     t = 2 * pair + u
                     for a in range(PASSES):
@@ -242,7 +278,7 @@ def tile_list_sharded_embedding_preconditioning_kernel(
 
         def precondition(rb, half):
             z[rb, half] = held([P, PACK * M_HALF], BF16, f"z{rb}{half}")
-            x_half = x[rb][:].rearrange("p (t m) -> p t m", t=PACK)[:, :, M_HALF * half : M_HALF * (half + 1)]
+            x_half = x[rb][:, 0 : PACK * (M, X1_STEP)[rb]].rearrange("p (t m) -> p t m", t=PACK)[:, :, M_HALF * half : M_HALF * (half + 1)]
             nc.vector.tensor_tensor(
                 z[rb, half][:].rearrange("p (c i t) -> p c t i", i=2, t=PACK),
                 x_half.rearrange("p t (c i) -> p c t i", i=2),
@@ -260,7 +296,7 @@ def tile_list_sharded_embedding_preconditioning_kernel(
         def rotate_pass(half, rb):
             for pair in range(N // P // 2):
                 if rb == 0:
-                    y_banks[half, pair] = psum.tile([P, BANK], F32, name="bank", tag="bank")
+                    y_banks[half, pair] = bank_tile(4 * half + pair)
                 for u in range(2):
                     n_tile = 2 * pair + u
                     nc.tensor.matmul_mx(
@@ -292,7 +328,7 @@ def tile_list_sharded_embedding_preconditioning_kernel(
         first_banks = {}
         for part in parts:
             for s in range(PACK):
-                first_banks[s, part] = psum.tile([P, BANK], F32, name="bank", tag="bank")
+                first_banks[s, part] = bank_tile(2 * s + part)
                 h_pass(first_banks[s, part], s, part, 0)
         for part in parts:
             for s in range(PACK):
@@ -301,7 +337,6 @@ def tile_list_sharded_embedding_preconditioning_kernel(
         round_wm(0, 0, nc.vector.tensor_copy)
         quantise_wm(0, 0)
         round_mom(0, nc.vector.tensor_copy)
-        load_wm(1, 1)
         quantise_mom(0)
         round_wm(1, 0, nc.vector.tensor_copy)
         wr = placed([P, PASSES, N], I32, "wr", WR_AT)
@@ -313,12 +348,11 @@ def tile_list_sharded_embedding_preconditioning_kernel(
             pick(s)
         for s in range(PACK, SLICES):
             for part in parts:
-                bank = psum.tile([P, BANK], F32, name="bank", tag="bank")
+                bank = bank_tile(2 * (s - PACK) + part)
                 for a in range(PASSES):
                     h_pass(bank, s, part, a)
                 h_out(bank, s, part)
-        pick(PACK)
-        for quad in range(QUADS):
+        for quad in MOVE_ORDER:
             row = QUAD * quad + WR_ROW
             nc.sync.dma_start(
                 planes[row : row + SCALE_ROWS, :, OF_W, :].bitcast(I32),
@@ -329,26 +363,31 @@ def tile_list_sharded_embedding_preconditioning_kernel(
         with nc.allow_non_contiguous_dma(reason="one rate a partition"):
             nc.sync.dma_start(rate_sb[:], rate.rearrange("(n_tile p) -> p n_tile", p=P))
         round_mom(1, nc.scalar.copy)
-        quantise_wm(0, 1)
         round_wm(1, 1, nc.vector.tensor_copy)
         quantise_wm(1, 1)
+        quantise_wm(0, 1)
         quantise_mom(1)
 
         for half in range(2):
             for rb in range(PASSES):
                 damping(rb, half)
-        for s in range(PACK + 1, SLICES):
-            pick(s)
-
-        for step in (precondition, quantise_z):
-            for rb in range(PASSES):
-                step(rb, 0)
-        for rb in range(PASSES):
-            rotate_pass(0, rb)
-        for rb in range(PASSES):
-            precondition(rb, 1)
-        for rb in range(PASSES):
-            quantise_z(rb, 1)
-            rotate_pass(1, rb)
+        pick(SLICES - 4)
+        pick(SLICES - 3)
+        pick_half(SLICES - 2, 0)
+        precondition(0, 0)
+        pick_half(SLICES - 1, 0)
+        quantise_z(0, 0)
+        rotate_pass(0, 0)
+        precondition(1, 0)
+        pick_half(SLICES - 2, 1)
+        quantise_z(1, 0)
+        rotate_pass(0, 1)
+        precondition(0, 1)
+        pick_half(SLICES - 1, 1)
+        quantise_z(0, 1)
+        rotate_pass(1, 0)
+        precondition(1, 1)
+        quantise_z(1, 1)
+        rotate_pass(1, 1)
         for half in range(2):
             store(half)

@@ -218,8 +218,8 @@ def tile_list_sharded_embedding_preconditioning_kernel(
                 rounded = stage.tile([P, PACK * K_PASS], BF16, name="rounded", tag="rounded", align_bytes=64)
             wm_rounded[a, rb] = rounded[:]
             copy(
-                wm_rounded[a, rb].rearrange("p (u w c j) -> p u c j w", u=2, w=2, j=PACK),
-                wm_raw[a, rb][:].rearrange("p j (c u w) -> p u c j w", u=2, w=2),
+                wm_rounded[a, rb].rearrange("p (t c j) -> p c j t", t=PACK, j=PACK),
+                wm_raw[a, rb][:].rearrange("p j (c t) -> p c j t", t=PACK),
             )
 
         def quantise_wm(a, rb):
@@ -280,9 +280,9 @@ def tile_list_sharded_embedding_preconditioning_kernel(
             z[rb, half] = held([P, PACK * M_HALF], BF16, f"z{rb}{half}")
             x_half = x[rb][:, 0 : PACK * (M, X1_STEP)[rb]].rearrange("p (t m) -> p t m", t=PACK)[:, :, M_HALF * half : M_HALF * (half + 1)]
             nc.vector.tensor_tensor(
-                z[rb, half][:].rearrange("p (c i t) -> p c t i", i=2, t=PACK),
-                x_half.rearrange("p t (c i) -> p c t i", i=2),
-                damp[rb, half][:].rearrange("p t (c i) -> p c t i", i=2),
+                z[rb, half][:].rearrange("p (c i t) -> p c t i", i=4, t=PACK),
+                x_half.rearrange("p t (c i) -> p c t i", i=4),
+                damp[rb, half][:].rearrange("p t (c i) -> p c t i", i=4),
                 MULT,
             )
 

@@ -31,9 +31,11 @@ M_HALF = M // 2
 WR_ROW = 8
 OF_V, OF_W = 0, 1
 MOVE_ORDER = (0, 2, 1, 3)
+SPLIT = 96
 ON_VECTOR = ((1, 0), (1, 2))
 
-TAB_AT = (0, 22)
+FIRST, SECOND = 1, 0
+TAB_AT = {FIRST: 0, SECOND: 22}
 WM_AT = {(0, 0): 0, (1, 0): 18, (0, 1): 26}
 WGT_AT = 8
 V_SC_AT = 30
@@ -42,7 +44,8 @@ WR_AT = WM_AT[1, 0]
 RATE_AT = WM_AT[0, 1]
 X1_STEP = 4 * M
 SQUARES = PACK * M_HALF
-LATE_MOM_AT = (M, 3 * X1_STEP - SQUARES)
+WM11_AT = X1_STEP + M_HALF
+LATE_MOM_AT = (3 * X1_STEP + M_HALF - SQUARES, 3 * X1_STEP + M_HALF)
 SQUARES_AT = {
     (1, 0): 2 * X1_STEP + M_HALF,
     (0, 0): 3 * X1_STEP + M_HALF - SQUARES,
@@ -94,7 +97,7 @@ def tile_list_sharded_embedding_preconditioning_kernel(
         nc.sync.dma_start(w4[:].bitcast(I32), w4_words.rearrange("a p n -> p a n").bitcast(I32))
         nc.sync.dma_start(idx2[:], offs2)
         nc.sync.dma_start(eps_sb[:, :, 0:PACK], eps.rearrange("(rb p t) -> p rb t", p=P, t=PACK))
-        load_table(0)
+        load_table(FIRST)
 
         e = held([P, SLICES], F32, "e")
         nc.scalar.activation(e[:].rearrange("p (rb t) -> p rb t", t=PACK), eps_sb[:, :, 0:PACK], ACT.Abs_reciprocal_sqrt)
@@ -117,9 +120,9 @@ def tile_list_sharded_embedding_preconditioning_kernel(
                     staged[first : first + SCALE_ROWS].rearrange("p w n -> p (w n)").bitcast(I32),
                 )
 
-        move_rows(0)
-        load_table(1)
-        move_rows(1)
+        move_rows(FIRST)
+        load_table(SECOND)
+        move_rows(SECOND)
         w4p = held([P, PASSES, 2 * H], U8, "w4p")
         nc.vector.tensor_copy(
             w4p[:].bitcast(U16).rearrange("p a (rb t c) -> p (a rb) t c", rb=PASSES, t=PACK),
@@ -140,7 +143,7 @@ def tile_list_sharded_embedding_preconditioning_kernel(
 
         def load_wm(a, rb):
             if (a, rb) == (1, 1):
-                wm_raw[a, rb] = x[1][:].rearrange("p (j r) -> p j r", j=PACK)[:, :, 0:K_PASS]
+                wm_raw[a, rb] = x[1][:, WM11_AT : WM11_AT + PACK * K_PASS].rearrange("p (j r) -> p j r", j=PACK)
             else:
                 wm_raw[a, rb] = placed([P, PACK, K_PASS], F32, f"wm_raw{a}{rb}", WM_AT[a, rb])
             rows = wm[K_PASS * a : K_PASS * (a + 1), K_PASS * rb : K_PASS * (rb + 1)]
@@ -162,13 +165,13 @@ def tile_list_sharded_embedding_preconditioning_kernel(
                 nc.sync.dma_start(mom_pass(half, a), rows.rearrange("(p j) m -> p j m", j=PACK))
 
         for part in parts:
-            gather_words(0, part)
+            gather_words(FIRST, part)
         load_wm(0, 0)
         wgt_sb = placed([P, M], F32, "wgt_sb", WGT_AT)
         nc.sync.dma_start(wgt_sb[:], wgt)
         load_mom(0)
         for part in parts:
-            gather_words(1, part)
+            gather_words(SECOND, part)
         load_wm(1, 0)
         load_wm(0, 1)
         load_mom(1)
@@ -181,8 +184,8 @@ def tile_list_sharded_embedding_preconditioning_kernel(
                 lhsT_scale=planes[:, a, OF_W, P * s : P * (s + 1)],
                 rhs=v[a, part][:].bitcast(FP8X4),
                 rhs_scale=planes[:, a, OF_V, BANK * part : BANK * (part + 1)],
-                start=(a == 0),
-                stop=(a == PASSES - 1),
+                start=(a == FIRST),
+                stop=(a == SECOND),
             )
 
         h = [held([P, S], F32, f"h{s}") for s in range(SLICES)]
@@ -211,21 +214,20 @@ def tile_list_sharded_embedding_preconditioning_kernel(
         wm_rounded = {}
         mom_rounded = {}
 
-        def round_wm(a, rb, copy):
+        def round_wm(a, rb, copy, cols=slice(0, P)):
             if (a, rb) == (1, 1):
-                rounded = held([P, PACK * K_PASS], BF16, "rounded_last")
-            else:
-                rounded = stage.tile([P, PACK * K_PASS], BF16, name="rounded", tag="rounded", align_bytes=64)
-            wm_rounded[a, rb] = rounded[:]
+                wm_rounded[a, rb] = held([P, PACK * K_PASS], BF16, "rounded_last")
+            elif cols.start == 0:
+                wm_rounded[a, rb] = stage.tile([P, PACK * K_PASS], BF16, name="rounded", tag="rounded", align_bytes=64)
             copy(
-                wm_rounded[a, rb].rearrange("p (t c j) -> p c j t", t=PACK, j=PACK),
-                wm_raw[a, rb][:].rearrange("p j (c t) -> p c j t", t=PACK),
+                wm_rounded[a, rb][:].rearrange("p (t c j) -> p c j t", t=PACK, j=PACK)[:, cols],
+                wm_raw[a, rb][:].rearrange("p j (c t) -> p c j t", t=PACK)[:, cols],
             )
 
         def quantise_wm(a, rb):
             wm_q[a, rb] = held([P, K_PASS], U32, f"wm_q{a}{rb}")
             wm_sc[a, rb] = held([P, K_PASS], U8, f"wm_sc{a}{rb}")
-            nc.vector.quantize_mx(out=wm_q[a, rb][:].bitcast(FP8X4), scales=wm_sc[a, rb][:], in_=wm_rounded[a, rb])
+            nc.vector.quantize_mx(out=wm_q[a, rb][:].bitcast(FP8X4), scales=wm_sc[a, rb][:], in_=wm_rounded[a, rb][:])
 
         def round_mom(half, copy):
             mom_rounded[half] = stage.tile([P, PACK * K_PASS], BF16, name="rounded", tag="rounded", align_bytes=64)
@@ -315,33 +317,33 @@ def tile_list_sharded_embedding_preconditioning_kernel(
                 n_tiles = slice(2 * pair, 2 * pair + 2)
                 y = y_half[:, n_tiles, :]
                 bank = y_banks[half, pair][:].rearrange("p (u m) -> p u m", u=2)
-                if (half, pair) in ON_VECTOR:
-                    rates = rate_sb[:, n_tiles].unsqueeze(2).to_broadcast([P, 2, M_HALF])
-                    nc.vector.tensor_tensor(y[:], bank, rates, MULT)
-                else:
-                    for u in range(2):
-                        n_tile = 2 * pair + u
-                        nc.scalar.activation(y[:, u, :], bank[:, u, :], ACT.Copy, scale=rate_sb[:, n_tile : n_tile + 1])
-                rows = out.rearrange("(n_tile p) m -> p n_tile m", p=P)
-                nc.sync.dma_start(rows[:, n_tiles, M_HALF * half : M_HALF * (half + 1)], y[:])
+                rows = out.rearrange("(n_tile p) m -> p n_tile m", p=P)[:, :, M_HALF * half : M_HALF * (half + 1)]
+                for u in range(2):
+                    n_tile = 2 * pair + u
+                    rates = rate_sb[:, n_tile : n_tile + 1]
+                    if (half, pair) in ON_VECTOR:
+                        nc.vector.tensor_scalar_mul(y[:, u, :], bank[:, u, :], rates)
+                    else:
+                        nc.scalar.activation(y[:, u, :], bank[:, u, :], ACT.Copy, scale=rates)
+                    if pair == 0:
+                        nc.sync.dma_start(rows[:, n_tile, :], y[:, u, :])
+                if pair:
+                    nc.sync.dma_start(rows[:, n_tiles, :], y[:])
 
         first_banks = {}
         for part in parts:
             for s in range(PACK):
                 first_banks[s, part] = bank_tile(2 * s + part)
-                h_pass(first_banks[s, part], s, part, 0)
+                h_pass(first_banks[s, part], s, part, FIRST)
         for part in parts:
             for s in range(PACK):
-                h_pass(first_banks[s, part], s, part, 1)
+                h_pass(first_banks[s, part], s, part, SECOND)
 
         round_wm(0, 0, nc.vector.tensor_copy)
         quantise_wm(0, 0)
         round_mom(0, nc.vector.tensor_copy)
         quantise_mom(0)
-        round_wm(1, 0, nc.vector.tensor_copy)
-        wr = placed([P, PASSES, N], I32, "wr", WR_AT)
-        nc.sync.dma_start(wr[:], wr_words.rearrange("a p n j -> p a (n j)").bitcast(I32))
-        quantise_wm(1, 0)
+        round_wm(1, 0, nc.vector.tensor_copy, slice(0, SPLIT))
         for s in range(PACK):
             for part in parts:
                 h_out(first_banks[s, part], s, part)
@@ -349,15 +351,20 @@ def tile_list_sharded_embedding_preconditioning_kernel(
         for s in range(PACK, SLICES):
             for part in parts:
                 bank = bank_tile(2 * (s - PACK) + part)
-                for a in range(PASSES):
+                for a in (FIRST, SECOND):
                     h_pass(bank, s, part, a)
                 h_out(bank, s, part)
+        pick(PACK)
         for quad in MOVE_ORDER:
             row = QUAD * quad + WR_ROW
             nc.sync.dma_start(
                 planes[row : row + SCALE_ROWS, :, OF_W, :].bitcast(I32),
                 wr_scales[:, SCALE_ROWS * quad : SCALE_ROWS * (quad + 1), :].rearrange("a q n -> q a n").bitcast(I32),
             )
+        round_wm(1, 0, nc.scalar.copy, slice(SPLIT, P))
+        wr = placed([P, PASSES, N], I32, "wr", WR_AT)
+        nc.sync.dma_start(wr[:], wr_words.rearrange("a p n j -> p a (n j)").bitcast(I32))
+        quantise_wm(1, 0)
         round_wm(0, 1, nc.scalar.copy)
         rate_sb = placed([P, N // P], F32, "rate_sb", RATE_AT)
         with nc.allow_non_contiguous_dma(reason="one rate a partition"):
@@ -371,7 +378,6 @@ def tile_list_sharded_embedding_preconditioning_kernel(
         for half in range(2):
             for rb in range(PASSES):
                 damping(rb, half)
-        pick(SLICES - 4)
         pick(SLICES - 3)
         pick_half(SLICES - 2, 0)
         precondition(0, 0)

@@ -31,7 +31,7 @@ M_HALF = M // 2
 WR_ROW = 8
 OF_V, OF_W = 0, 1
 MOVE_ORDER = (0, 2, 1, 3)
-SPLIT = 96
+SPLIT = 64
 ON_VECTOR = ((1, 0), (1, 2))
 
 FIRST, SECOND = 1, 0

@@ -30,16 +30,17 @@ SLICES = H // P
 M_HALF = M // 2
 WR_ROW = 8
 OF_V, OF_W = 0, 1
-MOVE_ORDER = (0, 2, 1, 3)
 SPLIT = 64
 ON_VECTOR = ((1, 0), (1, 2))
 
 FIRST, SECOND = 1, 0
 TAB_AT = {FIRST: 0, SECOND: 22}
-WM_AT = {(0, 0): 0, (1, 0): 18, (0, 1): 26}
-WGT_AT = 8
+TAB_AHEAD = 1024
+WM_AT = {(0, 0): 0, (1, 0): 20, (0, 1): 28}
+W4_LATE_AT = 8
+WGT_AT = 10
 V_SC_AT = 30
-MOM_AT = (10, 34)
+MOM_AT = (12, 36)
 WR_AT = WM_AT[1, 0]
 RATE_AT = WM_AT[0, 1]
 X1_STEP = 4 * M
@@ -77,27 +78,45 @@ def tile_list_sharded_embedding_preconditioning_kernel(
         tab = {}
         tab_sc = held([P, T], U8, "tab_sc")
         w4_sc = held([P, H], U8, "w4_sc")
-        w4 = held([P, PASSES, 2 * H], U8, "w4")
         eps_sb = held([P, PASSES, 2 * PACK], F32, "eps_sb")
-        planes = held([P, PASSES, 2, H], U8, "planes")
+        planes = [held([P, 2, H], U8, f"planes{a}") for a in range(PASSES)]
         one = held([P, 1], F32, "one")
 
         nc.vector.memset(w4_sc[0:ARRIVE].bitcast(I32), 0)
         nc.vector.memset(tab_sc[0:ARRIVE].bitcast(I32), 0)
-        nc.vector.memset(planes[:].rearrange("p a w n -> p (a w n)").bitcast(I32), 0)
+        for a in (FIRST, SECOND):
+            nc.vector.memset(planes[a][:].rearrange("p w n -> p (w n)").bitcast(I32), 0)
         nc.vector.memset(one[:], 1.0)
 
-        def load_table(a):
-            tab[a] = placed([P, T], I32, f"tab{a}", TAB_AT[a])
-            nc.sync.dma_start(tab[a][:], tab_words[a].rearrange("p n j -> p (n j)").bitcast(I32))
+        def load_table(into, a, cols):
+            nc.sync.dma_start(into, tab_words[a].rearrange("p n j -> p (n j)").bitcast(I32)[:, cols])
+
+        w4 = {}
+        w4p = {}
+
+        def load_w4(rb):
+            shape = [P, PASSES, 2 * K_PASS]
+            w4[rb] = placed(shape, U8, "w4_late", W4_LATE_AT) if rb else held(shape, U8, "w4_early")
+            words = w4_words.rearrange("a p n -> p a n")[:, :, 2 * K_PASS * rb : 2 * K_PASS * (rb + 1)]
+            nc.sync.dma_start(w4[rb][:].bitcast(I32), words.bitcast(I32))
+
+        def deal_w4(rb):
+            w4p[rb] = held([P, PASSES, 2 * K_PASS], U8, f"w4p{rb}")
+            nc.vector.tensor_copy(
+                w4p[rb][:].bitcast(U16).rearrange("p a (t c) -> p a t c", t=PACK),
+                w4[rb][:].bitcast(U16).rearrange("p a (c t) -> p a t c", t=PACK),
+            )
 
         nc.sync.dma_start(idx[:], offs)
         for rows, scales in ((tab_sc, tab_scales), (w4_sc, w4_scales)):
             nc.sync.dma_start(rows[ARRIVE:, :].bitcast(I32), scales.rearrange("a q n -> (a q) n").bitcast(I32))
-        nc.sync.dma_start(w4[:].bitcast(I32), w4_words.rearrange("a p n -> p a n").bitcast(I32))
+        load_w4(0)
         nc.sync.dma_start(idx2[:], offs2)
         nc.sync.dma_start(eps_sb[:, :, 0:PACK], eps.rearrange("(rb p t) -> p rb t", p=P, t=PACK))
-        load_table(FIRST)
+        tab[FIRST] = placed([P, T], I32, "tab_first", TAB_AT[FIRST])
+        load_table(tab[FIRST][:], FIRST, slice(0, T))
+        tab_ahead = held([P, TAB_AHEAD], I32, "tab_ahead")
+        load_table(tab_ahead[:], SECOND, slice(0, TAB_AHEAD))
 
         e = held([P, SLICES], F32, "e")
         nc.scalar.activation(e[:].rearrange("p (rb t) -> p rb t", t=PACK), eps_sb[:, :, 0:PACK], ACT.Abs_reciprocal_sqrt)
@@ -112,22 +131,18 @@ def tile_list_sharded_embedding_preconditioning_kernel(
         nc.vector.tensor_copy(staged[:, OF_V, :].bitcast(I32), v_sc[:].bitcast(I32))
 
         def move_rows(a):
-            for quad in MOVE_ORDER:
-                row = QUAD * quad
-                first = ARRIVE + SCALE_ROWS * (QUADS * a + quad)
+            first = ARRIVE + SCALE_ROWS * QUADS * a
+            for r in range(SCALE_ROWS):
                 nc.sync.dma_start(
-                    planes[row : row + SCALE_ROWS, a].rearrange("p w n -> p (w n)").bitcast(I32),
-                    staged[first : first + SCALE_ROWS].rearrange("p w n -> p (w n)").bitcast(I32),
+                    planes[a][r:P:QUAD].rearrange("p w n -> p (w n)").bitcast(I32),
+                    staged[first + r : first + SCALE_ROWS * QUADS : SCALE_ROWS].rearrange("p w n -> p (w n)").bitcast(I32),
                 )
 
         move_rows(FIRST)
-        load_table(SECOND)
+        tab[SECOND] = placed([P, T], I32, "tab_second", TAB_AT[SECOND])
+        load_table(tab[SECOND][:, TAB_AHEAD:], SECOND, slice(TAB_AHEAD, T))
         move_rows(SECOND)
-        w4p = held([P, PASSES, 2 * H], U8, "w4p")
-        nc.vector.tensor_copy(
-            w4p[:].bitcast(U16).rearrange("p a (rb t c) -> p (a rb) t c", rb=PASSES, t=PACK),
-            w4[:].bitcast(U16).rearrange("p a (rb c t) -> p (a rb) t c", rb=PASSES, t=PACK),
-        )
+        deal_w4(0)
 
         v = {}
 
@@ -166,7 +181,9 @@ def tile_list_sharded_embedding_preconditioning_kernel(
 
         for part in parts:
             gather_words(FIRST, part)
+        nc.vector.tensor_copy(tab[SECOND][:, 0:TAB_AHEAD], tab_ahead[:])
         load_wm(0, 0)
+        load_w4(1)
         wgt_sb = placed([P, M], F32, "wgt_sb", WGT_AT)
         nc.sync.dma_start(wgt_sb[:], wgt)
         load_mom(0)
@@ -178,12 +195,13 @@ def tile_list_sharded_embedding_preconditioning_kernel(
         load_wm(1, 1)
 
         def h_pass(bank, s, part, a):
+            rb, t = divmod(s, PACK)
             nc.tensor.matmul_mx(
                 out=bank[:],
-                lhsT=w4p[:, a, 2 * P * s : 2 * P * (s + 1)].bitcast(FP4X4),
-                lhsT_scale=planes[:, a, OF_W, P * s : P * (s + 1)],
+                lhsT=w4p[rb][:, a, 2 * P * t : 2 * P * (t + 1)].bitcast(FP4X4),
+                lhsT_scale=planes[a][:, OF_W, P * s : P * (s + 1)],
                 rhs=v[a, part][:].bitcast(FP8X4),
-                rhs_scale=planes[:, a, OF_V, BANK * part : BANK * (part + 1)],
+                rhs_scale=planes[a][:, OF_V, BANK * part : BANK * (part + 1)],
                 start=(a == FIRST),
                 stop=(a == SECOND),
             )
@@ -304,7 +322,7 @@ def tile_list_sharded_embedding_preconditioning_kernel(
                     nc.tensor.matmul_mx(
                         out=y_banks[half, pair][:, M_HALF * u : M_HALF * (u + 1)],
                         lhsT=wr[:, rb, P * n_tile : P * (n_tile + 1)].bitcast(FP8X4),
-                        lhsT_scale=planes[WR_ROW:, rb, OF_W, P * n_tile : P * (n_tile + 1)],
+                        lhsT_scale=planes[SECOND][WR_ROW:, rb, P * n_tile : P * (n_tile + 1)],
                         rhs=z_q[rb, half][:].bitcast(FP8X4),
                         rhs_scale=z_sc[rb, half][:],
                         start=(rb == 0 and u == 0),
@@ -340,6 +358,7 @@ def tile_list_sharded_embedding_preconditioning_kernel(
                 h_pass(first_banks[s, part], s, part, SECOND)
 
         round_wm(0, 0, nc.vector.tensor_copy)
+        deal_w4(1)
         quantise_wm(0, 0)
         round_mom(0, nc.vector.tensor_copy)
         quantise_mom(0)
@@ -355,11 +374,10 @@ def tile_list_sharded_embedding_preconditioning_kernel(
                     h_pass(bank, s, part, a)
                 h_out(bank, s, part)
         pick(PACK)
-        for quad in MOVE_ORDER:
-            row = QUAD * quad + WR_ROW
+        for r in range(SCALE_ROWS):
             nc.sync.dma_start(
-                planes[row : row + SCALE_ROWS, :, OF_W, :].bitcast(I32),
-                wr_scales[:, SCALE_ROWS * quad : SCALE_ROWS * (quad + 1), :].rearrange("a q n -> q a n").bitcast(I32),
+                planes[SECOND][WR_ROW + r : P : QUAD].bitcast(I32),
+                wr_scales[:, r :: SCALE_ROWS, :].rearrange("a q n -> q a n").bitcast(I32),
             )
         round_wm(1, 0, nc.scalar.copy, slice(SPLIT, P))
         wr = placed([P, PASSES, N], I32, "wr", WR_AT)

@@ -28,6 +28,7 @@ GROUP = 16
 BANK = 512
 SLICES = H // P
 M_HALF = M // 2
+PAIR = 2
 WR_ROW = 8
 OF_V, OF_W = 0, 1
 SPLIT = 64
@@ -238,8 +239,8 @@ def tile_list_sharded_embedding_preconditioning_kernel(
             elif cols.start == 0:
                 wm_rounded[a, rb] = stage.tile([P, PACK * K_PASS], BF16, name="rounded", tag="rounded", align_bytes=64)
             copy(
-                wm_rounded[a, rb][:].rearrange("p (t c j) -> p c j t", t=PACK, j=PACK)[:, cols],
-                wm_raw[a, rb][:].rearrange("p j (c t) -> p c j t", t=PACK)[:, cols],
+                wm_rounded[a, rb][:].rearrange("p (u i c j) -> p u c j i", u=2, i=PAIR, j=PACK)[:, :, cols],
+                wm_raw[a, rb][:].rearrange("p j (c u i) -> p u c j i", u=2, i=PAIR)[:, :, cols],
             )
 
         def quantise_wm(a, rb):
@@ -252,8 +253,8 @@ def tile_list_sharded_embedding_preconditioning_kernel(
             for a in range(PASSES):
                 of_pass = mom_rounded[half][:, PACK * M_HALF * a : PACK * M_HALF * (a + 1)]
                 copy(
-                    of_pass.rearrange("p (c i j) -> p c j i", i=4, j=PACK),
-                    mom_pass(half, a).rearrange("p j (c i) -> p c j i", i=4),
+                    of_pass.rearrange("p (c i j) -> p c j i", i=PAIR, j=PACK),
+                    mom_pass(half, a).rearrange("p j (c i) -> p c j i", i=PAIR),
                 )
 
         def quantise_mom(half):
@@ -300,9 +301,9 @@ def tile_list_sharded_embedding_preconditioning_kernel(
             z[rb, half] = held([P, PACK * M_HALF], BF16, f"z{rb}{half}")
             x_half = x[rb][:, 0 : PACK * (M, X1_STEP)[rb]].rearrange("p (t m) -> p t m", t=PACK)[:, :, M_HALF * half : M_HALF * (half + 1)]
             nc.vector.tensor_tensor(
-                z[rb, half][:].rearrange("p (c i t) -> p c t i", i=4, t=PACK),
-                x_half.rearrange("p t (c i) -> p c t i", i=4),
-                damp[rb, half][:].rearrange("p t (c i) -> p c t i", i=4),
+                z[rb, half][:].rearrange("p (c i t) -> p c t i", i=PAIR, t=PACK),
+                x_half.rearrange("p t (c i) -> p c t i", i=PAIR),
+                damp[rb, half][:].rearrange("p t (c i) -> p c t i", i=PAIR),
                 MULT,
             )
 

@@ -31,7 +31,7 @@ M_HALF = M // 2
 PAIR = 2
 WR_ROW = 8
 OF_V, OF_W = 0, 1
-SPLIT = 64
+SPLIT = 32
 ON_VECTOR = ((1, 0), (1, 2))
 
 FIRST, SECOND = 1, 0
@@ -46,8 +46,10 @@ WR_AT = WM_AT[1, 0]
 RATE_AT = WM_AT[0, 1]
 X1_STEP = 4 * M
 SQUARES = PACK * M_HALF
-WM11_AT = X1_STEP + M_HALF
-LATE_MOM_AT = (3 * X1_STEP + M_HALF - SQUARES, 3 * X1_STEP + M_HALF)
+PAIR_COLS = 2 * K_PASS
+ROOT_ORDER = {(0, 0): (0, 1, 2, 3), (1, 0): (0, 1, 3, 2), (0, 1): (0, 1, 3, 2), (1, 1): (0, 1, 2, 3)}
+WM11_AT = X1_STEP + M
+LATE_MOM_AT = (M, 3 * X1_STEP + M_HALF)
 SQUARES_AT = {
     (1, 0): 2 * X1_STEP + M_HALF,
     (0, 0): 3 * X1_STEP + M_HALF - SQUARES,
@@ -79,7 +81,6 @@ def tile_list_sharded_embedding_preconditioning_kernel(
         tab = {}
         tab_sc = held([P, T], U8, "tab_sc")
         w4_sc = held([P, H], U8, "w4_sc")
-        eps_sb = held([P, PASSES, 2 * PACK], F32, "eps_sb")
         planes = [held([P, 2, H], U8, f"planes{a}") for a in range(PASSES)]
         one = held([P, 1], F32, "one")
 
@@ -113,14 +114,13 @@ def tile_list_sharded_embedding_preconditioning_kernel(
             nc.sync.dma_start(rows[ARRIVE:, :].bitcast(I32), scales.rearrange("a q n -> (a q) n").bitcast(I32))
         load_w4(0)
         nc.sync.dma_start(idx2[:], offs2)
-        nc.sync.dma_start(eps_sb[:, :, 0:PACK], eps.rearrange("(rb p t) -> p rb t", p=P, t=PACK))
         tab[FIRST] = placed([P, T], I32, "tab_first", TAB_AT[FIRST])
         load_table(tab[FIRST][:], FIRST, slice(0, T))
         tab_ahead = held([P, TAB_AHEAD], I32, "tab_ahead")
         load_table(tab_ahead[:], SECOND, slice(0, TAB_AHEAD))
 
-        e = held([P, SLICES], F32, "e")
-        nc.scalar.activation(e[:].rearrange("p (rb t) -> p rb t", t=PACK), eps_sb[:, :, 0:PACK], ACT.Abs_reciprocal_sqrt)
+        warm = held([P, 1], F32, "warm")
+        nc.scalar.activation(warm[:], one[:], ACT.Abs_reciprocal_sqrt)
 
         v_sc = placed([P, S], U8, "v_sc", V_SC_AT)
         nc.vector.tensor_copy(v_sc[:], tab_sc[:].indirect(idx[:]))
@@ -171,14 +171,13 @@ def tile_list_sharded_embedding_preconditioning_kernel(
 
         x = [held([P, PACK * M], F32, "x0"), placed([P, PACK * X1_STEP], F32, "x1", MOM_AT[1])]
 
-        def load_mom(half):
+        def load_mom(half, a):
             if half:
                 mom_raw[half] = x[1]
-            else:
+            elif a == 0:
                 mom_raw[half] = placed([P, PASSES * PACK * M_HALF], F32, f"mom_raw{half}", MOM_AT[half])
-            for a in range(PASSES):
-                rows = mom[K_PASS * a : K_PASS * (a + 1), M_HALF * half : M_HALF * (half + 1)]
-                nc.sync.dma_start(mom_pass(half, a), rows.rearrange("(p j) m -> p j m", j=PACK))
+            rows = mom[K_PASS * a : K_PASS * (a + 1), M_HALF * half : M_HALF * (half + 1)]
+            nc.sync.dma_start(mom_pass(half, a), rows.rearrange("(p j) m -> p j m", j=PACK))
 
         for part in parts:
             gather_words(FIRST, part)
@@ -187,13 +186,15 @@ def tile_list_sharded_embedding_preconditioning_kernel(
         load_w4(1)
         wgt_sb = placed([P, M], F32, "wgt_sb", WGT_AT)
         nc.sync.dma_start(wgt_sb[:], wgt)
-        load_mom(0)
+        load_mom(0, 0)
+        load_mom(0, 1)
         for part in parts:
             gather_words(SECOND, part)
         load_wm(1, 0)
         load_wm(0, 1)
-        load_mom(1)
+        load_mom(1, 0)
         load_wm(1, 1)
+        load_mom(1, 1)
 
         def h_pass(bank, s, part, a):
             rb, t = divmod(s, PACK)
@@ -210,7 +211,7 @@ def tile_list_sharded_embedding_preconditioning_kernel(
         h = [held([P, S], F32, f"h{s}") for s in range(SLICES)]
 
         def h_out(bank, s, part):
-            nc.scalar.activation(h[s][:, BANK * part : BANK * (part + 1)], bank[:], ACT.Copy, scale=e[:, s : s + 1])
+            nc.scalar.copy(h[s][:, BANK * part : BANK * (part + 1)], bank[:])
 
         def pick(s):
             at = (M, X1_STEP)[s // PACK] * (s % PACK)
@@ -233,32 +234,42 @@ def tile_list_sharded_embedding_preconditioning_kernel(
         wm_rounded = {}
         mom_rounded = {}
 
-        def round_wm(a, rb, copy, cols=slice(0, P)):
+        def round_wm(a, rb, copy, cols=slice(0, P), pairs=slice(0, 2)):
+            count = pairs.stop - pairs.start
             if (a, rb) == (1, 1):
-                wm_rounded[a, rb] = held([P, PACK * K_PASS], BF16, "rounded_last")
+                wm_rounded[a, rb, pairs.start] = held([P, count * PAIR_COLS], BF16, f"rounded_last{pairs.start}")[:]
             elif cols.start == 0:
-                wm_rounded[a, rb] = stage.tile([P, PACK * K_PASS], BF16, name="rounded", tag="rounded", align_bytes=64)
+                both = stage.tile([P, PACK * K_PASS], BF16, name="rounded", tag="rounded", align_bytes=64)
+                wm_rounded[a, rb, 0] = both[:]
+                wm_rounded[a, rb, 1] = both[:, PAIR_COLS:]
             copy(
-                wm_rounded[a, rb][:].rearrange("p (u i c j) -> p u c j i", u=2, i=PAIR, j=PACK)[:, :, cols],
-                wm_raw[a, rb][:].rearrange("p j (c u i) -> p u c j i", u=2, i=PAIR)[:, :, cols],
+                wm_rounded[a, rb, pairs.start].rearrange("p (u i c j) -> p u c j i", u=count, i=PAIR, j=PACK)[:, :, cols],
+                wm_raw[a, rb][:].rearrange("p j (c u i) -> p u c j i", u=2, i=PAIR)[:, pairs, cols],
             )
 
-        def quantise_wm(a, rb):
-            wm_q[a, rb] = held([P, K_PASS], U32, f"wm_q{a}{rb}")
-            wm_sc[a, rb] = held([P, K_PASS], U8, f"wm_sc{a}{rb}")
-            nc.vector.quantize_mx(out=wm_q[a, rb][:].bitcast(FP8X4), scales=wm_sc[a, rb][:], in_=wm_rounded[a, rb][:])
+        def quantise_wm(a, rb, pairs=slice(0, 2)):
+            count = pairs.stop - pairs.start
+            name = f"{a}{rb}{pairs.start}"
+            follows = f"rounded_last{pairs.start}" if (a, rb) == (0, 1) else None
+            codes = held([P, count * 2 * P], U32, "wm_q" + name, follows)
+            scales = held([P, count * 2 * P], U8, "wm_sc" + name)
+            rounded = wm_rounded[a, rb, pairs.start][:, 0 : count * PAIR_COLS]
+            nc.vector.quantize_mx(out=codes[:].bitcast(FP8X4), scales=scales[:], in_=rounded)
+            for u in range(2 * count):
+                wm_q[a, rb, 2 * pairs.start + u] = codes[:, P * u : P * (u + 1)]
+                wm_sc[a, rb, 2 * pairs.start + u] = scales[:, P * u : P * (u + 1)]
 
-        def round_mom(half, copy):
-            mom_rounded[half] = stage.tile([P, PACK * K_PASS], BF16, name="rounded", tag="rounded", align_bytes=64)
-            for a in range(PASSES):
-                of_pass = mom_rounded[half][:, PACK * M_HALF * a : PACK * M_HALF * (a + 1)]
-                copy(
-                    of_pass.rearrange("p (c i j) -> p c j i", i=PAIR, j=PACK),
-                    mom_pass(half, a).rearrange("p j (c i) -> p c j i", i=PAIR),
-                )
+        def round_mom(half, a, copy):
+            if a == 0:
+                mom_rounded[half] = stage.tile([P, PACK * K_PASS], BF16, name="rounded", tag="rounded", align_bytes=64)
+            of_pass = mom_rounded[half][:, PACK * M_HALF * a : PACK * M_HALF * (a + 1)]
+            copy(
+                of_pass.rearrange("p (c i j) -> p c j i", i=PAIR, j=PACK),
+                mom_pass(half, a).rearrange("p j (c i) -> p c j i", i=PAIR),
+            )
 
         def quantise_mom(half):
-            mom_q[half] = held([P, PASSES * M_HALF], U32, f"mom_q{half}", "rounded_last" if half else None)
+            mom_q[half] = held([P, PASSES * M_HALF], U32, f"mom_q{half}")
             mom_sc[half] = held([P, PASSES * M_HALF], U8, f"mom_sc{half}")
             nc.vector.quantize_mx(out=mom_q[half][:].bitcast(FP8X4), scales=mom_sc[half][:], in_=mom_rounded[half][:])
 
@@ -268,49 +279,54 @@ def tile_list_sharded_embedding_preconditioning_kernel(
             damp[rb, half] = held([P, PACK, M_HALF], F32, f"damp{rb}{half}")
             if (rb, half) in SQUARES_AT:
                 at = SQUARES_AT[rb, half]
-                square = x[1][:, at : at + SQUARES].rearrange("p (t m) -> p t m", t=PACK)
+                square = x[1][:, at : at + SQUARES]
             else:
-                square = held([P, PACK, M_HALF], F32, f"square{rb}{half}")
+                square = held([P, SQUARES], F32, f"square{rb}{half}")[:]
+            order = ROOT_ORDER[rb, half]
+            rows = {}
             for pair in range(PACK // 2):
                 bank = bank_tile(4 * half + 2 * rb + pair)
-                for u in range(2):
-                    t = 2 * pair + u
-                    for a in range(PASSES):
+                for a in (rb, 1 - rb):
+                    for u in range(2):
+                        t = 2 * pair + u
                         nc.tensor.matmul_mx(
                             out=bank[:, M_HALF * u : M_HALF * (u + 1)],
-                            lhsT=wm_q[a, rb][:, P * t : P * (t + 1)].bitcast(FP8X4),
-                            lhsT_scale=wm_sc[a, rb][:, P * t : P * (t + 1)],
+                            lhsT=wm_q[a, rb, t].bitcast(FP8X4),
+                            lhsT_scale=wm_sc[a, rb, t],
                             rhs=mom_q[half][:, M_HALF * a : M_HALF * (a + 1)].bitcast(FP8X4),
                             rhs_scale=mom_sc[half][:, M_HALF * a : M_HALF * (a + 1)],
-                            start=(a == 0),
-                            stop=(a == PASSES - 1),
+                            start=(a == rb and u == 0),
+                            stop=(a != rb and u == 1),
                         )
+                at = BANK * (pair if order[-1] == PACK - 1 else 1 - pair)
+                nc.scalar.activation(square[:, at : at + BANK], bank[:], ACT.Square)
                 for u in range(2):
-                    t = 2 * pair + u
-                    s = PACK * rb + t
-                    nc.scalar.activation(
-                        square[:, t, :], bank[:, M_HALF * u : M_HALF * (u + 1)], ACT.Square, scale=e[:, s : s + 1]
-                    )
-            nc.scalar.activation(damp[rb, half][:], square[:], ACT.Abs_reciprocal_sqrt, bias=one[:])
+                    rows[2 * pair + u] = square[:, at + M_HALF * u : at + M_HALF * (u + 1)]
+            for t in order:
+                nc.scalar.activation(damp[rb, half][:, t, :], rows[t], ACT.Abs_reciprocal_sqrt, bias=eps_sb[:, rb, t : t + 1])
 
         z = {}
         z_q = {}
         z_sc = {}
 
-        def precondition(rb, half):
-            z[rb, half] = held([P, PACK * M_HALF], BF16, f"z{rb}{half}")
-            x_half = x[rb][:, 0 : PACK * (M, X1_STEP)[rb]].rearrange("p (t m) -> p t m", t=PACK)[:, :, M_HALF * half : M_HALF * (half + 1)]
+        def precondition(rb, half, cols=slice(0, M_HALF)):
+            if cols.start == 0:
+                z[rb, half] = held([P, PACK * M_HALF], BF16, f"z{rb}{half}")
+            x_rows = x[rb][:, 0 : PACK * (M, X1_STEP)[rb]].rearrange("p (t m) -> p t m", t=PACK)
+            x_half = x_rows[:, :, M_HALF * half : M_HALF * (half + 1)]
             nc.vector.tensor_tensor(
-                z[rb, half][:].rearrange("p (c i t) -> p c t i", i=PAIR, t=PACK),
-                x_half.rearrange("p t (c i) -> p c t i", i=PAIR),
-                damp[rb, half][:].rearrange("p t (c i) -> p c t i", i=PAIR),
+                z[rb, half][:, PACK * cols.start : PACK * cols.stop].rearrange("p (c i t) -> p c t i", i=PAIR, t=PACK),
+                x_half[:, :, cols].rearrange("p t (c i) -> p c t i", i=PAIR),
+                damp[rb, half][:, :, cols].rearrange("p t (c i) -> p c t i", i=PAIR),
                 MULT,
             )
 
-        def quantise_z(rb, half):
-            z_q[rb, half] = held([P, M_HALF], U32, f"z_q{rb}{half}")
-            z_sc[rb, half] = held([P, M_HALF], U8, f"z_sc{rb}{half}")
-            nc.vector.quantize_mx(out=z_q[rb, half][:].bitcast(FP8X4), scales=z_sc[rb, half][:], in_=z[rb, half][:])
+        def quantise_z(rb, half, cols=slice(0, M_HALF)):
+            if cols.start == 0:
+                z_q[rb, half] = held([P, M_HALF], U32, f"z_q{rb}{half}")
+                z_sc[rb, half] = held([P, M_HALF], U8, f"z_sc{rb}{half}")
+            rounded = z[rb, half][:, PACK * cols.start : PACK * cols.stop]
+            nc.vector.quantize_mx(out=z_q[rb, half][:, cols].bitcast(FP8X4), scales=z_sc[rb, half][:, cols], in_=rounded)
 
         y_banks = {}
 
@@ -361,9 +377,12 @@ def tile_list_sharded_embedding_preconditioning_kernel(
         round_wm(0, 0, nc.vector.tensor_copy)
         deal_w4(1)
         quantise_wm(0, 0)
-        round_mom(0, nc.vector.tensor_copy)
+        for a in range(PASSES):
+            round_mom(0, a, nc.vector.tensor_copy)
         quantise_mom(0)
         round_wm(1, 0, nc.vector.tensor_copy, slice(0, SPLIT))
+        eps_sb = placed([P, PASSES, 2 * PACK], F32, "eps_sb", MOM_AT[0])
+        nc.sync.dma_start(eps_sb[:, :, 0:PACK], eps.rearrange("(rb p t) -> p rb t", p=P, t=PACK))
         for s in range(PACK):
             for part in parts:
                 h_out(first_banks[s, part], s, part)
@@ -375,6 +394,7 @@ def tile_list_sharded_embedding_preconditioning_kernel(
                     h_pass(bank, s, part, a)
                 h_out(bank, s, part)
         pick(PACK)
+        pick(PACK + 1)
         for r in range(SCALE_ROWS):
             nc.sync.dma_start(
                 planes[SECOND][WR_ROW + r : P : QUAD].bitcast(I32),
@@ -388,16 +408,19 @@ def tile_list_sharded_embedding_preconditioning_kernel(
         rate_sb = placed([P, N // P], F32, "rate_sb", RATE_AT)
         with nc.allow_non_contiguous_dma(reason="one rate a partition"):
             nc.sync.dma_start(rate_sb[:], rate.rearrange("(n_tile p) -> p n_tile", p=P))
-        round_mom(1, nc.scalar.copy)
-        round_wm(1, 1, nc.vector.tensor_copy)
-        quantise_wm(1, 1)
-        quantise_wm(0, 1)
+        round_mom(1, 0, nc.scalar.copy)
+        for pair in range(2):
+            round_wm(1, 1, nc.vector.tensor_copy, pairs=slice(pair, pair + 1))
+        for pair in range(2):
+            quantise_wm(1, 1, slice(pair, pair + 1))
+        for pair in range(2):
+            quantise_wm(0, 1, slice(pair, pair + 1))
+        round_mom(1, 1, nc.vector.tensor_copy)
         quantise_mom(1)
 
         for half in range(2):
             for rb in range(PASSES):
                 damping(rb, half)
-        pick(SLICES - 3)
         pick_half(SLICES - 2, 0)
         precondition(0, 0)
         pick_half(SLICES - 1, 0)
@@ -411,8 +434,11 @@ def tile_list_sharded_embedding_preconditioning_kernel(
         pick_half(SLICES - 1, 1)
         quantise_z(0, 1)
         rotate_pass(1, 0)
-        precondition(1, 1)
-        quantise_z(1, 1)
+        quarters = (slice(0, M_HALF // 2), slice(M_HALF // 2, M_HALF))
+        for cols in quarters:
+            precondition(1, 1, cols)
+        for cols in quarters:
+            quantise_z(1, 1, cols)
         rotate_pass(1, 1)
         for half in range(2):
             store(half)

@@ -31,21 +31,23 @@ M_HALF = M // 2
 PAIR = 2
 WR_ROW = 8
 OF_V, OF_W = 0, 1
-SPLIT = 32
+SPLIT = 56
 ON_VECTOR = ((1, 0), (1, 2))
 
 FIRST, SECOND = 1, 0
 TAB_AT = {FIRST: 0, SECOND: 22}
 TAB_AHEAD = 1024
-WM_AT = {(0, 0): 0, (1, 0): 20, (0, 1): 28}
-W4_LATE_AT = 8
+WM_AT = {(0, 0): 12, (1, 0): 20, (0, 1): 28}
+W4_LATE_AT = 20
 WGT_AT = 10
-V_SC_AT = 30
-MOM_AT = (12, 36)
+V_SC_AT = 21.5
+MOM_AT = (0, 36)
+EPS_AT = WM_AT[0, 0]
 WR_AT = WM_AT[1, 0]
 RATE_AT = WM_AT[0, 1]
 X1_STEP = 4 * M
 SQUARES = PACK * M_HALF
+MOM_PIECES = ((0, slice(0, M)), (1, slice(0, M_HALF)), (1, slice(M_HALF, M)))
 PAIR_COLS = 2 * K_PASS
 ROOT_ORDER = {(0, 0): (0, 1, 2, 3), (1, 0): (0, 1, 3, 2), (0, 1): (0, 1, 3, 2), (1, 1): (0, 1, 2, 3)}
 WM11_AT = X1_STEP + M
@@ -71,7 +73,7 @@ def tile_list_sharded_embedding_preconditioning_kernel(
             return keep.tile(shape, dtype, name=name, tag=tag or name, align_bytes=64)
 
         def placed(shape, dtype, name, kib):
-            return shared.tile(shape, dtype, name=name, align_bytes=64, offset=1024 * kib)
+            return shared.tile(shape, dtype, name=name, align_bytes=64, offset=int(1024 * kib))
 
         def bank_tile(number):
             return psum.tile([P, BANK], F32, name=f"bank{number}", tag=f"bank{number}")
@@ -102,9 +104,9 @@ def tile_list_sharded_embedding_preconditioning_kernel(
             words = w4_words.rearrange("a p n -> p a n")[:, :, 2 * K_PASS * rb : 2 * K_PASS * (rb + 1)]
             nc.sync.dma_start(w4[rb][:].bitcast(I32), words.bitcast(I32))
 
-        def deal_w4(rb):
+        def deal_w4(rb, copy):
             w4p[rb] = held([P, PASSES, 2 * K_PASS], U8, f"w4p{rb}")
-            nc.vector.tensor_copy(
+            copy(
                 w4p[rb][:].bitcast(U16).rearrange("p a (t c) -> p a t c", t=PACK),
                 w4[rb][:].bitcast(U16).rearrange("p a (c t) -> p a t c", t=PACK),
             )
@@ -142,8 +144,10 @@ def tile_list_sharded_embedding_preconditioning_kernel(
         move_rows(FIRST)
         tab[SECOND] = placed([P, T], I32, "tab_second", TAB_AT[SECOND])
         load_table(tab[SECOND][:, TAB_AHEAD:], SECOND, slice(TAB_AHEAD, T))
+        load_w4(1)
         move_rows(SECOND)
-        deal_w4(0)
+        deal_w4(0, nc.scalar.copy)
+        deal_w4(1, nc.scalar.copy)
 
         v = {}
 
@@ -165,36 +169,33 @@ def tile_list_sharded_embedding_preconditioning_kernel(
             rows = wm[K_PASS * a : K_PASS * (a + 1), K_PASS * rb : K_PASS * (rb + 1)]
             nc.sync.dma_start(wm_raw[a, rb][:], rows.rearrange("(p j) r -> p j r", j=PACK))
 
-        def mom_pass(half, a):
-            at = LATE_MOM_AT[a] if half else PACK * M_HALF * a
-            return mom_raw[half][:, at : at + PACK * M_HALF].rearrange("p (j m) -> p j m", j=PACK)
 
         x = [held([P, PACK * M], F32, "x0"), placed([P, PACK * X1_STEP], F32, "x1", MOM_AT[1])]
 
-        def load_mom(half, a):
-            if half:
-                mom_raw[half] = x[1]
-            elif a == 0:
-                mom_raw[half] = placed([P, PASSES * PACK * M_HALF], F32, f"mom_raw{half}", MOM_AT[half])
-            rows = mom[K_PASS * a : K_PASS * (a + 1), M_HALF * half : M_HALF * (half + 1)]
-            nc.sync.dma_start(mom_pass(half, a), rows.rearrange("(p j) m -> p j m", j=PACK))
+        def load_mom(piece):
+            a, cols = MOM_PIECES[piece]
+            if piece:
+                at = LATE_MOM_AT[piece - 1]
+                mom_raw[piece] = x[1][:, at : at + PACK * M_HALF].rearrange("p (j m) -> p j m", j=PACK)
+            else:
+                mom_raw[piece] = placed([P, PACK, M], F32, "mom_raw0", MOM_AT[0])[:]
+            rows = mom[K_PASS * a : K_PASS * (a + 1), cols]
+            nc.sync.dma_start(mom_raw[piece], rows.rearrange("(p j) m -> p j m", j=PACK))
 
         for part in parts:
             gather_words(FIRST, part)
         nc.vector.tensor_copy(tab[SECOND][:, 0:TAB_AHEAD], tab_ahead[:])
-        load_wm(0, 0)
-        load_w4(1)
+        load_mom(0)
         wgt_sb = placed([P, M], F32, "wgt_sb", WGT_AT)
         nc.sync.dma_start(wgt_sb[:], wgt)
-        load_mom(0, 0)
-        load_mom(0, 1)
+        load_wm(0, 0)
         for part in parts:
             gather_words(SECOND, part)
         load_wm(1, 0)
+        load_mom(1)
         load_wm(0, 1)
-        load_mom(1, 0)
         load_wm(1, 1)
-        load_mom(1, 1)
+        load_mom(2)
 
         def h_pass(bank, s, part, a):
             rb, t = divmod(s, PACK)
@@ -259,21 +260,28 @@ def tile_list_sharded_embedding_preconditioning_kernel(
                 wm_q[a, rb, 2 * pairs.start + u] = codes[:, P * u : P * (u + 1)]
                 wm_sc[a, rb, 2 * pairs.start + u] = scales[:, P * u : P * (u + 1)]
 
-        def round_mom(half, a, copy):
-            if a == 0:
-                mom_rounded[half] = stage.tile([P, PACK * K_PASS], BF16, name="rounded", tag="rounded", align_bytes=64)
-            of_pass = mom_rounded[half][:, PACK * M_HALF * a : PACK * M_HALF * (a + 1)]
+        def round_mom(piece, copy):
+            if piece:
+                mom_rounded[piece] = held([P, PACK * M_HALF], BF16, f"mom_rounded{piece}")
+            else:
+                mom_rounded[piece] = stage.tile([P, PACK * K_PASS], BF16, name="rounded", tag="rounded", align_bytes=64)
             copy(
-                of_pass.rearrange("p (c i j) -> p c j i", i=PAIR, j=PACK),
-                mom_pass(half, a).rearrange("p j (c i) -> p c j i", i=PAIR),
+                mom_rounded[piece][:].rearrange("p (c i j) -> p c j i", i=PAIR, j=PACK),
+                mom_raw[piece].rearrange("p j (c i) -> p c j i", i=PAIR),
             )
 
-        def quantise_mom(half):
-            mom_q[half] = held([P, PASSES * M_HALF], U32, f"mom_q{half}")
-            mom_sc[half] = held([P, PASSES * M_HALF], U8, f"mom_sc{half}")
-            nc.vector.quantize_mx(out=mom_q[half][:].bitcast(FP8X4), scales=mom_sc[half][:], in_=mom_rounded[half][:])
+        def quantise_mom(piece):
+            a, cols = MOM_PIECES[piece]
+            width = cols.stop - cols.start
+            codes = held([P, width], U32, f"mom_q{piece}")
+            scales = held([P, width], U8, f"mom_sc{piece}")
+            nc.vector.quantize_mx(out=codes[:].bitcast(FP8X4), scales=scales[:], in_=mom_rounded[piece][:])
+            for at in range(0, width, M_HALF):
+                mom_q[(cols.start + at) // M_HALF, a] = codes[:, at : at + M_HALF]
+                mom_sc[(cols.start + at) // M_HALF, a] = scales[:, at : at + M_HALF]
 
         damp = {}
+        y_sb = [held([P, N // P, M_HALF], F32, f"y{half}") for half in range(2)]
 
         def damping(rb, half):
             damp[rb, half] = held([P, PACK, M_HALF], F32, f"damp{rb}{half}")
@@ -281,22 +289,23 @@ def tile_list_sharded_embedding_preconditioning_kernel(
                 at = SQUARES_AT[rb, half]
                 square = x[1][:, at : at + SQUARES]
             else:
-                square = held([P, SQUARES], F32, f"square{rb}{half}")[:]
+                square = y_sb[0][:].rearrange("p n m -> p (n m)")[:, 0:SQUARES]
             order = ROOT_ORDER[rb, half]
             rows = {}
             for pair in range(PACK // 2):
                 bank = bank_tile(4 * half + 2 * rb + pair)
-                for a in (rb, 1 - rb):
+                first = 1 if (rb, half) == (1, 0) else 0
+                for a in (first, 1 - first):
                     for u in range(2):
                         t = 2 * pair + u
                         nc.tensor.matmul_mx(
                             out=bank[:, M_HALF * u : M_HALF * (u + 1)],
                             lhsT=wm_q[a, rb, t].bitcast(FP8X4),
                             lhsT_scale=wm_sc[a, rb, t],
-                            rhs=mom_q[half][:, M_HALF * a : M_HALF * (a + 1)].bitcast(FP8X4),
-                            rhs_scale=mom_sc[half][:, M_HALF * a : M_HALF * (a + 1)],
-                            start=(a == rb and u == 0),
-                            stop=(a != rb and u == 1),
+                            rhs=mom_q[half, a].bitcast(FP8X4),
+                            rhs_scale=mom_sc[half, a],
+                            start=(a == first and u == 0),
+                            stop=(a != first and u == 1),
                         )
                 at = BANK * (pair if order[-1] == PACK - 1 else 1 - pair)
                 nc.scalar.activation(square[:, at : at + BANK], bank[:], ACT.Square)
@@ -313,11 +322,12 @@ def tile_list_sharded_embedding_preconditioning_kernel(
             if cols.start == 0:
                 z[rb, half] = held([P, PACK * M_HALF], BF16, f"z{rb}{half}")
             x_rows = x[rb][:, 0 : PACK * (M, X1_STEP)[rb]].rearrange("p (t m) -> p t m", t=PACK)
+            run = 4 if (rb, half) == (1, 0) else PAIR
             x_half = x_rows[:, :, M_HALF * half : M_HALF * (half + 1)]
             nc.vector.tensor_tensor(
-                z[rb, half][:, PACK * cols.start : PACK * cols.stop].rearrange("p (c i t) -> p c t i", i=PAIR, t=PACK),
-                x_half[:, :, cols].rearrange("p t (c i) -> p c t i", i=PAIR),
-                damp[rb, half][:, :, cols].rearrange("p t (c i) -> p c t i", i=PAIR),
+                z[rb, half][:, PACK * cols.start : PACK * cols.stop].rearrange("p (c i t) -> p c t i", i=run, t=PACK),
+                x_half[:, :, cols].rearrange("p t (c i) -> p c t i", i=run),
+                damp[rb, half][:, :, cols].rearrange("p t (c i) -> p c t i", i=run),
                 MULT,
             )
 
@@ -347,7 +357,7 @@ def tile_list_sharded_embedding_preconditioning_kernel(
                     )
 
         def store(half):
-            y_half = held([P, N // P, M_HALF], F32, f"y{half}", None if half else "square11")
+            y_half = y_sb[half]
             for pair in range(N // P // 2):
                 n_tiles = slice(2 * pair, 2 * pair + 2)
                 y = y_half[:, n_tiles, :]
@@ -370,18 +380,17 @@ def tile_list_sharded_embedding_preconditioning_kernel(
             for s in range(PACK):
                 first_banks[s, part] = bank_tile(2 * s + part)
                 h_pass(first_banks[s, part], s, part, FIRST)
-        for part in parts:
-            for s in range(PACK):
-                h_pass(first_banks[s, part], s, part, SECOND)
+        for s0 in range(0, PACK, 2):
+            for part in parts:
+                for s in (s0, s0 + 1):
+                    h_pass(first_banks[s, part], s, part, SECOND)
 
-        round_wm(0, 0, nc.vector.tensor_copy)
-        deal_w4(1)
-        quantise_wm(0, 0)
-        for a in range(PASSES):
-            round_mom(0, a, nc.vector.tensor_copy)
+        round_mom(0, nc.vector.tensor_copy)
         quantise_mom(0)
+        round_wm(0, 0, nc.vector.tensor_copy)
+        quantise_wm(0, 0)
         round_wm(1, 0, nc.vector.tensor_copy, slice(0, SPLIT))
-        eps_sb = placed([P, PASSES, 2 * PACK], F32, "eps_sb", MOM_AT[0])
+        eps_sb = placed([P, PASSES, 2 * PACK], F32, "eps_sb", EPS_AT)
         nc.sync.dma_start(eps_sb[:, :, 0:PACK], eps.rearrange("(rb p t) -> p rb t", p=P, t=PACK))
         for s in range(PACK):
             for part in parts:
@@ -401,22 +410,23 @@ def tile_list_sharded_embedding_preconditioning_kernel(
                 wr_scales[:, r :: SCALE_ROWS, :].rearrange("a q n -> q a n").bitcast(I32),
             )
         round_wm(1, 0, nc.scalar.copy, slice(SPLIT, P))
+        round_mom(1, nc.scalar.copy)
         wr = placed([P, PASSES, N], I32, "wr", WR_AT)
         nc.sync.dma_start(wr[:], wr_words.rearrange("a p n j -> p a (n j)").bitcast(I32))
         quantise_wm(1, 0)
+        quantise_mom(1)
         round_wm(0, 1, nc.scalar.copy)
         rate_sb = placed([P, N // P], F32, "rate_sb", RATE_AT)
         with nc.allow_non_contiguous_dma(reason="one rate a partition"):
             nc.sync.dma_start(rate_sb[:], rate.rearrange("(n_tile p) -> p n_tile", p=P))
-        round_mom(1, 0, nc.scalar.copy)
         for pair in range(2):
             round_wm(1, 1, nc.vector.tensor_copy, pairs=slice(pair, pair + 1))
         for pair in range(2):
             quantise_wm(1, 1, slice(pair, pair + 1))
         for pair in range(2):
             quantise_wm(0, 1, slice(pair, pair + 1))
-        round_mom(1, 1, nc.vector.tensor_copy)
-        quantise_mom(1)
+        round_mom(2, nc.vector.tensor_copy)
+        quantise_mom(2)
 
         for half in range(2):
             for rb in range(PASSES):

@@ -31,16 +31,17 @@ M_HALF = M // 2
 PAIR = 2
 WR_ROW = 8
 OF_V, OF_W = 0, 1
-SPLIT = 56
+SPLIT = 48
 ON_VECTOR = ((1, 0), (1, 2))
 
 FIRST, SECOND = 1, 0
-TAB_AT = {FIRST: 0, SECOND: 22}
-TAB_AHEAD = 1024
+TAB_AT = {FIRST: 0, SECOND: 23}
+TAB_AHEAD = 1280
 WM_AT = {(0, 0): 12, (1, 0): 20, (0, 1): 28}
+W4_SECOND_AT = 22
 W4_LATE_AT = 20
 WGT_AT = 10
-V_SC_AT = 21.5
+V_SC_AT = 21.875
 MOM_AT = (0, 36)
 EPS_AT = WM_AT[0, 0]
 WR_AT = WM_AT[1, 0]
@@ -98,23 +99,27 @@ def tile_list_sharded_embedding_preconditioning_kernel(
         w4 = {}
         w4p = {}
 
-        def load_w4(rb):
-            shape = [P, PASSES, 2 * K_PASS]
-            w4[rb] = placed(shape, U8, "w4_late", W4_LATE_AT) if rb else held(shape, U8, "w4_early")
-            words = w4_words.rearrange("a p n -> p a n")[:, :, 2 * K_PASS * rb : 2 * K_PASS * (rb + 1)]
-            nc.sync.dma_start(w4[rb][:].bitcast(I32), words.bitcast(I32))
+        def load_w4(rb, passes, kib):
+            shape = [P, passes.stop - passes.start, 2 * K_PASS]
+            name = f"w4_{rb}{passes.start}"
+            w4[rb, passes.start] = held(shape, U8, name) if kib is None else placed(shape, U8, name, kib)
+            words = w4_words.rearrange("a p n -> p a n")[:, passes, 2 * K_PASS * rb : 2 * K_PASS * (rb + 1)]
+            nc.sync.dma_start(w4[rb, passes.start][:].bitcast(I32), words.bitcast(I32))
 
-        def deal_w4(rb, copy):
-            w4p[rb] = held([P, PASSES, 2 * K_PASS], U8, f"w4p{rb}")
-            copy(
-                w4p[rb][:].bitcast(U16).rearrange("p a (t c) -> p a t c", t=PACK),
-                w4[rb][:].bitcast(U16).rearrange("p a (c t) -> p a t c", t=PACK),
+        def deal_w4(rb, passes):
+            count = passes.stop - passes.start
+            dealt = held([P, count, 2 * K_PASS], U8, f"w4p{rb}{passes.start}")
+            nc.scalar.copy(
+                dealt[:].bitcast(U16).rearrange("p a (t c) -> p a t c", t=PACK),
+                w4[rb, passes.start][:].bitcast(U16).rearrange("p a (c t) -> p a t c", t=PACK),
             )
+            for a in range(count):
+                w4p[rb, passes.start + a] = dealt[:, a, :]
 
         nc.sync.dma_start(idx[:], offs)
         for rows, scales in ((tab_sc, tab_scales), (w4_sc, w4_scales)):
             nc.sync.dma_start(rows[ARRIVE:, :].bitcast(I32), scales.rearrange("a q n -> (a q) n").bitcast(I32))
-        load_w4(0)
+        load_w4(0, slice(FIRST, FIRST + 1), None)
         nc.sync.dma_start(idx2[:], offs2)
         tab[FIRST] = placed([P, T], I32, "tab_first", TAB_AT[FIRST])
         load_table(tab[FIRST][:], FIRST, slice(0, T))
@@ -124,7 +129,7 @@ def tile_list_sharded_embedding_preconditioning_kernel(
         warm = held([P, 1], F32, "warm")
         nc.scalar.activation(warm[:], one[:], ACT.Abs_reciprocal_sqrt)
 
-        v_sc = placed([P, S], U8, "v_sc", V_SC_AT)
+        v_sc = placed([P, S + 256], U8, "v_sc", V_SC_AT)[:, 0:S]
         nc.vector.tensor_copy(v_sc[:], tab_sc[:].indirect(idx[:]))
         staged = held([P, 2, H], U8, "staged")
         nc.vector.tensor_copy(
@@ -144,10 +149,12 @@ def tile_list_sharded_embedding_preconditioning_kernel(
         move_rows(FIRST)
         tab[SECOND] = placed([P, T], I32, "tab_second", TAB_AT[SECOND])
         load_table(tab[SECOND][:, TAB_AHEAD:], SECOND, slice(TAB_AHEAD, T))
-        load_w4(1)
+        load_w4(0, slice(SECOND, SECOND + 1), W4_SECOND_AT)
+        load_w4(1, slice(0, PASSES), W4_LATE_AT)
         move_rows(SECOND)
-        deal_w4(0, nc.scalar.copy)
-        deal_w4(1, nc.scalar.copy)
+        deal_w4(0, slice(FIRST, FIRST + 1))
+        deal_w4(0, slice(SECOND, SECOND + 1))
+        deal_w4(1, slice(0, PASSES))
 
         v = {}
 
@@ -201,7 +208,7 @@ def tile_list_sharded_embedding_preconditioning_kernel(
             rb, t = divmod(s, PACK)
             nc.tensor.matmul_mx(
                 out=bank[:],
-                lhsT=w4p[rb][:, a, 2 * P * t : 2 * P * (t + 1)].bitcast(FP4X4),
+                lhsT=w4p[rb, a][:, 2 * P * t : 2 * P * (t + 1)].bitcast(FP4X4),
                 lhsT_scale=planes[a][:, OF_W, P * s : P * (s + 1)],
                 rhs=v[a, part][:].bitcast(FP8X4),
                 rhs_scale=planes[a][:, OF_V, BANK * part : BANK * (part + 1)],

from contextlib import ExitStack

import concourse.mybir as mybir

K, H, N, T, S, M = 1024, 1024, 1024, 4096, 1024, 512
FLOPS = 2 * K * H * S + 2 * K * H * M + 2 * H * N * M

F32 = mybir.dt.float32
BF16 = mybir.dt.bfloat16
I32 = mybir.dt.int32
U32 = mybir.dt.uint32
U16 = mybir.dt.uint16
U8 = mybir.dt.uint8
FP8X4 = mybir.dt.float8_e4m3fn_x4
FP4X4 = mybir.dt.float4_e2m1fn_x4
ACT = mybir.ActivationFunctionType
MULT = mybir.AluOpType.mult

P = 128
PACK = 4
K_PASS = P * PACK
PASSES = 2
QUADS = 4
QUAD = P // QUADS
SCALE_ROWS = 4
ARRIVE = P - QUAD
GROUP = 16
BANK = 512
SLICES = H // P
M_HALF = M // 2
PAIR = 2
WR_ROW = 8
OF_V, OF_W = 0, 1
SPLIT = 48
ON_VECTOR = ((1, 0), (1, 2))

FIRST, SECOND = 1, 0
TAB_AT = {FIRST: 0, SECOND: 23}
TAB_AHEAD = 1280
WM_AT = {(0, 0): 12, (1, 0): 20, (0, 1): 28}
W4_SECOND_AT = 22
W4_LATE_AT = 20
WGT_AT = 10
V_SC_AT = 21.875
MOM_AT = (0, 36)
EPS_AT = WM_AT[0, 0]
WR_AT = WM_AT[1, 0]
RATE_AT = WM_AT[0, 1]
X1_STEP = 4 * M
SQUARES = PACK * M_HALF
MOM_PIECES = ((0, slice(0, M)), (1, slice(0, M_HALF)), (1, slice(M_HALF, M)))
PAIR_COLS = 2 * K_PASS
ROOT_ORDER = {(0, 0): (0, 1, 2, 3), (1, 0): (0, 1, 3, 2), (0, 1): (0, 1, 3, 2), (1, 1): (0, 1, 2, 3)}
WM11_AT = X1_STEP + M
LATE_MOM_AT = (M, 3 * X1_STEP + M_HALF)
SQUARES_AT = {
    (1, 0): 2 * X1_STEP + M_HALF,
    (0, 0): 3 * X1_STEP + M_HALF - SQUARES,
    (0, 1): 3 * X1_STEP + M_HALF,
}


def tile_list_sharded_embedding_preconditioning_kernel(
    tc, tab_words, tab_scales, offs, w4_words, w4_scales, offs2, wgt, mom, wm, eps, wr_words, wr_scales, rate, out
):
    nc = tc.nc
    with ExitStack() as ctx:
        keep = ctx.enter_context(tc.tile_pool(name="keep", bufs=1))
        stage = ctx.enter_context(tc.tile_pool(name="stage", bufs=3))
        shared = ctx.enter_context(tc.tile_pool(name="shared", bufs=1))
        psum = ctx.enter_context(tc.psum_pool(name="psum", bufs=1))

        def held(shape, dtype, name, tag=None):
            return keep.tile(shape, dtype, name=name, tag=tag or name, align_bytes=64)

        def placed(shape, dtype, name, kib):
            return shared.tile(shape, dtype, name=name, align_bytes=64, offset=int(1024 * kib))

        def bank_tile(number):
            return psum.tile([P, BANK], F32, name=f"bank{number}", tag=f"bank{number}")

        idx = keep.tile([P, S // GROUP], U16, name="idx")
        idx2 = keep.tile([P, M // GROUP], U16, name="idx2")
        tab = {}
        tab_sc = held([P, T], U8, "tab_sc")
        w4_sc = held([P, H], U8, "w4_sc")
        planes = [held([P, 2, H], U8, f"planes{a}") for a in range(PASSES)]
        one = held([P, 1], F32, "one")

        nc.vector.memset(w4_sc[0:ARRIVE].bitcast(I32), 0)
        nc.vector.memset(tab_sc[0:ARRIVE].bitcast(I32), 0)
        for a in (FIRST, SECOND):
            nc.vector.memset(planes[a][:].rearrange("p w n -> p (w n)").bitcast(I32), 0)
        nc.vector.memset(one[:], 1.0)

        def load_table(into, a, cols):
            nc.sync.dma_start(into, tab_words[a].rearrange("p n j -> p (n j)").bitcast(I32)[:, cols])

        w4 = {}
        w4p = {}

        def load_w4(rb, passes, kib):
            shape = [P, passes.stop - passes.start, 2 * K_PASS]
            name = f"w4_{rb}{passes.start}"
            w4[rb, passes.start] = held(shape, U8, name) if kib is None else placed(shape, U8, name, kib)
            words = w4_words.rearrange("a p n -> p a n")[:, passes, 2 * K_PASS * rb : 2 * K_PASS * (rb + 1)]
            nc.sync.dma_start(w4[rb, passes.start][:].bitcast(I32), words.bitcast(I32))

        def deal_w4(rb, passes):
            count = passes.stop - passes.start
            dealt = held([P, count, 2 * K_PASS], U8, f"w4p{rb}{passes.start}")
            nc.scalar.copy(
                dealt[:].bitcast(U16).rearrange("p a (t c) -> p a t c", t=PACK),
                w4[rb, passes.start][:].bitcast(U16).rearrange("p a (c t) -> p a t c", t=PACK),
            )
            for a in range(count):
                w4p[rb, passes.start + a] = dealt[:, a, :]

        nc.sync.dma_start(idx[:], offs)
        for rows, scales in ((tab_sc, tab_scales), (w4_sc, w4_scales)):
            nc.sync.dma_start(rows[ARRIVE:, :].bitcast(I32), scales.rearrange("a q n -> (a q) n").bitcast(I32))
        load_w4(0, slice(FIRST, FIRST + 1), None)
        nc.sync.dma_start(idx2[:], offs2)
        tab[FIRST] = placed([P, T], I32, "tab_first", TAB_AT[FIRST])
        load_table(tab[FIRST][:], FIRST, slice(0, T))
        tab_ahead = held([P, TAB_AHEAD], I32, "tab_ahead")
        load_table(tab_ahead[:], SECOND, slice(0, TAB_AHEAD))

        warm = held([P, 1], F32, "warm")
        nc.scalar.activation(warm[:], one[:], ACT.Abs_reciprocal_sqrt)

        v_sc = placed([P, S + 256], U8, "v_sc", V_SC_AT)[:, 0:S]
        nc.vector.tensor_copy(v_sc[:], tab_sc[:].indirect(idx[:]))
        staged = held([P, 2, H], U8, "staged")
        nc.vector.tensor_copy(
            staged[:, OF_W, :].rearrange("p (rb t c) -> p rb t c", rb=PASSES, t=PACK),
            w4_sc[:].rearrange("p (rb c t) -> p rb t c", rb=PASSES, t=PACK),
        )
        nc.vector.tensor_copy(staged[:, OF_V, :].bitcast(I32), v_sc[:].bitcast(I32))

        def move_rows(a):
            first = ARRIVE + SCALE_ROWS * QUADS * a
            for r in range(SCALE_ROWS):
                nc.sync.dma_start(
                    planes[a][r:P:QUAD].rearrange("p w n -> p (w n)").bitcast(I32),
                    staged[first + r : first + SCALE_ROWS * QUADS : SCALE_ROWS].rearrange("p w n -> p (w n)").bitcast(I32),
                )

        move_rows(FIRST)
        tab[SECOND] = placed([P, T], I32, "tab_second", TAB_AT[SECOND])
        load_table(tab[SECOND][:, TAB_AHEAD:], SECOND, slice(TAB_AHEAD, T))
        load_w4(0, slice(SECOND, SECOND + 1), W4_SECOND_AT)
        load_w4(1, slice(0, PASSES), W4_LATE_AT)
        move_rows(SECOND)
        deal_w4(0, slice(FIRST, FIRST + 1))
        deal_w4(0, slice(SECOND, SECOND + 1))
        deal_w4(1, slice(0, PASSES))

        v = {}

        def gather_words(a, part):
            v[a, part] = held([P, BANK], U32, f"v{a}{part}")
            cols = BANK // GROUP
            entries = idx[:, cols * part : cols * (part + 1)]
            nc.vector.tensor_copy(v[a, part][:], tab[a][:].bitcast(U32).indirect(entries))

        parts = range(S // BANK)
        wm_raw = {}
        mom_raw = {}

        def load_wm(a, rb):
            if (a, rb) == (1, 1):
                wm_raw[a, rb] = x[1][:, WM11_AT : WM11_AT + PACK * K_PASS].rearrange("p (j r) -> p j r", j=PACK)
            else:
                wm_raw[a, rb] = placed([P, PACK, K_PASS], F32, f"wm_raw{a}{rb}", WM_AT[a, rb])
            rows = wm[K_PASS * a : K_PASS * (a + 1), K_PASS * rb : K_PASS * (rb + 1)]
            nc.sync.dma_start(wm_raw[a, rb][:], rows.rearrange("(p j) r -> p j r", j=PACK))


        x = [held([P, PACK * M], F32, "x0"), placed([P, PACK * X1_STEP], F32, "x1", MOM_AT[1])]

        def load_mom(piece):
            a, cols = MOM_PIECES[piece]
            if piece:
                at = LATE_MOM_AT[piece - 1]
                mom_raw[piece] = x[1][:, at : at + PACK * M_HALF].rearrange("p (j m) -> p j m", j=PACK)
            else:
                mom_raw[piece] = placed([P, PACK, M], F32, "mom_raw0", MOM_AT[0])[:]
            rows = mom[K_PASS * a : K_PASS * (a + 1), cols]
            nc.sync.dma_start(mom_raw[piece], rows.rearrange("(p j) m -> p j m", j=PACK))

        for part in parts:
            gather_words(FIRST, part)
        nc.vector.tensor_copy(tab[SECOND][:, 0:TAB_AHEAD], tab_ahead[:])
        load_mom(0)
        wgt_sb = placed([P, M], F32, "wgt_sb", WGT_AT)
        nc.sync.dma_start(wgt_sb[:], wgt)
        load_wm(0, 0)
        for part in parts:
            gather_words(SECOND, part)
        load_wm(1, 0)
        load_mom(1)
        load_wm(0, 1)
        load_wm(1, 1)
        load_mom(2)

        def h_pass(bank, s, part, a):
            rb, t = divmod(s, PACK)
            nc.tensor.matmul_mx(
                out=bank[:],
                lhsT=w4p[rb, a][:, 2 * P * t : 2 * P * (t + 1)].bitcast(FP4X4),
                lhsT_scale=planes[a][:, OF_W, P * s : P * (s + 1)],
                rhs=v[a, part][:].bitcast(FP8X4),
                rhs_scale=planes[a][:, OF_V, BANK * part : BANK * (part + 1)],
                start=(a == FIRST),
                stop=(a == SECOND),
            )

        h = [held([P, S], F32, f"h{s}") for s in range(SLICES)]

        def h_out(bank, s, part):
            nc.scalar.copy(h[s][:, BANK * part : BANK * (part + 1)], bank[:])

        def pick(s):
            at = (M, X1_STEP)[s // PACK] * (s % PACK)
            nc.vector.tensor_tensor(x[s // PACK][:, at : at + M], h[s][:].indirect(idx2[:]), wgt_sb[:], MULT)

        def pick_half(s, half):
            at = X1_STEP * (s - PACK) + M_HALF * half
            cols = M_HALF // GROUP
            nc.vector.tensor_tensor(
                x[1][:, at : at + M_HALF],
                h[s][:].indirect(idx2[:, cols * half : cols * (half + 1)]),
                wgt_sb[:, M_HALF * half : M_HALF * (half + 1)],
                MULT,
            )

        wm_q = {}
        wm_sc = {}
        mom_q = {}
        mom_sc = {}
        wm_rounded = {}
        mom_rounded = {}

        def round_wm(a, rb, copy, cols=slice(0, P), pairs=slice(0, 2)):
            count = pairs.stop - pairs.start
            if (a, rb) == (1, 1):
                wm_rounded[a, rb, pairs.start] = held([P, count * PAIR_COLS], BF16, f"rounded_last{pairs.start}")[:]
            elif cols.start == 0:
                both = stage.tile([P, PACK * K_PASS], BF16, name="rounded", tag="rounded", align_bytes=64)
                wm_rounded[a, rb, 0] = both[:]
                wm_rounded[a, rb, 1] = both[:, PAIR_COLS:]
            copy(
                wm_rounded[a, rb, pairs.start].rearrange("p (u i c j) -> p u c j i", u=count, i=PAIR, j=PACK)[:, :, cols],
                wm_raw[a, rb][:].rearrange("p j (c u i) -> p u c j i", u=2, i=PAIR)[:, pairs, cols],
            )

        def quantise_wm(a, rb, pairs=slice(0, 2)):
            count = pairs.stop - pairs.start
            name = f"{a}{rb}{pairs.start}"
            follows = f"rounded_last{pairs.start}" if (a, rb) == (0, 1) else None
            codes = held([P, count * 2 * P], U32, "wm_q" + name, follows)
            scales = held([P, count * 2 * P], U8, "wm_sc" + name)
            rounded = wm_rounded[a, rb, pairs.start][:, 0 : count * PAIR_COLS]
            nc.vector.quantize_mx(out=codes[:].bitcast(FP8X4), scales=scales[:], in_=rounded)
            for u in range(2 * count):
                wm_q[a, rb, 2 * pairs.start + u] = codes[:, P * u : P * (u + 1)]
                wm_sc[a, rb, 2 * pairs.start + u] = scales[:, P * u : P * (u + 1)]

        def round_mom(piece, copy):
            if piece:
                mom_rounded[piece] = held([P, PACK * M_HALF], BF16, f"mom_rounded{piece}")
            else:
                mom_rounded[piece] = stage.tile([P, PACK * K_PASS], BF16, name="rounded", tag="rounded", align_bytes=64)
            copy(
                mom_rounded[piece][:].rearrange("p (c i j) -> p c j i", i=PAIR, j=PACK),
                mom_raw[piece].rearrange("p j (c i) -> p c j i", i=PAIR),
            )

        def quantise_mom(piece):
            a, cols = MOM_PIECES[piece]
            width = cols.stop - cols.start
            codes = held([P, width], U32, f"mom_q{piece}")
            scales = held([P, width], U8, f"mom_sc{piece}")
            nc.vector.quantize_mx(out=codes[:].bitcast(FP8X4), scales=scales[:], in_=mom_rounded[piece][:])
            for at in range(0, width, M_HALF):
                mom_q[(cols.start + at) // M_HALF, a] = codes[:, at : at + M_HALF]
                mom_sc[(cols.start + at) // M_HALF, a] = scales[:, at : at + M_HALF]

        damp = {}
        y_sb = [held([P, N // P, M_HALF], F32, f"y{half}") for half in range(2)]

        def damping(rb, half):
            damp[rb, half] = held([P, PACK, M_HALF], F32, f"damp{rb}{half}")
            if (rb, half) in SQUARES_AT:
                at = SQUARES_AT[rb, half]
                square = x[1][:, at : at + SQUARES]
            else:
                square = y_sb[0][:].rearrange("p n m -> p (n m)")[:, 0:SQUARES]
            order = ROOT_ORDER[rb, half]
            rows = {}
            for pair in range(PACK // 2):
                bank = bank_tile(4 * half + 2 * rb + pair)
                first = 1 if (rb, half) == (1, 0) else 0
                for a in (first, 1 - first):
                    for u in range(2):
                        t = 2 * pair + u
                        nc.tensor.matmul_mx(
                            out=bank[:, M_HALF * u : M_HALF * (u + 1)],
                            lhsT=wm_q[a, rb, t].bitcast(FP8X4),
                            lhsT_scale=wm_sc[a, rb, t],
                            rhs=mom_q[half, a].bitcast(FP8X4),
                            rhs_scale=mom_sc[half, a],
                            start=(a == first and u == 0),
                            stop=(a != first and u == 1),
                        )
                at = BANK * (pair if order[-1] == PACK - 1 else 1 - pair)
                nc.scalar.activation(square[:, at : at + BANK], bank[:], ACT.Square)
                for u in range(2):
                    rows[2 * pair + u] = square[:, at + M_HALF * u : at + M_HALF * (u + 1)]
            for t in order:
                nc.scalar.activation(damp[rb, half][:, t, :], rows[t], ACT.Abs_reciprocal_sqrt, bias=eps_sb[:, rb, t : t + 1])

        z = {}
        z_q = {}
        z_sc = {}

        def precondition(rb, half, cols=slice(0, M_HALF)):
            if cols.start == 0:
                z[rb, half] = held([P, PACK * M_HALF], BF16, f"z{rb}{half}")
            x_rows = x[rb][:, 0 : PACK * (M, X1_STEP)[rb]].rearrange("p (t m) -> p t m", t=PACK)
            run = 4 if (rb, half) == (1, 0) else PAIR
            x_half = x_rows[:, :, M_HALF * half : M_HALF * (half + 1)]
            nc.vector.tensor_tensor(
                z[rb, half][:, PACK * cols.start : PACK * cols.stop].rearrange("p (c i t) -> p c t i", i=run, t=PACK),
                x_half[:, :, cols].rearrange("p t (c i) -> p c t i", i=run),
                damp[rb, half][:, :, cols].rearrange("p t (c i) -> p c t i", i=run),
                MULT,
            )

        def quantise_z(rb, half, cols=slice(0, M_HALF)):
            if cols.start == 0:
                z_q[rb, half] = held([P, M_HALF], U32, f"z_q{rb}{half}")
                z_sc[rb, half] = held([P, M_HALF], U8, f"z_sc{rb}{half}")
            rounded = z[rb, half][:, PACK * cols.start : PACK * cols.stop]
            nc.vector.quantize_mx(out=z_q[rb, half][:, cols].bitcast(FP8X4), scales=z_sc[rb, half][:, cols], in_=rounded)

        y_banks = {}

        def rotate_pass(half, rb):
            for pair in range(N // P // 2):
                if rb == 0:
                    y_banks[half, pair] = bank_tile(4 * half + pair)
                for u in range(2):
                    n_tile = 2 * pair + u
                    nc.tensor.matmul_mx(
                        out=y_banks[half, pair][:, M_HALF * u : M_HALF * (u + 1)],
                        lhsT=wr[:, rb, P * n_tile : P * (n_tile + 1)].bitcast(FP8X4),
                        lhsT_scale=planes[SECOND][WR_ROW:, rb, P * n_tile : P * (n_tile + 1)],
                        rhs=z_q[rb, half][:].bitcast(FP8X4),
                        rhs_scale=z_sc[rb, half][:],
                        start=(rb == 0 and u == 0),
                        stop=(rb == PASSES - 1 and u == 1),
                    )

        def store(half):
            y_half = y_sb[half]
            for pair in range(N // P // 2):
                n_tiles = slice(2 * pair, 2 * pair + 2)
                y = y_half[:, n_tiles, :]
                bank = y_banks[half, pair][:].rearrange("p (u m) -> p u m", u=2)
                rows = out.rearrange("(n_tile p) m -> p n_tile m", p=P)[:, :, M_HALF * half : M_HALF * (half + 1)]
                for u in range(2):
                    n_tile = 2 * pair + u
                    rates = rate_sb[:, n_tile : n_tile + 1]
                    if (half, pair) in ON_VECTOR:
                        nc.vector.tensor_scalar_mul(y[:, u, :], bank[:, u, :], rates)
                    else:
                        nc.scalar.activation(y[:, u, :], bank[:, u, :], ACT.Copy, scale=rates)
                    if pair == 0:
                        nc.sync.dma_start(rows[:, n_tile, :], y[:, u, :])
                if pair:
                    nc.sync.dma_start(rows[:, n_tiles, :], y[:])

        first_banks = {}
        for part in parts:
            for s in range(PACK):
                first_banks[s, part] = bank_tile(2 * s + part)
                h_pass(first_banks[s, part], s, part, FIRST)
        for s0 in range(0, PACK, 2):
            for part in parts:
                for s in (s0, s0 + 1):
                    h_pass(first_banks[s, part], s, part, SECOND)

        round_mom(0, nc.vector.tensor_copy)
        quantise_mom(0)
        round_wm(0, 0, nc.vector.tensor_copy)
        quantise_wm(0, 0)
        round_wm(1, 0, nc.vector.tensor_copy, slice(0, SPLIT))
        eps_sb = placed([P, PASSES, 2 * PACK], F32, "eps_sb", EPS_AT)
        nc.sync.dma_start(eps_sb[:, :, 0:PACK], eps.rearrange("(rb p t) -> p rb t", p=P, t=PACK))
        for s in range(PACK):
            for part in parts:
                h_out(first_banks[s, part], s, part)
            pick(s)
        for s in range(PACK, SLICES):
            for part in parts:
                bank = bank_tile(2 * (s - PACK) + part)
                for a in (FIRST, SECOND):
                    h_pass(bank, s, part, a)
                h_out(bank, s, part)
        pick(PACK)
        pick(PACK + 1)
        for r in range(SCALE_ROWS):
            nc.sync.dma_start(
                planes[SECOND][WR_ROW + r : P : QUAD].bitcast(I32),
                wr_scales[:, r :: SCALE_ROWS, :].rearrange("a q n -> q a n").bitcast(I32),
            )
        round_wm(1, 0, nc.scalar.copy, slice(SPLIT, P))
        round_mom(1, nc.scalar.copy)
        wr = placed([P, PASSES, N], I32, "wr", WR_AT)
        nc.sync.dma_start(wr[:], wr_words.rearrange("a p n j -> p a (n j)").bitcast(I32))
        quantise_wm(1, 0)
        quantise_mom(1)
        round_wm(0, 1, nc.scalar.copy)
        rate_sb = placed([P, N // P], F32, "rate_sb", RATE_AT)
        with nc.allow_non_contiguous_dma(reason="one rate a partition"):
            nc.sync.dma_start(rate_sb[:], rate.rearrange("(n_tile p) -> p n_tile", p=P))
        for pair in range(2):
            round_wm(1, 1, nc.vector.tensor_copy, pairs=slice(pair, pair + 1))
        for pair in range(2):
            quantise_wm(1, 1, slice(pair, pair + 1))
        for pair in range(2):
            quantise_wm(0, 1, slice(pair, pair + 1))
        round_mom(2, nc.vector.tensor_copy)
        quantise_mom(2)

        for half in range(2):
            for rb in range(PASSES):
                damping(rb, half)
        pick_half(SLICES - 2, 0)
        precondition(0, 0)
        pick_half(SLICES - 1, 0)
        quantise_z(0, 0)
        rotate_pass(0, 0)
        precondition(1, 0)
        pick_half(SLICES - 2, 1)
        quantise_z(1, 0)
        rotate_pass(0, 1)
        precondition(0, 1)
        pick_half(SLICES - 1, 1)
        quantise_z(0, 1)
        rotate_pass(1, 0)
        quarters = (slice(0, M_HALF // 2), slice(M_HALF // 2, M_HALF))
        for cols in quarters:
            precondition(1, 1, cols)
        for cols in quarters:
            quantise_z(1, 1, cols)
        rotate_pass(1, 1)
        for half in range(2):
            store(half)
